import numpy as np, ml_dtypes
CORES = [66,74,82,90,194,202,210,218]
N = 8
BF = ml_dtypes.bfloat16
def gentries(a):
    return np.ascontiguousarray(a.reshape(8, 16, -1).transpose(0, 2, 1)).reshape(8, -1)
def gtable(e):
    e = np.asarray(e); return np.ascontiguousarray(e.reshape(8, -1, 16).transpose(0, 2, 1)).reshape(128, -1).astype(np.int32)
W0, B, LN, RO, SP, CAP = 2048, 128, 1536, 2, 4, 384
W = W0 + RO * B
def parts(rng):
    scale = np.array([0.5, 1, 1.5, 2, 3, 4, 6, 8])[np.argsort(rng.random((N, 8)), axis=1)][:, :, None, None]; dens = 0.1 + 0.6 * rng.random((N, 8, 1, W0))
    cnt = np.where(rng.random((N, 8, 16, W0)) < dens, np.minimum(15, 1 + (scale * rng.standard_exponential((N, 8, 16, W0))).astype(np.int64)), 0)
    hot = rng.integers(0, W0, (N, 8, 64))
    def some(n, share):
        return np.where(rng.random((N, 8, n)) < share, np.take_along_axis(hot, rng.integers(0, 64, (N, 8, n)), 2), rng.integers(0, W0, (N, 8, n)))
    ptr = some(16 * W0, 0.4).reshape(N, 8, 16, W0); suf = (np.arange(W0) * rng.random((N, 8, W0))).astype(np.int64)
    return cnt, ptr, suf, rng.integers(0, W0, (N, 8, W0)), some(LN, 0.3), rng.integers(0, 256, (N, 8, RO * SP, LN))
def levels(rng, cnt, suf, v, g):
    x = np.arange(W0); b = np.where(x <= 16, 3, np.where(x <= 32, 2, np.where(x <= 48, 1, 0)))
    cnt[:, g] = np.where((np.arange(16) >> 2)[:, None] == b, rng.integers(1, 16, (N, 16, W0)), 0)
    suf[:, g] = rng.integers(1, 17, (N, W0)) + 16 * np.maximum(2 - b, 0)
    v[:, g, :SP - 1, :B] = rng.integers(240, 256, (N, SP - 1, B)); v[:, g, SP - 1, :B] = rng.integers(0, 128, (N, B))
def clones(rng, cnt, ptr, suf, lnk, cx, v, g):
    o = 1 + np.argsort(rng.random((N, W0 - 1)), axis=1); x = o[:, :B]; b = o[:, B:2 * B]; u = o[:, 2 * B:3 * B]
    qi = np.arange(N)[:, None]; z = rng.integers(1, 16, (N, B)); ct = cnt[:, g]; pt = ptr[:, g]
    for y in (x, u):
        ct[qi, :, y] = 0; ct[qi, 0, y] = 1; pt[qi, 0, y] = y
    ct[qi, :, b] = 0; ct[qi, z, b] = 1; pt[qi, z, b] = u
    suf[qi, g, x] = b; suf[qi, g, u] = x; lnk[qi, g, u] = np.maximum(lnk[qi, g, u], 1); cx[:, g, :B] = x
    v[:, g, :, :B] = rng.integers(0, 64, (N, RO * SP, B))
    for s in (SP - 2, 2 * SP - 2): v[:, g, s, :B] = rng.integers(128, 256, (N, B))
    if (RO - 2) * SP > 2:
        v[:, g, RO * SP - 2, :B] = rng.integers(64, 128, (N, B)); v[:, g, RO * SP - 1, :B] = rng.integers(128, 256, (N, B))
def kept(rng, cnt, ptr, suf, cx, v, g):
    o = 1 + np.argsort(rng.random((N, W0 - 1)), axis=1)[:, :(SP + 1) * B]; h = o[:, :SP * B]; b = o[:, SP * B:]
    qi = np.arange(N)[:, None]; z = rng.integers(1, 16, (N, B)); ct = cnt[:, g]; pt = ptr[:, g]
    ct[qi, :, h] = 0; ct[qi, 0, h] = 1; pt[qi, 0, h] = h; suf[qi, g, h] = o[:, B:]
    ct[qi, :, b] = 0; ct[qi, z, b] = 1; cx[:, g] = o[:, np.arange(LN) % B]
    v[:, g, :SP] = rng.integers(0, 128, (N, SP, LN)); v[1::2, g, SP - 1, :B] = rng.integers(128, 256, (N // 2, B))
    v[:, g, 2 * SP - 1, :B] = rng.integers(0, 128, (N, B))
def filled(rng, cnt, ptr, suf, lnk, cx, v, g):
    o = 1 + np.argsort(rng.random((N, W0 - 1)), axis=1)[:, :(2 * SP + 1) * B]; x = o[:, :B]; y = o[:, B:]; b1 = o[:, SP * B:(SP + 1) * B]; b2 = o[:, 2 * SP * B:]
    qi = np.arange(N)[:, None]; ct = cnt[:, g]; pt = ptr[:, g]
    ct[qi, :, o] = 0; ct[qi, 0, o] = 1; pt[qi, 0, o] = o
    for b, lo in ((b1, 1), (b2, 8)):
        ct[qi, 0, b] = 0; ct[qi, rng.integers(lo, lo + 7, (N, B)), b] = 1
    suf[qi, g, x] = np.roll(x, -1, axis=1); suf[qi, g, y[:, :-B]] = y[:, B:]; lnk[qi, g, x] = np.roll(y[:, :B], -1, axis=0)
    cx[:, g] = x[:, np.arange(LN) % B]
    v[:, g, :2 * SP] = rng.integers(0, 128, (N, 2 * SP, LN)); v[:, g, SP - 1, :B] = rng.integers(128, 256, (N, B))
    q4 = np.arange(N) % 4; v[:, g, 2 * SP - 1, :B // 2] += 128 * ((q4 == 1) | (q4 == 2))[:, None]
    if RO > 2: v[:, g, 3 * SP - 1, :B // 2] = rng.integers(0, 128, (N, B // 2))
def pack(cnt, ptr, suf, lnk, cx, v):
    return {"tab": np.ascontiguousarray((16 * ptr + cnt).reshape(N, 128, W0)).astype(np.int32), "suf": suf.astype(np.int32), "lnk": lnk.astype(np.int32),
            "cx": np.stack([gtable(a) for a in cx]), "vv": v.reshape(N, 8, RO * SP * LN).astype(np.float32).astype(BF)}
def setup_inputs(rng):
    return pack(*parts(rng))
def setup_inputs_room(rng):
    cnt, ptr, suf, lnk, cx, v = parts(rng)
    cnt = np.where(np.arange(16)[:, None] == rng.integers(0, 16, (N, 8, 1, W0)), np.maximum(cnt, 1), cnt); ptr = np.maximum(ptr, 1); cx = np.maximum(cx, 1)
    v[:, :, :SP - 1] = rng.integers(0, 128, (N, 8, SP - 1, LN)); opts = (0, 1, CAP - 1, CAP, CAP + 1, LN)
    for q in range(N):
        o = rng.permutation(6)
        for g in range(6):
            m = opts[g] if q == 0 else opts[5 - g] if q == 1 else opts[int(o[g])]
            v[q, g, SP - 1] = np.where(rng.permutation(LN) < m, rng.integers(240, 256, LN), rng.integers(0, 128, LN))
    for g in (6, 7):
        levels(rng, cnt, suf, v, g)
        for q in range(N): cx[q, g, :B] = 64 + rng.permutation(W0 - 64)[:B]
    return pack(cnt, ptr, suf, lnk, cx, v)
def setup_inputs_ties(rng):
    cnt, ptr, suf, lnk, cx, v = parts(rng)
    rows = np.array([4, 1, 2, 8, 1, 0, 16, 4, 8, 8, 16]); vals = np.array([3, 1, 1, 1, 15, 0, 15, 1, 3, 7, 3]); k = rng.integers(0, 11, (N, 8, W0))
    order = np.argsort(rng.random((N, 8, W0, 16)), axis=-1)
    cnt = np.where(order < rows[k][..., None], vals[k][..., None], 0).transpose(0, 1, 3, 2)
    v = np.where(rng.random(v.shape) < 0.6, 16 * rng.integers(0, 17, v.shape), 15 * rng.integers(0, 18, v.shape)) + np.where(rng.random(v.shape) < 0.6, 0, rng.integers(-1, 2, v.shape))
    return pack(cnt, ptr, suf, lnk, cx, np.minimum(np.maximum(v, 0), 255))
def setup_inputs_alike(rng):
    cnt, ptr, suf, lnk, cx, v = parts(rng); few = rng.integers(1, W0, (N, 8, 6))
    def some(n, m):
        return np.take_along_axis(few, rng.integers(0, m, (N, 8, n)), 2)
    ptr = some(16 * W0, 6).reshape(N, 8, 16, W0); suf = np.where(rng.random((N, 8, W0)) < 0.5, some(W0, 6), suf); lnk = np.where(rng.random((N, 8, W0)) < 0.5, some(W0, 6), lnk); cx = some(LN, 4)
    levels(rng, cnt, suf, v, 3); cx[:, 3, :B] = rng.choice(np.array([70, W0 - 1]), (N, B))
    cx[:, 5] = cx[:, 5, :1]; v[:, 5] = v[:, 5, :, :1]
    filled(rng, cnt, ptr, suf, lnk, cx, v, 2); kept(rng, cnt, ptr, suf, cx, v, 6); clones(rng, cnt, ptr, suf, lnk, cx, v, 7)
    return pack(cnt, ptr, suf, lnk, cx, v)
def setup_inputs_ends(rng):
    cnt, ptr, suf, lnk, cx, v = parts(rng); e = np.array([0, 1, W0 - 1])
    ptr = np.where(rng.random(ptr.shape) < 0.3, rng.choice(e, ptr.shape), ptr); lnk = np.where(rng.random(lnk.shape) < 0.5, rng.choice(e, lnk.shape), lnk); cx = np.where(rng.random(cx.shape) < 0.5, rng.choice(e, cx.shape), cx)
    suf[:, 1::2] = np.where(rng.random((N, 4, W0)) < 0.3, np.arange(W0), rng.integers(0, W0, (N, 4, W0))); suf[:, 2] = 0; suf[:, 4] = 0; suf[:, 5] = 0
    cnt[:, 4, :, 0] = 0; cnt[:, 5, :, 0] = 15; cnt[:, 6] = 15 * (cnt[:, 6] > 0); cnt[:, 7, :, W0 - 1] = 0; cnt[:, 0, :, W0 - 1] = 15
    v = np.where(rng.random(v.shape) < 0.7, rng.choice(np.array([0, 1, 127, 128, 239, 240, 254, 255]), v.shape), v)
    return pack(cnt, ptr, suf, lnk, cx, v)
def setup_inputs_spread(rng):
    def low(*shape):
        return np.minimum((W0 * rng.random(shape) ** rng.integers(1, 5, shape[:2] + (1,) * (len(shape) - 2))).astype(np.int64), W0 - 1)
    cnt = np.where(rng.random((N, 8, 16, W0)) < rng.random((N, 8, 1, W0)) ** 2, np.minimum(np.exp2(4 * rng.random((N, 8, 16, W0)) * rng.random((N, 8, 1, W0)) ** 0.5).astype(np.int64), 15), 0)
    v = np.minimum((256 * rng.random((N, 8, RO * SP, LN)) ** 3).astype(np.int64), 255)
    return pack(cnt, low(N, 8, 16, W0), low(N, 8, W0), W0 - 1 - low(N, 8, W0), low(N, 8, LN), np.where(rng.random(v.shape) < 0.5, v, 255 - v))
def check_inputs(d):
    bad = []
    for k, hi in (("tab", 16 * W0 - 1), ("suf", W0 - 1), ("lnk", W0 - 1), ("cx", W0 - 1)):
        if np.min(d[k]) < 0 or np.max(d[k]) > hi: bad.append("range of " + k)
    v = np.asarray(d["vv"]).astype(np.float32)
    if not np.all((v >= 0) & (v <= 255) & (v == np.floor(v))): bad.append("range of vv")
    return bad
def reference(tab, suf, lnk, cx, vv):
    k = tab.astype(np.int32).reshape(N, 8, 16, W0)
    C = np.zeros((N, 8, 16, W), np.int32); S = np.zeros((N, 8, 16, W), np.int32); C[..., :W0] = k & 15; S[..., :W0] = k >> 4
    F = np.zeros((N, 8, W), np.int32); L = np.zeros((N, 8, W), np.int32); F[..., :W0] = suf; L[..., :W0] = lnk
    v = vv.astype(np.float32).astype(np.int32).reshape(N, 8, RO, SP, 1, LN)
    c = np.stack([gentries(a) for a in cx]).astype(np.int32); e = np.zeros((N, 8, 16, LN), np.int32); f = np.full((N, 8, LN), -1, np.int32)
    qi = np.arange(N)[:, None, None]; gi = np.arange(8)[None, :, None]
    for t in range(RO):
        for s in range(SP):
            cc = np.take_along_axis(C, c[:, :, None, :], 3)
            n = cc * (1 - e); P = np.add.accumulate(n, axis=2, dtype=np.int32); E = np.add.reduce((n > 0).astype(np.int32), axis=2)
            z = np.add.reduce((256 * P <= v[:, :, t, s] * (P[:, :, 15] + E)[:, :, None, :]).astype(np.int32), axis=2)
            z = np.where(c == 0, np.minimum(z, 15), z); esc = z == 16
            d, fb = c, f
            f = np.where(esc, np.where(fb < 0, d, fb), -1)
            e = np.where(esc[:, :, None, :], np.maximum(e, (cc > 0).astype(np.int32)), 0)
            c = np.where(esc, F[qi, gi, d], S[qi, gi, np.minimum(z, 15), d])
        for q in range(N):
            for g in range(8):
                j = np.nonzero(~esc[q, g, :B] & (fb[q, g, :B] >= 0))[0]
                a = j[np.unique(fb[q, g, j], return_index=True)[1]]
                w = W0 + B * t + a; to = c[q, g, a]
                cw = (C[q, g][:, to] + 1) >> 1; sw = S[q, g][:, to]
                C[q, g][:, w] = cw; S[q, g][:, w] = sw; F[q, g, w] = to; L[q, g, w] = L[q, g, to]
                C[q, g, z[q, g, a], fb[q, g, a]] = 1; S[q, g, z[q, g, a], fb[q, g, a]] = w
                b = j[np.unique(d[q, g, j], return_index=True)[1]]
                C[q, g, z[q, g, b], d[q, g, b]] = np.minimum(15, C[q, g, z[q, g, b], d[q, g, b]] + 1)
        slot = esc & (np.add.accumulate(esc.astype(np.int32), axis=2) <= CAP)
        c2 = np.array(c); e2 = np.array(e); f2 = np.array(f)
        for r in range(N):
            q = (r - 1) % N
            for g in range(8):
                a = np.nonzero(slot[q, g])[0]; b = np.nonzero(slot[r, g])[0]; m = min(len(a), len(b)); a = a[:m]; b = b[:m]
                c2[r, g, b] = L[q, g, c[q, g, a]]; e2[r, g][:, b] = e[q, g][:, a]; f2[r, g, b] = -1
        c, e, f = c2, e2, f2
    return {"yn": C.reshape(N, 128, W).astype(np.float32).astype(BF), "yc": np.stack([gtable(a) for a in c]).astype(np.float32)}

@@ -1,0 +1,638 @@
+from concourse.mybir import AluOpType, ActivationFunctionType
+
+OP = AluOpType
+AF = ActivationFunctionType
+RO, SP = 2, 4
+NW = 2560
+H = 768
+F32, B16, I32, F16, U16 = "float32", "bfloat16", "int32", "float16", "uint16"
+SCRATCH = {}
+WHERE = {}
+
+
+def sb(dtype, **kw):
+    for name, n in kw.items():
+        SCRATCH[name] = ("sbuf", [128, n], dtype)
+
+
+def pool(buf, dtype, **kw):
+    o = 0
+    for name, n in kw.items():
+        WHERE[name] = (buf, o, n)
+        o += -(-n // 16) * 16
+    SCRATCH[buf] = ("sbuf", [128, o], dtype)
+
+
+sb(I32, tabI=2048, CI=2048, CPI=544, CPL=544)
+sb(F32, YB=2048, ST=NW, DT=NW, Y0=H, Y1=H, LBB=H, SW=1920)
+sb(B16, W1=2048, WT=NW, AUX=NW, VV=12288, w0=H, w1=H, n0=H, n1=H, x0=H, x1=H, k0=H, k1=H, MM=1920, YN=2304, BIT=10240, LBA=H,
+   VW=1920, A2=1536, SND0=792, SND1=792, RCV0=792, RCV1=792, LW=1920, SELK=1024, NSELK=1024, EQF=1024, EQD=1024, ABD=1024,
+   COMB=1440, ZB=1536, FB=2048)
+sb(F16, X0=H, X1=H, COMBX=144)
+sb(U16, CL=960)
+pool("zi", I32, CXI=96, CIT=96, i_rm=16, i_pc=16, i_g8=8, i_bm=128, i_dp=128, i_sf=128, i_wr=128, i_k=128, i_u=128)
+pool("zf", F32, RM=16, PC=1, G8=8, SH32=128, JI=96, JL=96, J2=96, J3=96, JD=24, JD2=24, DUM0=16, DUM1=16, CLF=96, YC=96, HT=40,
+     DL=40, hd=40, d1=40, FS=40, KT=16, KT2=16, KK=16, CAND=16, CS=104, Z96=96, CNT=96, OKT=96, TT=96, TT2=96, POSF=96, PRE=24,
+     LNF=24, T1=24, RX1=24, RX2=24, AO=8, AO2=8, BO=8, BO2=8, HF=8, xs=128, kk=128, K8=8, NK8=8, COLS=64, ZF=512, d0c=1)
+pool("zb", B16, BM=128, IDN=128, NI=128, LT=128, LTB=128, TRI=128, R15=128, ESC=128, CANDM=128, BID=128, N01=128, NI2K=128,
+     U1=128, U2=128, LTu=128, SELF=128, SF2=128, E0=128, ID2=128, ONES=128, OB=240, SWb=384, E16=96, HB=544, LB=544, XF=256,
+     XC=128, AR=256, OA=128, nOA=128, OA2=128, OBm=128, tg=128, s1=128, s2=128, s3=128, ug=128, FLs=128, fd=128, xt=128)
+pool("zh", F16, SH16=128, WR=128, tS=128, qS=128, Sc=128)
+pool("zu", U16, POS=96, LNE=24, TO=24, FK=16, OFF=8, OFD=8)
+for nm, nc in (("PA", 1536), ("PB", 1536), ("LAp", 512), ("LBp", 512)):
+    SCRATCH[nm] = ("psum", [128, nc], F32)
+
+SEMAPHORES = ["v", "s", "t", "q", "arr0", "arr1", "snt0", "snt1"] + ["d%d" % i for i in range(60)]
+CA, CE, CF, CID, CSA, CSB, CLK, C0, C7, C8 = range(10)
+
+
+def rank_program(g, core, T, topo):
+    rank = T.rank_of(core)
+    if rank is None:
+        return
+    Q = {"v": g.vector, "s": g.scalar, "t": g.tensor, "q": g, "y": g.sync}
+    cnt = {"v": 0, "s": 0, "t": 0, "q": 0}
+    know = {q: {} for q in Q}
+    res, acc, used, nd = {}, {}, {}, [0]
+
+    def do_waits(q, R, W):
+        deps = []
+        for k in R:
+            if k[0] != "#":
+                deps += res.get(k, ([], []))[0]
+        for k in W:
+            if k[0] != "#":
+                ws, rs = res.get(k, ([], []))
+                deps += ws + [e for e in rs if e[0] != q]
+        for k in list(R) + list(W):
+            if k[0] == "#":
+                deps += [e for e in acc.get(k, []) if e[0] != q]
+        best = {}
+        for e in deps:
+            if know[q].get(e[1], 0) < e[2] and (e[1] not in best or best[e[1]][2] < e[2]):
+                best[e[1]] = e
+        for e in [e for e in best.values() if not any(o is not e and o[3].get(e[1], 0) >= e[2] for o in best.values())]:
+            Q[q].wait_ge(T.sem[e[1]], e[2])
+            k = know[q]
+            k[e[1]] = max(k.get(e[1], 0), e[2])
+            for s, v in e[3].items():
+                k[s] = max(k.get(s, 0), v)
+
+    def record(ent, R, W):
+        for k in W:
+            if k[0] != "#":
+                res[k] = ([ent], [])
+        for k in R:
+            if k[0] != "#" and k not in W:
+                ws, rs = res.get(k, ([], []))
+                res[k] = (ws, [e for e in rs if e[0] != ent[0]] + [ent])
+        for k in list(R) + list(W):
+            if k[0] == "#":
+                acc[k] = [ent]
+
+    def op(q, R, W, *fns):
+        do_waits(q, R, W)
+        for fn in fns:
+            fn(Q[q]).then_inc(T.sem[q], 1)
+            cnt[q] += 1
+        clock = dict(know[q])
+        clock[q] = cnt[q]
+        record((q, q, cnt[q], clock), R, W)
+
+    def dma(q, R, W, *pairs):
+        do_waits(q, R, W)
+        name = "d%d" % nd[0]
+        nd[0] += 1
+        for o, i in pairs:
+            Q[q].dma_start(o, i).then_inc(T.sem[name], 16)
+        used[name] = 16 * len(pairs)
+        record((name, name, 16 * len(pairs), dict(know[q])), R, W)
+
+    def z(name, a=0, b=None, st=1):
+        buf, o, n = WHERE[name]
+        return T[buf][:, o + a:o + (n if b is None else b):st]
+
+    def ts(out, a, s1, o1, s2=None, o2=None):
+        if o2 is None:
+            return lambda e: e.tensor_scalar(out, a, s1, None, o1)
+        return lambda e: e.tensor_scalar(out, a, s1, s2, o1, o2)
+
+    def tt(out, a, b, o):
+        return lambda e: e.tensor_tensor(out, a, b, o)
+
+    def cp(out, a):
+        return lambda e: e.tensor_copy(out, a)
+
+    def ms(out, c):
+        return lambda e: e.memset(out, c)
+
+    def ac(out, a, f, **kw):
+        return lambda e: e.activation(out, a, f, **kw)
+
+    def mm(out, l, r, st, sp):
+        return lambda e: e.matmul(out, l, r, st, sp)
+
+    def V(R, W, *f):
+        op("v", R, W, *f)
+
+    def S(R, W, *f):
+        op("s", R, W, *f)
+
+    def PE(R, W, *f):
+        op("t", R, W, *f)
+
+    def tz(out, a, s1, o1, *more):
+        V([a], [out], ts(z(out), z(a), s1, o1, *more))
+
+    def t2(out, a, b, o):
+        V([a, b], [out], tt(z(out), z(a), z(b), o))
+
+    PX, LP = [T.PA, T.PB], [T.LAp, T.LBp]
+    PK0, PK2, LK = ["#A0", "#B0"], ["#A2", "#B2"], ["#LA", "#LB"]
+    w, n, x, cond, X, Y = ([T["%s%d" % (a, p)] for p in (0, 1)] for a in ("w", "n", "x", "k", "X", "Y"))
+    AUXK = ["AUX"] + ["ar%d" % i for i in range(10)]
+
+    def comb(v, i):
+        return T.COMB[:, v * 144 + 15 - i:v * 144 + 143 - i]
+
+    def combx(i):
+        return T.COMBX[:, 15 - i:143 - i]
+
+    def RMc(r):
+        return z("RM", r, r + 1)
+
+    dma("y", [], ["cpF"], (T.CPI[:, 256:384], T.suf[:, :]))
+    dma("s", [], ["cpT"], (T.CPI[:, 0:128], T.tab[0:128:16, :]))
+    dma("y", [], ["cpL"], (T.CPI[:, 128:256], T.lnk[:, :]))
+    for k in range(4):
+        dma("s" if k % 2 == 0 else "y", [], ["tab%d" % k], (T.tabI[:, 512 * k:512 * k + 512], T.tab[:, 512 * k:512 * k + 512]))
+    dma("y", [], ["CXI"], (z("CXI"), T.cx[:, :]))
+
+    def iota(tile, key, pattern, base, cm, **kw):
+        op("q", [], [key], lambda e: e.iota(tile, pattern, base, cm, **kw))
+    fl = {"allow_small_or_imprecise_dtypes": True}
+    iota(z("i_rm"), "i_rm", [[-1, 16]], 0, 1)
+    iota(z("i_g8"), "i_g8", [[-16, 8]], 0, 1)
+    iota(z("i_bm"), "i_bm", [[-16, 8], [0, 16]], 0, 1)
+    iota(z("i_dp"), "i_dp", [[1, 128]], 0, -1)
+    iota(z("i_sf"), "i_sf", [[1, 128]], -15, -16)
+    iota(T.CPI[:, 384:512], "cpj", [[1, 128]], 0, 128)
+    iota(T.CPI[:, 512:544], "cpk", [[1, 32]], 0, 32)
+    iota(z("i_pc"), "i_pc", [[0, 16]], 0, 1)
+    iota(z("JI"), "JI", [[16, 96]], 0, 0, **fl)
+    iota(z("i_wr"), "i_wr", [[1, 128]], 0, 0)
+    for i in range(10):
+        iota(T.BIT[:, 1024 * i:1024 * i + 1024], "bit%d" % i, [[0, 1024 >> (i + 1)], [1, 2], [0, 1 << i]], 0, 0, **fl)
+
+    SR, BA = OP.logical_shift_right, OP.bitwise_and
+    V([], ["AUX"], ms(T.AUX[:, :], 0.0))
+    V([], ["COMB"], ms(T.COMB[:, :], 0.0))
+    V([], ["COMBX"], ms(T.COMBX[:, :], 0.0))
+    tz("i_rm", "i_rm", 15, BA)
+    tz("i_g8", "i_g8", 4, OP.arith_shift_right)
+    tz("i_bm", "i_bm", 4, OP.arith_shift_right)
+    tz("RM", "i_rm", 0.0, OP.is_equal)
+    tz("G8", "i_g8", 0.0, OP.is_equal)
+    tz("BM", "i_bm", 0.0, OP.is_equal)
+    tz("U1", "i_dp", -1.0, OP.is_equal)
+    tz("IDN", "i_dp", 0.0, OP.is_equal)
+    tz("LTu", "i_dp", 0.0, OP.is_ge)
+    t2("U1", "U1", "BM", OP.mult)
+    V(["G8", "COMBX"], ["COMBX"], cp(T.COMBX[:, 15:143:16], z("G8")))
+    tz("SELF", "i_sf", 0.0, OP.is_equal, 32.0, OP.mult)
+    tz("SF2", "i_sf", -128.0, OP.is_equal)
+    t2("SH32", "U1", "IDN", OP.subtract)
+    t2("SELF", "SELF", "SF2", OP.add)
+    t2("LTB", "LTu", "BM", OP.mult)
+    V([], ["ONES"], ms(z("ONES"), 1.0))
+    V([], ["WTz"], ms(T.WT[:, 2048:NW], 0.0))
+    V([], ["DTz"], ms(T.DT[:, 2048:2304], 0.0))
+    V([], ["DL"], ms(z("DL"), 0.0))
+    ncol = [0]
+
+    def column(terms):
+        prev, key = None, None
+        for r, wt in terms:
+            c = ncol[0]
+            ncol[0] += 1
+            out = z("COLS", c, c + 1)
+            kw = {"bias": prev} if key else {}
+            S(["RM"] + ([key] if key else []), ["col%d" % c], ac(out, RMc(r), AF.Identity, scale=float(wt), **kw))
+            prev, key = out, "col%d" % c
+        return prev, key
+
+    def make_comb(v, col, key):
+        S([key, "G8", "COMB"], ["cb%d" % v], ac(T.COMB[:, v * 144 + 15:v * 144 + 143:16], z("G8"), AF.Copy, scale=col))
+
+    def scaled(out, a, col, key):
+        S([a, key], [out], ac(z(out), z(a), AF.Copy, scale=col))
+
+    colB, kB = column([(4, 1), (9, 1)])
+    S(["AUX", kB], ["AUX"], ac(T.AUX[:, 0:2304], T.AUX[:, 0:2304], AF.Identity, bias=colB))
+    colR, kR = column([(15, 4096)])
+    S(["AUX", "RM"], ["AUX"], ac(T.AUX[:, 2304:NW], T.AUX[:, 2304:NW], AF.Identity, bias=RMc(4)))
+    S(["AUX", kR], ["AUX"], ac(T.AUX[:, 0:1], T.AUX[:, 0:1], AF.Identity, bias=colR))
+    colF, kF = column([(15, -1152 - 4128)])
+    make_comb(CF, *column([(4, -1152 - 4128), (5, 32), (6, 1)]))
+    make_comb(CA, *column([(0, 32), (1, 1), (4, -4128)]))
+    make_comb(CE, RMc(15), "RM")
+    scaled("NI", "IDN", -1.0, "IDN")
+    scaled("LT", "LTB", 256.0, "LTB")
+    scaled("R15", "IDN", RMc(15), "RM")
+    scaled("ESC", "BM", *column([(15, -32)]))
+
+    b32 = 129.0 - 31.0 / 64
+    V(["cpj"], ["cpj"], ts(T.CPI[:, 384:512], T.CPI[:, 384:512], 2047, BA))
+    V(["cpk"], ["cpk"], ts(T.CPI[:, 512:544], T.CPI[:, 512:544], 511, BA))
+    V(["cpF", "cpL"], ["HBa"], ts(z("HB", 128, 384), T.CPI[:, 128:384], 1.0 / 32, OP.mult, b32, OP.add))
+    V(["cpT"], ["cpl0"], ts(T.CPL[:, 0:128], T.CPI[:, 0:128], 4, SR, 31, BA))
+    V(["cpF", "cpL", "cpj", "cpk"], ["cpl1"], ts(T.CPL[:, 128:544], T.CPI[:, 128:544], 31, BA))
+    V(["cpT"], ["HBb"], ts(z("HB", 0, 128), T.CPI[:, 0:128], 1.0 / 512, OP.mult, 129.0 - 511.0 / 1024, OP.add))
+    V(["cpl0", "cpl1"], ["LB"], cp(z("LB"), T.CPL[:, :]))
+    dma("y", ["HBa"], ["fb0"], (T.FB[0:8, :], z("HB", 256, 384)))
+    dma("y", ["LB"], ["fb1"], (T.FB[8:16, :], z("LB", 256, 384)))
+    V(["cpj"], ["HBc"], ts(z("HB", 384, 512), T.CPI[:, 384:512], 1.0 / 32, OP.mult, b32, OP.add))
+    V(["cpk"], ["HBd"], ts(z("HB", 512, 544), T.CPI[:, 512:544], 1.0 / 32, OP.mult, b32 + 64.0, OP.add))
+    for j, (r, key, t, a) in enumerate(((5, "HBa", "HB", 256), (6, "LB", "LB", 256), (0, "HBb", "HB", 0), (1, "LB", "LB", 0),
+                                        (2, "HBa", "HB", 128), (3, "LB", "LB", 128), (7, "HBc", "HB", 384), (8, "LB", "LB", 384))):
+        dma("y", [key, "AUX"], ["ar%d" % j], (T.AUX[r:128:16, 0:2048], z(t, a, a + 128)))
+    dma("y", ["HBd", "AUX"], ["ar8"], (T.AUX[7:128:16, 2048:NW], z("HB", 512, 544)))
+    dma("y", ["LB", "AUX"], ["ar9"], (T.AUX[8:128:16, 2048:NW], z("LB", 512, 544)))
+    for key, a, b in (("vv0", 0, 1536), ("vv1", 1536, 6144), ("vv2", 6144, 12288)):
+        dma("y", [], [key], *[(T.VV[i:128:16, a:b], T.vv[:, a:b]) for i in range(16)])
+
+    for k in range(4):
+        a, b = 512 * k, 512 * k + 512
+        V(["tab%d" % k], ["yb%d" % k], ts(T.YB[:, a:b], T.tabI[:, a:b], -7.5, OP.add, 201326592.0, OP.add))
+        V(["tab%d" % k], ["ci%d" % k], ts(T.CI[:, a:b], T.tabI[:, a:b], 15, BA))
+        S(["yb%d" % k], ["st%d" % k], ac(T.ST[:, a:b], T.YB[:, a:b], AF.Identity, bias=-12584064.0, scale=0.0625))
+    pieces = [(k, 512 * k, PX[k // 2][:, 1024 * (k % 2):1024 * (k % 2) + 512], (PK0 if k % 2 == 0 else PK2)[k // 2]) for k in range(4)]
+    o = WHERE["SELF"][1]
+    for k, a, P, pk in pieces:
+        PE(["st%d" % k, "SH32", "SELF", "fb0", "fb1"], [pk], mm(P, z("SH32"), T.ST[:, a:a + 512], True, False),
+           mm(P, T.zb[0:16, o:o + 128], T.FB[0:16, a:a + 512], False, True))
+        V(["ci%d" % k], ["w1%d" % k], ts(T.W1[:, a:a + 512], T.CI[:, a:a + 512], 1.03, OP.mult, 128.48, OP.add))
+        V(["w1%d" % k], ["wt%d" % k], ts(T.WT[:, a:a + 512], T.W1[:, a:a + 512], -128.0, OP.add))
+    for k, a, P, pk in pieces:
+        S([pk, kF], ["dt%d" % k], ac(T.DT[:, a:a + 512], P, AF.Identity, bias=colF))
+    V(["CXI"], ["c0_0", "c0_1"], cp(T.CL[:, 0:96], z("CXI")))
+    WTK = ["WT", "WTz"] + ["wt%d" % k for k in range(4)]
+    DTK = ["DT", "DTz"] + ["dt%d" % k for k in range(4)]
+    STK = ["STz"] + ["st%d" % k for k in range(4)]
+    cR, nkR = column([(15, -1)])
+    S([nkR], ["d0c"], ac(z("d0c"), cR, AF.Identity, bias=1.0))
+    S(["d0c", "dt0"], ["dt0"], ac(T.DT[:, 0:1], T.DT[:, 0:1], AF.Copy, scale=z("d0c")))
+
+    def zeros():
+        dma("y", ["ZB", "VW"], ["VW"], (T.VW[:, 0:384], T.ZB[:, 0:384]))
+        dma("y", ["ZF", "SW"], ["SW"], (T.SW[:, 0:384], z("ZF", 0, 384)))
+        dma("y", ["ZB", "LW"], ["LW"], (T.LW[:, 0:1536], T.ZB[:, :]))
+
+    def late_a():
+        V([], ["HT"], ms(z("HT"), 0.0))
+        V([], ["ZB"], ms(T.ZB[:, :], 0.0))
+        V([], ["ZF"], ms(z("ZF"), 0.0))
+        dma("y", ["ZB"], ["LBA"], (T.LBA[:, :], T.ZB[:, 0:H]))
+        dma("y", ["ZF"], ["STz"], (T.ST[:, 2048:NW], z("ZF")))
+        zeros()
+        V([], ["OB"], ms(z("OB"), 0.0))
+        V([], ["CS"], ms(z("CS", 0, 8), 0.0))
+        V([], ["Z96"], ms(z("Z96"), 0.0))
+        tz("i_pc", "i_pc", 15, BA)
+        tz("TRI", "i_dp", 0.0, OP.is_le, 8192.0, OP.mult)
+        tz("U2", "i_dp", 1.0, OP.is_equal)
+        V(["OB"], ["OB"], ms(z("OB", 112, 128), 1.0))
+        V(["i_pc"], ["PC"], cp(z("PC"), z("i_pc", 0, 1)))
+        tz("WR", "i_wr", 896.0, OP.add)
+        V(["SH32"], ["SH16"], cp(z("SH16"), z("SH32")))
+        t2("U2", "U2", "BM", OP.mult)
+        t2("BID", "U2", "IDN", OP.subtract)
+
+    late, todo = {}, []
+
+    def drain(m):
+        for _ in range(min(m, len(todo))):
+            todo.pop(0)()
+
+    def later(f, *a):
+        todo.append(lambda: f(*a))
+
+    def shifted(out, a, na, c, o=0):
+        S([a, "PC"], [out], ac(z(out, o, o + na), z(a, 0, na), AF.Identity, bias=c))
+
+    def later_comb(v, terms):
+        later(lambda: make_comb(v, *column(terms)))
+
+    def key_tiles(gg):
+        for tile, kt in (("SELK", "K8"), ("NSELK", "NK8")):
+            S(["ONES", kt], [tile + str(gg)], ac(T[tile][:, 128 * gg:128 * gg + 128], z("ONES"), AF.Copy, scale=z(kt, gg, gg + 1)))
+
+    def lane_bits():
+        S(["LBA", "RM"], ["LBA"], ac(T.LBA[:, :], T.LBA[:, :], AF.Identity, bias=RMc(15)))
+        for i in range(10):
+            dma("y", ["bit%d" % i, "LBA"], ["lb%d" % i], (T.LBA[i:128:16, :], T.BIT[0:8, 1024 * i:1024 * i + H]))
+
+    def slot_combs():
+        sa = column([(i, 1 << i) for i in range(10)] + [(15, 2048)])
+        make_comb(CSA, *sa)
+        c = ncol[0]
+        ncol[0] += 1
+        S(["RM", sa[1]], ["colx"], ac(z("COLS", c, c + 1), RMc(15), AF.Identity, bias=sa[0], scale=768.0))
+        make_comb(CSB, z("COLS", c, c + 1), "colx")
+
+    LBK = ["LBA"] + ["lb%d" % i for i in range(10)]
+
+    def keep():
+        late["keep"] = column([(0, 1), (1, 1), (2, 1), (3, 1)])
+    later(shifted, "JL", "JI", 96, z("PC"))
+    later(shifted, "J2", "JL", 96, -1663.0)
+    later(shifted, "J3", "JL", 96, 384.0)
+    later(shifted, "JD", "JL", 24, 1536.0)
+    later(shifted, "JD2", "JL", 24, 3584.0)
+    for t in range(2):
+        later(shifted, "DUM%d" % t, "JL", 8, 2304.0 + 128 * t)
+        later(shifted, "DUM%d" % t, "JL", 8, 2304.0 + 128 * t, 8)
+    later(scaled, "E0", "IDN", RMc(0), "RM")
+    later(scaled, "ID2", "IDN", 2.0, "IDN")
+    later(scaled, "NI2K", "IDN", -2048.0, "IDN")
+    later(lambda: scaled("CANDM", "BM", *column([(9, -1)])))
+    later_comb(CLK, [(2, 32), (3, 1), (4, -32)])
+    later_comb(CID, [(4, -1152 - 4128), (7, 32), (8, 1)])
+    for v, r in ((C0, 0), (C7, 7), (C8, 8)):
+        later(make_comb, v, RMc(r), "RM")
+    later(lambda: scaled("K8", "G8", *column([(7, 32), (8, 1)])))
+    later(scaled, "NK8", "K8", -1.0, "K8")
+    later(lane_bits)
+    later(lambda: scaled("N01", "NI", *column([(0, 1), (1, 1)])))
+    later(keep)
+    for gg in range(8):
+        later(key_tiles, gg)
+    later(slot_combs)
+    later(lambda: S(LBK, ["LBB"], ac(T.LBB[:, :], T.LBA[:, :], AF.Identity, bias=-200.0, scale=400.0)))
+
+    def lists(p, idx):
+        return T.CL[:, idx * 96 + 48 * p:idx * 96 + 48 * p + 48], "c%d_%d" % (idx, p)
+
+    def p1(p, idx, k):
+        off, ck = lists(p, idx)
+        P = PX[p]
+        S(AUXK + [ck], ["x%d" % p], ac(x[p][:, :], T.AUX[:, 0:2304].indirect(off), AF.Copy))
+        wi = T.WT[:, 0:2304].indirect(off)
+        V(WTK + [ck] + (["m%d" % p] if k else []), ["w%d" % p],
+          tt(w[p][:, :], wi, T.MM[:, H * p:H * p + H], OP.mult) if k else cp(w[p][:, :], wi))
+        PE(["w%d" % p, "BM"], [PK0[p]], mm(P[:, 0:512], z("BM"), w[p][:, 0:512], True, True),
+           mm(P[:, 512:768], z("BM"), w[p][:, 512:768], True, True))
+        PE(["x%d" % p, "cb%d" % CA], [LK[p]],
+           *[mm(LP[p][:, 0:48], comb(CA, i), x[p][:, i:H:16], i == 0, False) for i in range(16)])
+        S(["w%d" % p], ["n%d" % p], ac(n[p][:, :], w[p][:, :], AF.Relu, bias=-1.0))
+        PE(["x%d" % p, "n%d" % p, "R15", "LT"], [PK0[p], PK2[p]],
+           mm(P[:, 768:1024], z("R15"), x[p][:, 0:256], True, False), mm(P[:, 768:1024], z("LT"), n[p][:, 0:256], False, True),
+           mm(P[:, 1024:1536], z("R15"), x[p][:, 256:768], True, False), mm(P[:, 1024:1536], z("LT"), n[p][:, 256:768], False, True))
+
+    def p2(p, idx, k):
+        off, ck = lists(p, idx)
+        P, s = PX[p], k % SP
+        vk = "vv%d" % (0 if k == 0 else 1 if k < 4 else 2)
+        V([vk, PK0[p]], ["Y%d" % p], tt(Y[p][:, :], T.VV[:, k * 1536 + H * p:k * 1536 + H * p + H], P[:, 0:768], OP.mult))
+        V(["Y%d" % p, PK0[p], PK2[p]], ["k%d" % p], tt(cond[p][:, :], P[:, 768:1536], Y[p][:, :], OP.is_le))
+        V(DTK + [ck, "k%d" % p], ["X%d" % p], tt(X[p][:, :], T.DT[:, 0:2304].indirect(off), cond[p][:, :], OP.mult))
+
+        def esc_list():
+            if s == SP - 1:
+                PE(["k%d" % p, "cb%d" % CE], [PK2[p]],
+                   *[mm(P[:, 1024:1072], comb(CE, i), cond[p][:, i:H:16], i == 0, i == 15) for i in range(16)])
+            elif p == 0:
+                PE(["k0", "cb%d" % CE], [PK2[0]],
+                   *[mm(P[:, 1024:1032], comb(CE, i), cond[0][:, i:128:16], i == 0, i == 15) for i in range(16)])
+                S([PK2[0]], ["HT"], ac(z("HT", s + 2, 40, 5), P[:, 1024:1032], AF.Copy))
+
+        def marks():
+            if k == RO * SP - 1:
+                return
+            f = []
+            for a, b in ((0, 512), (512, 768)):
+                if k:
+                    f.append(mm(P[:, a:b], z("IDN"), T.MM[:, H * p + a:H * p + b], True, False))
+                f += [mm(P[:, a:b], z("NI"), w[p][:, a:b], k == 0, False), mm(P[:, a:b], z("ESC"), cond[p][:, a:b], False, True)]
+            PE(["w%d" % p, "k%d" % p, "IDN", "NI", "ESC"] + (["m%d" % p] if k else []), [PK0[p]], *f)
+            S([PK0[p]], ["m%d" % p],
+              ac(T.MM[:, H * p:H * p + H], P[:, 0:768], AF.Sigmoid, bias=8064.0 if k else 8320.0, scale=256.0))
+
+        def xlist():
+            PE(["X%d" % p, "COMBX"], [LK[p]],
+               *[mm(LP[p][:, 0:48], combx(i), X[p][:, i:H:16], False, i == 15) for i in range(16)])
+        if s < SP - 1:
+            marks()
+            xlist()
+            esc_list()
+            return None
+        esc_list()
+        xlist()
+        return marks
+
+    def v5(p, idx, rnd):
+        off, ck = lists(p, idx)
+        if rnd == 0:
+            V([LK[p]], [ck], cp(off, LP[p][:, 0:48]))
+        else:
+            t = z("CIT", 48 * p, 48 * p + 48)
+            V([LK[p]], ["cit%d" % p], cp(t, LP[p][:, 0:48]))
+            V(["cit%d" % p], ["cit%d" % p], ts(t, t, 4095, BA))
+            V(["cit%d" % p], [ck], cp(off, t))
+
+    nxt = T.cores[(rank + 1) % len(T.cores)]
+    rid, pid = topo.addr(nxt, core)
+    rmask, ne = topo.mask(core, nxt), len(topo.engines(core, nxt))
+
+    for rnd in range(RO):
+        base = 5 * rnd
+        for s in range(SP):
+            k, idx = rnd * SP + s, base + s
+            for p in (0, 1):
+                if s:
+                    v5(p, idx, rnd)
+                p1(p, idx, k)
+                drain(7 if k and p else 0)
+            if k == 0:
+                late_a()
+            V(["c%d_0" % idx], ["DL"], cp(z("DL", s + 1, 40, 5), T.CL[:, idx * 96:idx * 96 + 8]))
+            for p in (0, 1):
+                mk = p2(p, idx, k)
+                if mk and p == 0:
+                    mk()
+                drain(4 if p == 0 else 0)
+            if k == SP:
+                zeros()
+        drain(len(todo))
+        i4 = base + SP
+        LA, LB = T.LAp, T.LBp
+        nl = T.CL[:, i4 * 96:i4 * 96 + 8]
+        nk = "c%d_0" % i4
+        V([PK2[0]], ["E16a"], cp(z("E16", 0, 48), T.PA[:, 1024:1072]))
+        v5(0, i4, rnd)
+        V([PK2[1]], ["E16b"], cp(z("E16", 48, 96), T.PB[:, 1024:1072]))
+        v5(1, i4, rnd)
+        PE(["E16a", "E16b", "LTB", "NI2K", "BM"], ["#LA"], mm(LA[:, 128:224], z("LTB"), z("E16"), True, False),
+           mm(LA[:, 128:224], z("NI2K"), z("E16"), False, True), mm(LA[:, 256:352], z("BM"), z("E16"), True, True))
+        off, ck = lists(0, i4)
+        S(AUXK + [ck], ["A20"], ac(T.A2[:, 0:H], T.AUX[:, 0:2304].indirect(off), AF.Copy))
+        mk()
+        off, ck = lists(1, i4)
+        S(AUXK + [ck], ["A21"], ac(T.A2[:, H:1536], T.AUX[:, 0:2304].indirect(off), AF.Copy))
+        DUM = "DUM%d" % rnd
+        t2("hd", "HT", "DL", OP.mult)
+        V(["HT", "E16a"], ["CAND"], tt(z("CAND", 0, 8), z("HT", 4, 40, 5), z("E16", 0, 8), OP.is_gt),
+          tt(z("CAND", 8, 16), z("HT", 4, 40, 5), z("E16", 0, 8), OP.is_gt))
+        t2("d1", "DL", "hd", OP.subtract)
+        V(["#LA", "Z96", "CS"], ["CS1"],
+          lambda e: e.tensor_tensor_scan(z("CS", 1, 97), LA[:, 256:352], z("Z96"), 0.0, OP.add, OP.add))
+        V(["#LA", "CS", "CS1"], ["CNT"], tt(z("CNT"), LA[:, 128:224], z("CS", 0, 96), OP.add))
+        tz("OKT", "CNT", -1663.5, OP.is_le)
+        t2("TT", "CNT", "J2", OP.subtract)
+        t2("TT2", "TT", "OKT", OP.mult)
+        t2("POSF", "TT2", "J3", OP.add)
+        V(["POSF"], ["POS"], cp(z("POS"), z("POSF")))
+        S(["LBB", "POS", "SW"], ["SW"], ac(T.SW[:, :].indirect(z("POS", 48, 96)), T.LBB[:, :], AF.Sigmoid))
+        V(LBK + ["POS", "VW"], ["VW"], cp(T.VW[:, :].indirect(z("POS", 0, 48)), T.LBA[:, :]))
+        PE(["VW", "cb%d" % CSA], ["#LA"],
+           *[mm(LA[:, 384:408], comb(CSA, i), T.VW[:, i:384:16], i == 0, False) for i in range(16)])
+        S(["SW"], ["SWb"], ac(z("SWb"), T.SW[:, 0:384], AF.Copy))
+        PE(["SWb", "cb%d" % CSB], ["#LA"],
+           *[mm(LA[:, 384:408], comb(CSB, i), z("SWb", i, 384, 16), False, i == 15) for i in range(16)])
+        V(["HT", "d1"], ["FS"], lambda e: e.tensor_tensor_scan(z("FS"), z("HT"), z("d1"), 0.0, OP.mult, OP.add))
+        V(["FS", "DL", DUM], ["KT"], tt(z("KT", 0, 8), z("FS", 3, 40, 5), z(DUM, 0, 8), OP.subtract),
+          tt(z("KT", 8, 16), z("DL", 4, 40, 5), z(DUM, 0, 8), OP.subtract))
+        t2("KT2", "KT", "CAND", OP.mult)
+        t2("KK", "KT2", DUM, OP.add)
+        V(["KK"], ["FK"], cp(z("FK"), z("KK")))
+        S(AUXK + ["FK"], ["XF"], ac(z("XF"), T.AUX[:, :].indirect(z("FK")), AF.Copy))
+        SND, RCV = T["SND%d" % rnd], T["RCV%d" % rnd]
+        sk, rk = "SND%d" % rnd, "RCV%d" % rnd
+        V(["#LA"], ["LNE"], ts(z("LNE"), LA[:, 384:408], -2048.0, OP.add, 0.0, OP.max))
+        V(["#LA"], ["T1"], ts(z("T1"), LA[:, 384:408], 2047.5, OP.is_ge))
+        V(["#LA"], [sk + "b"], ts(SND[:, 384:408], LA[:, 384:408], 2047.5, OP.is_ge))
+        S(["A20", "A21", "LNE"], [sk + "a"], ac(SND[:, 0:384], T.A2[:, :].indirect(z("LNE")), AF.Copy))
+        width = 408
+        if rnd == 0:
+            V(["m0", "m1", "LNE"], [sk + "c"], cp(SND[:, 408:792], T.MM[:, 0:1536].indirect(z("LNE"))))
+            width = 792
+        do_waits("q", [sk + c for c in "abc"[:2 if rnd else 3]], [])
+        g.remote_dma(RCV[:, 0:width], SND[:, 0:width], T.sem["arr%d" % rnd], T.sem["snt%d" % rnd], pid, rid, rmask)
+        used["snt%d" % rnd] = ne
+        used["arr%d" % rnd] = ne
+        record(("rem%d" % rnd, "arr%d" % rnd, ne, {}), [], [rk])
+        V(["#LA", "JD2"], ["LNF"], tt(z("LNF"), LA[:, 384:408], z("JD2"), OP.subtract))
+        S(WTK + [nk], ["ug"], ac(z("ug"), T.WT[:, 0:2304].indirect(nl), AF.Copy))
+        t2("PRE", "LNF", "T1", OP.mult)
+
+        for h in (0, 1):
+            f = []
+            xf = z("XF", 128 * h, 128 * h + 128)
+            for gg in range(8):
+                o = PX[h][:, 128 * gg:128 * gg + 128]
+                f += [mm(o, T.SELK[:, 128 * gg:128 * gg + 128], xf, True, False),
+                      mm(o, xf, T.NSELK[:, 128 * gg:128 * gg + 128], False, False), mm(o, z("IDN"), z("TRI"), False, True)]
+            PE(["XF", "IDN", "TRI"] + [c + "SELK%d" % i for i in range(8) for c in ("", "N")], [PK0[h]], *f)
+        V(["#A0"], ["EQF"], ts(T.EQF[:, :], T.PA[:, 0:1024], 0.0, OP.is_equal))
+        S(["#B0"], ["ABD"], ac(T.ABD[:, :], T.PB[:, 0:1024], AF.Abs))
+        S(["ABD"], ["EQD"], ac(T.EQD[:, :], T.ABD[:, :], AF.Relu, bias=1.0, scale=-1.0))
+        oh = LB[:, 256:384]
+        PE(["k0", "BID", "E0", "ONES"], ["#LB"], mm(oh, z("BID"), cond[0][:, 0:128], True, False), mm(oh, z("E0"), z("ONES"), False, True))
+
+        def dup(h, EQ, ek):
+            o = PX[h][:, 1024:1152]
+            PE([ek, "OB", "XF", "CANDM"], [PK2[h]],
+               *([mm(o, z("OB", 112 - 16 * gg, 240 - 16 * gg), EQ[:, 128 * gg:128 * gg + 128], gg == 0, False) for gg in range(8)]
+                 + [mm(o, z("CANDM"), z("XF", 128 * h, 128 * h + 128), False, True)]))
+
+        def winners(h):
+            P = PX[h]
+            V([PK2[h]], ["AR%d" % h], ts(z("AR", 128 * h, 128 * h + 128), P[:, 1024:1152], -0.5, OP.is_lt))
+            PE(["AR%d" % h, "cb%d" % C0], [PK2[h]],
+               *[mm(P[:, 1280:1288], comb(C0, i), z("AR", 128 * h + i, 128 * h + 128, 16), i == 0, i == 15) for i in range(16)])
+
+        def offsets(h, o1, o2, off):
+            V([PK2[h], "KT2"], [o1], tt(z(o1), PX[h][:, 1280:1288], z("KT2", 8 * h, 8 * h + 8), OP.mult))
+            V([o1, DUM], [o2], tt(z(o2), z(o1), z(DUM, 0, 8), OP.add))
+            V([o2], [off], cp(z(off), z(o2)))
+        dup(0, T.EQF, "EQF")
+        winners(0)
+        V(["#LB", "AR0"], ["OA"], tt(z("OA"), oh, z("AR", 0, 128), OP.mult))
+        S(["OA"], ["nOA"], ac(z("nOA"), z("OA"), AF.Identity, bias=1.0, scale=-1.0))
+        scaled("OA2", "OA", 2.0, "OA")
+        offsets(0, "AO", "AO2", "OFF")
+        dup(1, T.EQD, "EQD")
+        wc = 2048 + 128 * rnd
+        tz("i_u", "ug", 0.53, OP.mult, 0.45, OP.add)
+        V(WTK + ["OFF", "nOA"], ["tg"], tt(z("tg"), T.WT[:, :].indirect(z("OFF")), z("nOA"), OP.mult))
+        winners(1)
+        if rnd == 0:
+            V(STK + ["OFF", "nOA"], ["tS"], tt(z("tS"), T.ST[:, :].indirect(z("OFF")), z("nOA"), OP.mult))
+            t2("qS", "OA", "WR", OP.mult)
+            V(STK + [nk], ["Sc"], cp(z("Sc"), T.ST[:, 0:2304].indirect(nl)))
+            S(AUXK + [nk], ["XC"], ac(z("XC"), T.AUX[:, 0:2304].indirect(nl), AF.Copy))
+            o = T.PA[:, 1408:1536]
+            PE(["SH16", "tS", "qS", "XF", "cb%d" % CF], ["#A2"], mm(o, z("SH16"), z("tS"), True, False),
+               mm(o, z("SH16"), z("qS"), False, False), mm(o, comb(CF, 15), z("XF", 0, 128), False, True))
+            PE(["OA", "cb%d" % C0], ["#A0"], mm(T.PA[:, 0:128], comb(C0, 0), z("OA"), True, False),
+               mm(T.PA[:, 0:128], comb(C0, 1), z("OA"), False, True))
+            o = T.PB[:, 0:128]
+            PE(AUXK + ["XF", "N01", "cb%d" % C7, "cb%d" % C8], ["#B0"], mm(o, comb(C7, 0), T.AUX[:, 2048:2176], True, False),
+               mm(o, comb(C8, 1), T.AUX[:, 2048:2176], False, False), mm(o, z("N01"), z("XF", 0, 128), False, True))
+            o = T.PB[:, 1408:1536]
+            PE(["SH16", "Sc", "XC", "cb%d" % CID], ["#B2"], mm(o, z("SH16"), z("Sc"), True, False),
+               mm(o, comb(CID, 15), z("XC"), False, True))
+            S(["#A2"], ["xs"], ac(z("xs"), T.PA[:, 1408:1536], AF.Copy))
+            S(["#A0"], ["FLs"], ac(z("FLs"), T.PA[:, 0:128], AF.Copy))
+            S(["#B2"], DTK, ac(T.DT[:, 2048:2176], o, AF.Copy))
+            scaled("xt", "XC", *late["keep"])
+        V(["tg", "OA2", "OFF"], WTK, tt(T.WT[:, :].indirect(z("OFF")), z("tg"), z("OA2"), OP.add))
+        V(["#LB", "AR1"], ["OBm"], tt(z("OBm"), oh, z("AR", 128, 256), OP.mult))
+        PE(["OBm", "ID2"], ["#LA"], mm(LA[:, 256:384], z("ID2"), z("OBm"), True, True))
+        offsets(1, "BO", "BO2", "OFD")
+        if rnd == 0:
+            tz("i_k", "xs", 1.0 / 4096, OP.mult)
+            V(["FLs", "#B0"], ["fd"], tt(z("fd"), z("FLs"), T.PB[:, 0:128], OP.mult))
+            tz("kk", "i_k", -4096.0, OP.mult)
+        V(WTK + ["OFD", "OBm"], ["s1"], tt(z("s1"), T.WT[:, :].indirect(z("OFD")), z("OBm"), OP.add))
+        if rnd == 0:
+            V(["XF", "fd", "OFF"], AUXK, tt(T.AUX[:, :].indirect(z("OFF")), z("XF", 0, 128), z("fd"), OP.add))
+        V(["s1", "#LA"], ["s2"], tt(z("s2"), z("s1"), LA[:, 256:384], OP.max))
+        if rnd == 0:
+            V(["kk", "xs", "OFF"], DTK, tt(T.DT[:, :].indirect(z("OFF")), z("kk"), z("xs"), OP.add))
+        tz("s3", "s2", 16.0, OP.min)
+        if rnd == 0:
+            V(["xt"] + AUXK, AUXK, tt(T.AUX[:, 2048:2176], z("xt"), T.AUX[:, 2048:2176], OP.add))
+        V(["s3", "OFD"], WTK, cp(T.WT[:, :].indirect(z("OFD")), z("s3")))
+        V(["i_u", "AR0"], WTK, tt(T.WT[:, wc:wc + 128], z("i_u"), z("AR", 0, 128), OP.mult))
+        V([nk, "c%d_1" % i4], ["CLF"], cp(z("CLF"), T.CL[:, i4 * 96:i4 * 96 + 96]))
+
+        def counts_out(a, b, q):
+            V(WTK, ["yn%d" % a], ts(T.YN[:, a:b], T.WT[:, a:b], -1.0, OP.add, 0.0, OP.max))
+            dma(q, ["yn%d" % a], [], (T.yn[:, a:b], T.YN[:, a:b]))
+        if rnd == RO - 1:
+            counts_out(0, 1152, "s")
+        V([rk, "PRE"], ["RX1"], tt(z("RX1"), RCV[:, 384:408], z("PRE"), OP.mult))
+        t2("RX2", "RX1", "JD", OP.add)
+        V(["RX2"], ["TO"], cp(z("TO"), z("RX2")))
+        V([rk, "TO", "LW"], ["LW"], cp(T.LW[:, :].indirect(z("TO")), RCV[:, 0:384]))
+        PE(["LW", "cb%d" % CLK], ["#LB"], *[mm(LB[:, 128:224], comb(CLK, i), T.LW[:, i:1536:16], i == 0, i == 15) for i in range(16)])
+        if rnd == 0:
+            V([rk, "TO", "m0", "m1"], ["m0", "m1"], cp(T.MM[:, :].indirect(z("TO")), RCV[:, 408:792]))
+        else:
+            counts_out(1152, 2304, "s")
+        V(["#LB", "CLF"], ["cit0", "cit1"], tt(z("CIT"), LB[:, 128:224], z("CLF"), OP.max))
+        V(["cit0", "cit1"], ["cit0", "cit1"], ts(z("CIT"), z("CIT"), 4095, BA))
+        if rnd < RO - 1:
+            V(["cit0", "cit1"], ["c%d_0" % (i4 + 1), "c%d_1" % (i4 + 1)], cp(T.CL[:, (i4 + 1) * 96:(i4 + 2) * 96], z("CIT")))
+            V(["#LB"], ["HF"], ts(z("HF"), LB[:, 128:136], 4095.5, OP.is_ge))
+            V(["FS"], ["DL"], cp(z("DL", 0, 40, 5), z("FS", 4, 40, 5)))
+            V(["HF", "E16a"], ["HT"], tt(z("HT", 1, 40, 5), z("E16", 0, 8), z("HF"), OP.subtract))
+        else:
+            V(["cit0", "cit1"], ["YC"], cp(z("YC"), z("CIT")))
+            dma("y", ["YC"], [], (T.yc[:, :], z("YC")))
+
+    for q in ("v", "s", "t", "q"):
+        g.wait_ge(T.sem[q], cnt[q])
+    for name, val in used.items():
+        g.wait_ge(T.sem[name], val)

@@ -1,11 +1,19 @@
-from concourse.mybir import AluOpType, ActivationFunctionType
+from concourse.mybir import AluOpType, ActivationFunctionType, AxisListType
 
 OP = AluOpType
 AF = ActivationFunctionType
 RO, SP = 2, 4
 NW = 2560
+OD = 2176
 H = 768
+B0 = 1280.0
+TINY = 2.0 ** -20
+M23, M35 = 1.5 * 2 ** 23, 1.5 * 2 ** 35
 F32, B16, I32, F16, U16 = "float32", "bfloat16", "int32", "float16", "uint16"
+ROWS = [(a, 512, 8) for a in range(8)] + [(512 + a, H, 4) for a in range(4)]
+TURN = [("lo", 8 * r, (r, 2), (0, 32)) for r in range(2)] + [("q2", 4 * r - 8, (r, 4), (32, 48)) for r in range(4)]
+BACK = [("lo", 0), ("hi", -8), ("q0", 8), ("q1", 4), ("q2", 0), ("q3", -4)]
+MASKS = {"lo": (0, 8), "hi": (8, 16), "q0": (0, 4), "q1": (4, 8), "q2": (8, 12), "q3": (12, 16)}
 SCRATCH = {}
 WHERE = {}
 
@@ -23,27 +31,29 @@ def pool(buf, dtype, **kw):
     SCRATCH[buf] = ("sbuf", [128, o], dtype)
 
 
-sb(I32, tabI=2048, CI=2048, CPI=544, CPL=544)
-sb(F32, YB=2048, ST=NW, DT=NW, Y0=H, Y1=H, LBB=H, SW=1920)
-sb(B16, W1=2048, WT=NW, AUX=NW, VV=12288, w0=H, w1=H, n0=H, n1=H, x0=H, x1=H, k0=H, k1=H, MM=1920, YN=2304, BIT=10240, LBA=H,
-   VW=1920, A2=1536, SND0=792, SND1=792, RCV0=792, RCV1=792, LW=1920, SELK=1024, NSELK=1024, EQF=1024, EQD=1024, ABD=1024,
-   COMB=1440, ZB=1536, FB=2048)
-sb(F16, X0=H, X1=H, COMBX=144)
+sb(I32, tabI=2048, CI=2048, CPI=416, CPL=288, BI=640)
+sb(F32, YB=2048, ST=NW, DT=OD + NW, LBB=H, SW=4608)
+sb(B16, WT=NW, AUX=NW, AUF=OD, VV=12288, VL=1024, w0=H, w1=H, k0=H, k1=H, MM=1920, YN=2304, BB=640, LBA=1024,
+   VW=4608, A2=1552, SND0=816, SND1=400, RCV0=816, RCV1=400, LW=1536, SELK=1024, NSELK=1024, EQF=1024, EQD=1024, ABD=1024,
+   COMB=864)
+sb(F16, X0=H, X1=H, COMBX=144, SH=2048, BC=1536, FB=2048, TU=960)
 sb(U16, CL=960)
-pool("zi", I32, CXI=96, CIT=96, i_rm=16, i_pc=16, i_g8=8, i_bm=128, i_dp=128, i_sf=128, i_wr=128, i_k=128, i_u=128)
-pool("zf", F32, RM=16, PC=1, G8=8, SH32=128, JI=96, JL=96, J2=96, J3=96, JD=24, JD2=24, DUM0=16, DUM1=16, CLF=96, YC=96, HT=40,
-     DL=40, hd=40, d1=40, FS=40, KT=16, KT2=16, KK=16, CAND=16, CS=104, Z96=96, CNT=96, OKT=96, TT=96, TT2=96, POSF=96, PRE=24,
-     LNF=24, T1=24, RX1=24, RX2=24, AO=8, AO2=8, BO=8, BO2=8, HF=8, xs=128, kk=128, K8=8, NK8=8, COLS=64, ZF=512, d0c=1)
-pool("zb", B16, BM=128, IDN=128, NI=128, LT=128, LTB=128, TRI=128, R15=128, ESC=128, CANDM=128, BID=128, N01=128, NI2K=128,
-     U1=128, U2=128, LTu=128, SELF=128, SF2=128, E0=128, ID2=128, ONES=128, OB=240, SWb=384, E16=96, HB=544, LB=544, XF=256,
-     XC=128, AR=256, OA=128, nOA=128, OA2=128, OBm=128, tg=128, s1=128, s2=128, s3=128, ug=128, FLs=128, fd=128, xt=128)
-pool("zh", F16, SH16=128, WR=128, tS=128, qS=128, Sc=128)
-pool("zu", U16, POS=96, LNE=24, TO=24, FK=16, OFF=8, OFD=8)
-for nm, nc in (("PA", 1536), ("PB", 1536), ("LAp", 512), ("LBp", 512)):
+pool("zi", I32, CXI=96, i_rm=16, i_pc=16, i_g8=8, i_bm=128, i_dp=160, i_sf=144, i_wr=128, i_jc=64)
+pool("zf", F32, RM=16, PC=1, G8=8, JI=96, JL=96, JQ=96, JD=24, DUM0=16, DUM1=16, CLF=96, YC=96, HT=40, FC=128,
+     DL=40, hd=40, d1=40, FS=40, KT=16, KT2=16, KK=16, CAND=16, D1=96, POSF=96, PRE=24, E8=8, MK=8, KB=1,
+     LNF=24, T1=24, RX1=24, RX2=24, AO=8, AO2=8, BO=8, BO2=8, HF=8, xs=128, kk=128, COLS=64, ZF=384,
+     a1=128, y=128, mx=96, rr=96, cc=96)
+pool("zb", B16, BM=128, IDN=128, NLT=128, NUT=128, N16=128, TRI=128, CANDM=128, BID=128, U1=128, U2=128, LTu=128, LTB=128,
+     SELV=144, OB=240, SWb=384, EB=112, HB=288, LB=288, XF=256, AR=256, OA=128, nOA=128, OA2=128, OBm=128, tg=128,
+     s1=128, s2=128, s3=128, ug=128, u2=128, ZB=384)
+pool("zh", F16, SH16=128, ID16=128, NI16=128, IDW=160, SELH=144, WR=128, tS=128, qS=128, QB=112, C16=96, RT=96, a16=128,
+     UU=128, eb=128, FH=128)
+pool("zu", U16, POS=96, POG=96, LNE=24, TO=24, FK=16, OFF=8, OFD=8, XL=96, FL=128)
+for nm, nc in (("PA", 1024), ("PB", 1024), ("PM", 1024), ("LA", 512), ("LB", 512)):
     SCRATCH[nm] = ("psum", [128, nc], F32)
 
 SEMAPHORES = ["v", "s", "t", "q", "arr0", "arr1", "snt0", "snt1"] + ["d%d" % i for i in range(60)]
-CA, CE, CF, CID, CSA, CSB, CLK, C0, C7, C8 = range(10)
+C1, CID, CSA, CSB, CLK, C0 = range(6)
 
 
 def rank_program(g, core, T, topo):
@@ -63,7 +73,7 @@ def rank_program(g, core, T, topo):
         for k in W:
             if k[0] != "#":
                 ws, rs = res.get(k, ([], []))
-                deps += ws + [e for e in rs if e[0] != q]
+                deps += ws + rs
         for k in list(R) + list(W):
             if k[0] == "#":
                 deps += [e for e in acc.get(k, []) if e[0] != q]
@@ -108,9 +118,9 @@ def rank_program(g, core, T, topo):
         used[name] = 16 * len(pairs)
         record((name, name, 16 * len(pairs), dict(know[q])), R, W)
 
-    def z(name, a=0, b=None, st=1):
+    def z(name, a=0, b=None, st=1, p=128):
         buf, o, n = WHERE[name]
-        return T[buf][:, o + a:o + (n if b is None else b):st]
+        return T[buf][0:p, o + a:o + (n if b is None else b):st]
 
     def ts(out, a, s1, o1, s2=None, o2=None):
         if o2 is None:
@@ -132,6 +142,9 @@ def rank_program(g, core, T, topo):
     def mm(out, l, r, st, sp):
         return lambda e: e.matmul(out, l, r, st, sp)
 
+    def group(*terms):
+        return [mm(o, l, r, j == 0, j == len(terms) - 1) for j, (o, l, r) in enumerate(terms)]
+
     def V(R, W, *f):
         op("v", R, W, *f)
 
@@ -147,26 +160,35 @@ def rank_program(g, core, T, topo):
     def t2(out, a, b, o):
         V([a, b], [out], tt(z(out), z(a), z(b), o))
 
-    PX, LP = [T.PA, T.PB], [T.LAp, T.LBp]
-    PK0, PK2, LK = ["#A0", "#B0"], ["#A2", "#B2"], ["#LA", "#LB"]
-    w, n, x, cond, X, Y = ([T["%s%d" % (a, p)] for p in (0, 1)] for a in ("w", "n", "x", "k", "X", "Y"))
-    AUXK = ["AUX"] + ["ar%d" % i for i in range(10)]
+    PX, LP, PK, LK = [T.PA, T.PB], [T.LA, T.LB], ["#A", "#B"], ["#LA", "#LB"]
+    LA, LB, PM = T.LA, T.LB, T.PM
+    w, cond, X = ([T["%s%d" % (a, p)] for p in (0, 1)] for a in ("w", "k", "X"))
+    AUXK = ["AUX"] + ["ar%d" % i for i in range(6)]
 
     def comb(v, i):
         return T.COMB[:, v * 144 + 15 - i:v * 144 + 143 - i]
 
-    def combx(i):
-        return T.COMBX[:, 15 - i:143 - i]
+    def combed(out, v, src, n):
+        return [(out, comb(v, i), src(i, n, 16)) for i in range(16)]
 
     def RMc(r):
         return z("RM", r, r + 1)
 
-    dma("y", [], ["cpF"], (T.CPI[:, 256:384], T.suf[:, :]))
-    dma("s", [], ["cpT"], (T.CPI[:, 0:128], T.tab[0:128:16, :]))
-    dma("y", [], ["cpL"], (T.CPI[:, 128:256], T.lnk[:, :]))
-    for k in range(4):
-        dma("s" if k % 2 == 0 else "y", [], ["tab%d" % k], (T.tabI[:, 512 * k:512 * k + 512], T.tab[:, 512 * k:512 * k + 512]))
+    def turn(mask, shift):
+        o = 160 * list(MASKS).index(mask) + 16 - shift
+        return T.TU[:, o:o + 128]
+
+    def tab_load(k, q):
+        dma(q, [], ["tab%d" % k], (T.tabI[:, 512 * k:512 * k + 512], T.tab[:, 512 * k:512 * k + 512]))
+    tab_load(0, "s")
     dma("y", [], ["CXI"], (z("CXI"), T.cx[:, :]))
+    tab_load(1, "y")
+    dma("s", [], ["vv0"], (T.VV[0:8, 0:6144], T.vv[:, 0:6144]))
+    tab_load(2, "s")
+    tab_load(3, "y")
+    dma("y", [], ["cpF"], (T.CPI[:, 288:416], T.suf[:, :]))
+    dma("y", [], ["cpL"], (T.CPI[:, 0:128], T.lnk[:, :]))
+    dma("y", [], ["vv1"], (T.VV[0:8, 6144:12288], T.vv[:, 6144:12288]))
 
     def iota(tile, key, pattern, base, cm, **kw):
         op("q", [], [key], lambda e: e.iota(tile, pattern, base, cm, **kw))
@@ -174,40 +196,59 @@ def rank_program(g, core, T, topo):
     iota(z("i_rm"), "i_rm", [[-1, 16]], 0, 1)
     iota(z("i_g8"), "i_g8", [[-16, 8]], 0, 1)
     iota(z("i_bm"), "i_bm", [[-16, 8], [0, 16]], 0, 1)
-    iota(z("i_dp"), "i_dp", [[1, 128]], 0, -1)
-    iota(z("i_sf"), "i_sf", [[1, 128]], -15, -16)
-    iota(T.CPI[:, 384:512], "cpj", [[1, 128]], 0, 128)
-    iota(T.CPI[:, 512:544], "cpk", [[1, 32]], 0, 32)
+    iota(z("i_dp"), "i_dp", [[1, 160]], -16, -1)
+    iota(z("i_sf"), "i_sf", [[1, 144]], -15, -16)
     iota(z("i_pc"), "i_pc", [[0, 16]], 0, 1)
+    iota(T.DT[:, 0:OD], "DF", [[0, OD]], 0, 0, **fl)
+    iota(T.CPI[:, 128:256], "cpj", [[1, 128]], 0, 128)
+    iota(T.CPI[:, 256:288], "cpk", [[1, 32]], 0, 32)
+    iota(z("i_jc"), "i_jc", [[1, 64]], 0, 64)
     iota(z("JI"), "JI", [[16, 96]], 0, 0, **fl)
     iota(z("i_wr"), "i_wr", [[1, 128]], 0, 0)
-    for i in range(10):
-        iota(T.BIT[:, 1024 * i:1024 * i + 1024], "bit%d" % i, [[0, 1024 >> (i + 1)], [1, 2], [0, 1 << i]], 0, 0, **fl)
+    iota(T.LBA[:, :], "LBA", [[0, 1024]], 1, 0, **fl)
+    iota(T.ST[:, 2048:NW], "STz", [[0, 512]], 0, 0, **fl)
+    for tile, sg in (("SELK", 1.0), ("NSELK", -1.0)):
+        iota(T[tile][:, :], tile, [[0, 1024]], 0, 0, **fl)
+        for r, wt in ((7, 32.0), (8, 1.0)):
+            op("q", [tile], [tile], lambda e, tile=tile, r=r, c=sg * wt: e.affine_select(
+                T[tile][:, :], T[tile][:, :], [[-16, 8], [0, 128]], OP.not_equal, c, -r, 1))
 
     SR, BA = OP.logical_shift_right, OP.bitwise_and
+    dp = z("i_dp", 16, 144)
     V([], ["AUX"], ms(T.AUX[:, :], 0.0))
-    V([], ["COMB"], ms(T.COMB[:, :], 0.0))
-    V([], ["COMBX"], ms(T.COMBX[:, :], 0.0))
     tz("i_rm", "i_rm", 15, BA)
     tz("i_g8", "i_g8", 4, OP.arith_shift_right)
     tz("i_bm", "i_bm", 4, OP.arith_shift_right)
     tz("RM", "i_rm", 0.0, OP.is_equal)
     tz("G8", "i_g8", 0.0, OP.is_equal)
     tz("BM", "i_bm", 0.0, OP.is_equal)
-    tz("U1", "i_dp", -1.0, OP.is_equal)
-    tz("IDN", "i_dp", 0.0, OP.is_equal)
-    tz("LTu", "i_dp", 0.0, OP.is_ge)
+    V([], ["COMB"], ms(T.COMB[:, :], 0.0))
+    tz("SELV", "i_sf", 0.0, OP.is_equal, 1.0 / 16, OP.mult)
+    for name, c, o in (("U1", -1.0, OP.is_equal), ("IDN", 0.0, OP.is_equal), ("LTu", 0.0, OP.is_ge), ("ID16", 0.0, OP.is_equal)):
+        V(["i_dp"], [name], ts(z(name), dp, c, o))
+    V([], ["COMBX"], ms(T.COMBX[:, :], 0.0))
     t2("U1", "U1", "BM", OP.mult)
+    V(["G8", "COMB"], ["cb%d" % C1], cp(T.COMB[:, C1 * 144 + 15:C1 * 144 + 143:16], z("G8")))
+    t2("SH16", "IDN", "U1", OP.subtract)
     V(["G8", "COMBX"], ["COMBX"], cp(T.COMBX[:, 15:143:16], z("G8")))
-    tz("SELF", "i_sf", 0.0, OP.is_equal, 32.0, OP.mult)
-    tz("SF2", "i_sf", -128.0, OP.is_equal)
-    t2("SH32", "U1", "IDN", OP.subtract)
-    t2("SELF", "SELF", "SF2", OP.add)
     t2("LTB", "LTu", "BM", OP.mult)
-    V([], ["ONES"], ms(z("ONES"), 1.0))
     V([], ["WTz"], ms(T.WT[:, 2048:NW], 0.0))
-    V([], ["DTz"], ms(T.DT[:, 2048:2304], 0.0))
-    V([], ["DL"], ms(z("DL"), 0.0))
+    tz("IDW", "i_dp", 0.0, OP.is_equal, float(OD), OP.mult)
+    for j, (a, b) in enumerate(MASKS.values()):
+        V(["RM"], ["mk%d" % j], lambda e, j=j, a=a, b=b: e.tensor_reduce(z("MK", j, j + 1), z("RM", a, b), AxisListType.X, OP.add))
+
+    def early_a():
+        V(["CXI"], ["c0_0", "c0_1"], cp(T.CL[:, 0:96], z("CXI")))
+        V(["CXI"], ["C160", "C161"], ts(z("C16"), z("CXI"), -1024.0, OP.add))
+
+    def early_b():
+        V(["cpF"], ["FC"], ts(z("FC"), T.CPI[:, 288:416], -1024.0, OP.add))
+        dma("y", ["FC", "DF"], ["DF"], (T.DT[15:128:16, 0:2048], z("FC")))
+        V(["IDW"] + ["mk%d" % j for j in range(6)], ["TU"],
+          *[ts(T.TU[:, 160 * j:160 * j + 160], z("IDW"), z("MK", j, j + 1), OP.mult) for j in range(6)])
+
+    def early_c():
+        V(["BM", "RM"], ["BC"], *[ts(T.BC[:, 128 * a:128 * a + 128], z("BM"), RMc(a), OP.mult) for a in range(12)])
     ncol = [0]
 
     def column(terms):
@@ -227,88 +268,124 @@ def rank_program(g, core, T, topo):
     def scaled(out, a, col, key):
         S([a, key], [out], ac(z(out), z(a), AF.Copy, scale=col))
 
+    def root(p):
+        S(["C16%d" % p], ["RT%d" % p], ac(z("RT", 48 * p, 48 * p + 48), z("C16", 48 * p, 48 * p + 48), AF.Sigmoid,
+                                             bias=-256 * 1023.5, scale=-256.0))
+
+    S(["RM"], ["KB"], ac(z("KB"), RMc(15), AF.Identity, bias=4096 * B0 - 128, scale=1e9))
     colB, kB = column([(4, 1), (9, 1)])
     S(["AUX", kB], ["AUX"], ac(T.AUX[:, 0:2304], T.AUX[:, 0:2304], AF.Identity, bias=colB))
-    colR, kR = column([(15, 4096)])
     S(["AUX", "RM"], ["AUX"], ac(T.AUX[:, 2304:NW], T.AUX[:, 2304:NW], AF.Identity, bias=RMc(4)))
-    S(["AUX", kR], ["AUX"], ac(T.AUX[:, 0:1], T.AUX[:, 0:1], AF.Identity, bias=colR))
-    colF, kF = column([(15, -1152 - 4128)])
-    make_comb(CF, *column([(4, -1152 - 4128), (5, 32), (6, 1)]))
-    make_comb(CA, *column([(0, 32), (1, 1), (4, -4128)]))
-    make_comb(CE, RMc(15), "RM")
-    scaled("NI", "IDN", -1.0, "IDN")
-    scaled("LT", "LTB", 256.0, "LTB")
-    scaled("R15", "IDN", RMc(15), "RM")
-    scaled("ESC", "BM", *column([(15, -32)]))
 
-    b32 = 129.0 - 31.0 / 64
-    V(["cpj"], ["cpj"], ts(T.CPI[:, 384:512], T.CPI[:, 384:512], 2047, BA))
-    V(["cpk"], ["cpk"], ts(T.CPI[:, 512:544], T.CPI[:, 512:544], 511, BA))
-    V(["cpF", "cpL"], ["HBa"], ts(z("HB", 128, 384), T.CPI[:, 128:384], 1.0 / 32, OP.mult, b32, OP.add))
-    V(["cpT"], ["cpl0"], ts(T.CPL[:, 0:128], T.CPI[:, 0:128], 4, SR, 31, BA))
-    V(["cpF", "cpL", "cpj", "cpk"], ["cpl1"], ts(T.CPL[:, 128:544], T.CPI[:, 128:544], 31, BA))
-    V(["cpT"], ["HBb"], ts(z("HB", 0, 128), T.CPI[:, 0:128], 1.0 / 512, OP.mult, 129.0 - 511.0 / 1024, OP.add))
-    V(["cpl0", "cpl1"], ["LB"], cp(z("LB"), T.CPL[:, :]))
-    dma("y", ["HBa"], ["fb0"], (T.FB[0:8, :], z("HB", 256, 384)))
-    dma("y", ["LB"], ["fb1"], (T.FB[8:16, :], z("LB", 256, 384)))
-    V(["cpj"], ["HBc"], ts(z("HB", 384, 512), T.CPI[:, 384:512], 1.0 / 32, OP.mult, b32, OP.add))
-    V(["cpk"], ["HBd"], ts(z("HB", 512, 544), T.CPI[:, 512:544], 1.0 / 32, OP.mult, b32 + 64.0, OP.add))
-    for j, (r, key, t, a) in enumerate(((5, "HBa", "HB", 256), (6, "LB", "LB", 256), (0, "HBb", "HB", 0), (1, "LB", "LB", 0),
-                                        (2, "HBa", "HB", 128), (3, "LB", "LB", 128), (7, "HBc", "HB", 384), (8, "LB", "LB", 384))):
-        dma("y", [key, "AUX"], ["ar%d" % j], (T.AUX[r:128:16, 0:2048], z(t, a, a + 128)))
-    dma("y", ["HBd", "AUX"], ["ar8"], (T.AUX[7:128:16, 2048:NW], z("HB", 512, 544)))
-    dma("y", ["LB", "AUX"], ["ar9"], (T.AUX[8:128:16, 2048:NW], z("LB", 512, 544)))
-    for key, a, b in (("vv0", 0, 1536), ("vv1", 1536, 6144), ("vv2", 6144, 12288)):
-        dma("y", [], [key], *[(T.VV[i:128:16, a:b], T.vv[:, a:b]) for i in range(16)])
+    def targets(rnd):
+        o = WHERE["SELV"][1]
+        for hs in range(8):
+            b = (8 * rnd + hs) * H
+            PE(["vv%d" % rnd, "SELV"], ["#M"], *group(*[(PM[:, 64 * hs:64 * hs + 64], T.zb[0:8, o + 15 - a:o + 143 - a],
+                                                         T.VV[0:8, b + c0:b + c1:st]) for a, (c0, c1, st) in enumerate(ROWS)]))
+        S(["#M"], ["VL%d" % rnd], ac(T.VL[:, 512 * rnd:512 * rnd + 512], PM[:, 0:512], AF.Copy))
 
-    for k in range(4):
+    def counts(k):
+        a, b = 512 * k, 512 * k + 512
+        V(["tab%d" % k], ["ci%d" % k], ts(T.CI[:, a:b], T.tabI[:, a:b], 15, BA))
+        V(["ci%d" % k], ["wt%d" % k], ts(T.WT[:, a:b], T.CI[:, a:b], -1.0 / 16, OP.add, -TINY, OP.max))
+
+    def pointers(k):
         a, b = 512 * k, 512 * k + 512
         V(["tab%d" % k], ["yb%d" % k], ts(T.YB[:, a:b], T.tabI[:, a:b], -7.5, OP.add, 201326592.0, OP.add))
-        V(["tab%d" % k], ["ci%d" % k], ts(T.CI[:, a:b], T.tabI[:, a:b], 15, BA))
-        S(["yb%d" % k], ["st%d" % k], ac(T.ST[:, a:b], T.YB[:, a:b], AF.Identity, bias=-12584064.0, scale=0.0625))
-    pieces = [(k, 512 * k, PX[k // 2][:, 1024 * (k % 2):1024 * (k % 2) + 512], (PK0 if k % 2 == 0 else PK2)[k // 2]) for k in range(4)]
-    o = WHERE["SELF"][1]
-    for k, a, P, pk in pieces:
-        PE(["st%d" % k, "SH32", "SELF", "fb0", "fb1"], [pk], mm(P, z("SH32"), T.ST[:, a:a + 512], True, False),
-           mm(P, T.zb[0:16, o:o + 128], T.FB[0:16, a:a + 512], False, True))
-        V(["ci%d" % k], ["w1%d" % k], ts(T.W1[:, a:a + 512], T.CI[:, a:a + 512], 1.03, OP.mult, 128.48, OP.add))
-        V(["w1%d" % k], ["wt%d" % k], ts(T.WT[:, a:a + 512], T.W1[:, a:a + 512], -128.0, OP.add))
-    for k, a, P, pk in pieces:
-        S([pk, kF], ["dt%d" % k], ac(T.DT[:, a:a + 512], P, AF.Identity, bias=colF))
-    V(["CXI"], ["c0_0", "c0_1"], cp(T.CL[:, 0:96], z("CXI")))
-    WTK = ["WT", "WTz"] + ["wt%d" % k for k in range(4)]
-    DTK = ["DT", "DTz"] + ["dt%d" % k for k in range(4)]
+        S(["yb%d" % k], ["sh%d" % k], ac(T.SH[:, a:b], T.YB[:, a:b], AF.Identity, bias=-12583936.0, scale=0.0625))
+
+    def differences(k):
+        a, b = 512 * k, 512 * k + 512
+        P, pk = ((T.PA, "#A"), (T.PB, "#B"), (PM, "#M"), (PM, "#M"))[k]
+        PE(["sh%d" % k, "SH16"], [pk], mm(P[:, 0:512], z("SH16"), T.SH[:, a:b], True, True))
+        S([pk], ["dt%d" % k], ac(T.DT[:, OD + a:OD + b], P[:, 0:512], AF.Copy))
+    counts(0)
+    early_a()
+    root(0)
+    root(1)
+    scaled("NLT", "LTB", -1.0, "LTB")
+    scaled("N16", "IDN", -1.0 / 16, "IDN")
+    counts(1)
+    pointers(0)
+    counts(2)
+    pointers(1)
+    targets(0)
+    differences(0)
+    differences(1)
+    counts(3)
+    WTK = ["WT", "WTz", "WTn"] + ["wt%d" % k for k in range(4)]
+    DTK = ["DT", "DF", "DTn", "DFn"] + ["dt%d" % k for k in range(4)]
     STK = ["STz"] + ["st%d" % k for k in range(4)]
-    cR, nkR = column([(15, -1)])
-    S([nkR], ["d0c"], ac(z("d0c"), cR, AF.Identity, bias=1.0))
-    S(["d0c", "dt0"], ["dt0"], ac(T.DT[:, 0:1], T.DT[:, 0:1], AF.Copy, scale=z("d0c")))
+    AFK = ["AFn"] + ["af%d" % k for k in range(8)]
 
     def zeros():
-        dma("y", ["ZB", "VW"], ["VW"], (T.VW[:, 0:384], T.ZB[:, 0:384]))
-        dma("y", ["ZF", "SW"], ["SW"], (T.SW[:, 0:384], z("ZF", 0, 384)))
-        dma("y", ["ZB", "LW"], ["LW"], (T.LW[:, 0:1536], T.ZB[:, :]))
+        dma("y", ["ZB", "VW"], ["VW"], (T.VW[:, 0:384], z("ZB")))
+        dma("y", ["ZF", "SW"], ["SW"], (T.SW[:, 0:384], z("ZF")))
 
     def late_a():
+        b32 = 129.0 - 31.0 / 64
+        V(["cpj"], ["cpj"], ts(T.CPI[:, 128:256], T.CPI[:, 128:256], 2047, BA))
+        V(["cpk"], ["cpk"], ts(T.CPI[:, 256:288], T.CPI[:, 256:288], 511, BA))
+        tz("i_jc", "i_jc", 1023, BA)
+        V(["cpL", "cpj"], ["HBa"], ts(z("HB", 0, 256), T.CPI[:, 0:256], 1.0 / 32, OP.mult, b32, OP.add))
+        V(["cpL", "cpj", "cpk"], ["cpl"], ts(T.CPL[:, :], T.CPI[:, 0:288], 31, BA))
+        V(["cpk"], ["HBb"], ts(z("HB", 256, 288), T.CPI[:, 256:288], 1.0 / 32, OP.mult, b32 + 64.0, OP.add))
+        V(["cpl"], ["LB"], cp(z("LB"), T.CPL[:, :]))
+        for j, (r, key, t, a) in enumerate(((2, "HBa", "HB", 0), (3, "LB", "LB", 0), (7, "HBa", "HB", 128), (8, "LB", "LB", 128))):
+            dma("y", [key, "AUX"], ["ar%d" % j], (T.AUX[r:128:16, 0:2048], z(t, a, a + 128)))
+        dma("y", ["HBb", "AUX"], ["ar4"], (T.AUX[7:128:16, 2048:NW], z("HB", 256, 288)))
+        dma("y", ["LB", "AUX"], ["ar5"], (T.AUX[8:128:16, 2048:NW], z("LB", 256, 288)))
+
+    def late_0():
+        V(["cpF"], ["FH"], cp(z("FH"), T.CPI[:, 288:416]))
+        dma("y", ["FH"], ["FB"], (T.FB[0:8, :], z("FH")))
+        tz("i_pc", "i_pc", 15, BA)
+        V([], ["DL"], ms(z("DL"), 0.0))
         V([], ["HT"], ms(z("HT"), 0.0))
-        V([], ["ZB"], ms(T.ZB[:, :], 0.0))
+        V(["i_pc"], ["PC"], cp(z("PC"), z("i_pc", 0, 1)))
+        tz("SELH", "i_sf", 0.0, OP.is_equal)
+
+    def suffix_list(j):
+        o = WHERE["SELH"][1]
+        P = LB[:, 256 + 64 * j:320 + 64 * j]
+        PE(["FB", "SELH"], ["#LB"], *group(*[(P, T.zh[0:8, o + 15 - i:o + 143 - i], T.FB[0:8, 1024 * j + i:1024 * j + 1024:16])
+                                             for i in range(16)]))
+
+    def late_b():
+        V(["i_jc"], ["BI"], *[ts(T.BI[:, 64 * i:64 * i + 64], z("i_jc"), i, SR, 1, BA) for i in range(10)])
+
+    def late_b2():
+        V(["BI"], ["BB"], cp(T.BB[:, :], T.BI[:, :]))
+        for i in range(10):
+            dma("y", ["BB", "LBA"], ["lb%d" % i], (T.LBA[i:128:16, :], T.BB[:, 64 * i:64 * i + 64]))
+
+    def late_c():
+        V([], ["ZB"], ms(z("ZB"), 0.0))
         V([], ["ZF"], ms(z("ZF"), 0.0))
-        dma("y", ["ZB"], ["LBA"], (T.LBA[:, :], T.ZB[:, 0:H]))
-        dma("y", ["ZF"], ["STz"], (T.ST[:, 2048:NW], z("ZF")))
         zeros()
         V([], ["OB"], ms(z("OB"), 0.0))
-        V([], ["CS"], ms(z("CS", 0, 8), 0.0))
-        V([], ["Z96"], ms(z("Z96"), 0.0))
-        tz("i_pc", "i_pc", 15, BA)
-        tz("TRI", "i_dp", 0.0, OP.is_le, 8192.0, OP.mult)
-        tz("U2", "i_dp", 1.0, OP.is_equal)
-        V(["OB"], ["OB"], ms(z("OB", 112, 128), 1.0))
-        V(["i_pc"], ["PC"], cp(z("PC"), z("i_pc", 0, 1)))
-        tz("WR", "i_wr", 896.0, OP.add)
-        V(["SH32"], ["SH16"], cp(z("SH16"), z("SH32")))
-        t2("U2", "U2", "BM", OP.mult)
-        t2("BID", "U2", "IDN", OP.subtract)
+        V([], ["EB"], ms(z("EB", 0, 16), 0.0))
+        V([], ["QB"], ms(z("QB", 0, 16), 0.0))
+        V([], ["D1"], ms(z("D1"), 16.0))
+        V([], ["A2z"], ms(T.A2[:, 1536:1552], 0.0))
+        V([], ["mz"], ms(T.MM[:, 1536:1552], 0.0))
 
-    late, todo = {}, []
+    def late_d():
+        V([], ["SND0z"], ms(T.SND0[:, 384:432], 0.0))
+        V([], ["SND1z"], ms(T.SND1[:, 384:400], 0.0))
+        V(["i_dp"], ["TRI"], ts(z("TRI"), dp, 0.0, OP.is_le, 8192.0, OP.mult))
+        V(["OB"], ["OB"], ms(z("OB", 112, 128), 1.0))
+        V(["PC", "D1"], ["D1"], cp(z("D1", 0, 1), z("PC")))
+
+    def late_e():
+        V(["i_dp"], ["U2"], ts(z("U2"), dp, 1.0, OP.is_equal))
+        tz("WR", "i_wr", 1024.0, OP.add)
+        t2("U2", "U2", "BM", OP.mult)
+        t2("NUT", "LTB", "BM", OP.subtract)
+        t2("BID", "IDN", "U2", OP.subtract)
+
+    todo = []
 
     def drain(m):
         for _ in range(min(m, len(todo))):
@@ -317,319 +394,361 @@ def rank_program(g, core, T, topo):
     def later(f, *a):
         todo.append(lambda: f(*a))
 
-    def shifted(out, a, na, c, o=0):
-        S([a, "PC"], [out], ac(z(out, o, o + na), z(a, 0, na), AF.Identity, bias=c))
+    def shifted(out, a, na, c, o=0, i=0, scale=1.0):
+        S([a, "PC"], [out], ac(z(out, o, o + na), z(a, i, i + na), AF.Identity, bias=c, scale=scale))
 
     def later_comb(v, terms):
         later(lambda: make_comb(v, *column(terms)))
 
-    def key_tiles(gg):
-        for tile, kt in (("SELK", "K8"), ("NSELK", "NK8")):
-            S(["ONES", kt], [tile + str(gg)], ac(T[tile][:, 128 * gg:128 * gg + 128], z("ONES"), AF.Copy, scale=z(kt, gg, gg + 1)))
-
-    def lane_bits():
-        S(["LBA", "RM"], ["LBA"], ac(T.LBA[:, :], T.LBA[:, :], AF.Identity, bias=RMc(15)))
-        for i in range(10):
-            dma("y", ["bit%d" % i, "LBA"], ["lb%d" % i], (T.LBA[i:128:16, :], T.BIT[0:8, 1024 * i:1024 * i + H]))
-
     def slot_combs():
-        sa = column([(i, 1 << i) for i in range(10)] + [(15, 2048)])
+        sa = column([(i, 1 << i) for i in range(10)] + [(15, -1536)])
         make_comb(CSA, *sa)
         c = ncol[0]
         ncol[0] += 1
         S(["RM", sa[1]], ["colx"], ac(z("COLS", c, c + 1), RMc(15), AF.Identity, bias=sa[0], scale=768.0))
         make_comb(CSB, z("COLS", c, c + 1), "colx")
 
+    def smalls():
+        shifted("JL", "JI", 96, z("PC"))
+        for p in (0, 1):
+            shifted("JQ", "JL", 48, 1536.0, 48 * p, 0, 2.0)
+        shifted("JD", "JL", 24, 1536.0)
+        for t in range(2):
+            shifted("DUM%d" % t, "JL", 8, 2304.0 + 128 * t)
+            shifted("DUM%d" % t, "JL", 8, 2304.0 + 128 * t, 8)
+        scaled("NI16", "IDN", -1.0, "IDN")
+
     LBK = ["LBA"] + ["lb%d" % i for i in range(10)]
 
-    def keep():
-        late["keep"] = column([(0, 1), (1, 1), (2, 1), (3, 1)])
-    later(shifted, "JL", "JI", 96, z("PC"))
-    later(shifted, "J2", "JL", 96, -1663.0)
-    later(shifted, "J3", "JL", 96, 384.0)
-    later(shifted, "JD", "JL", 24, 1536.0)
-    later(shifted, "JD2", "JL", 24, 3584.0)
-    for t in range(2):
-        later(shifted, "DUM%d" % t, "JL", 8, 2304.0 + 128 * t)
-        later(shifted, "DUM%d" % t, "JL", 8, 2304.0 + 128 * t, 8)
-    later(scaled, "E0", "IDN", RMc(0), "RM")
-    later(scaled, "ID2", "IDN", 2.0, "IDN")
-    later(scaled, "NI2K", "IDN", -2048.0, "IDN")
-    later(lambda: scaled("CANDM", "BM", *column([(9, -1)])))
-    later_comb(CLK, [(2, 32), (3, 1), (4, -32)])
-    later_comb(CID, [(4, -1152 - 4128), (7, 32), (8, 1)])
-    for v, r in ((C0, 0), (C7, 7), (C8, 8)):
-        later(make_comb, v, RMc(r), "RM")
-    later(lambda: scaled("K8", "G8", *column([(7, 32), (8, 1)])))
-    later(scaled, "NK8", "K8", -1.0, "K8")
-    later(lane_bits)
-    later(lambda: scaled("N01", "NI", *column([(0, 1), (1, 1)])))
-    later(keep)
-    for gg in range(8):
-        later(key_tiles, gg)
+    def plain_pointers(k):
+        S(["yb%d" % k], ["st%d" % k], ac(T.ST[:, 512 * k:512 * k + 512], T.YB[:, 512 * k:512 * k + 512], AF.Identity,
+                                         bias=-12583936.0, scale=0.0625))
+
+    def suffix_aux(k):
+        S(AUXK + ["FL"], ["af%d" % k], ac(T.AUF[:, 256 * k:256 * k + 256], T.AUX[:, 0:2048].indirect(z("FL", 16 * k, 16 * k + 16)), AF.Copy))
+    later(smalls)
+    later(lambda: (scaled("CANDM", "BM", *column([(9, -1)])), make_comb(CLK, *column([(2, 32), (3, 1), (4, -32)])),
+                   make_comb(C0, RMc(0), "RM")))
     later(slot_combs)
-    later(lambda: S(LBK, ["LBB"], ac(T.LBB[:, :], T.LBA[:, :], AF.Identity, bias=-200.0, scale=400.0)))
+    later_comb(CID, [(4, -1024 - 4128), (7, 32), (8, 1)])
+    for k in range(8):
+        later(suffix_aux, k)
+    later(lambda: S(LBK, ["LBB"], ac(T.LBB[:, :], T.LBA[:, 0:H], AF.Identity, bias=-200.0, scale=400.0)))
 
     def lists(p, idx):
         return T.CL[:, idx * 96 + 48 * p:idx * 96 + 48 * p + 48], "c%d_%d" % (idx, p)
 
-    def p1(p, idx, k):
+    def zs(name, p, n=64, a=0, st=1):
+        return z(name, n * p + a, n * p + n, st)
+
+    def halves(P, l, src):
+        return [(P[:, 0:512], l, src[:, 0:512]), (P[:, 512:H], l, src[:, 512:H])]
+
+    def spread(P, src, p, close):
+        return [mm(P[:, c0:c1:st], T.BC[:, 128 * a:128 * a + 128], zs(src, p), False, close and a in (7, 11))
+                for a, (c0, c1, st) in enumerate(ROWS)]
+
+    def s0(p, idx, k):
         off, ck = lists(p, idx)
-        P = PX[p]
-        S(AUXK + [ck], ["x%d" % p], ac(x[p][:, :], T.AUX[:, 0:2304].indirect(off), AF.Copy))
         wi = T.WT[:, 0:2304].indirect(off)
-        V(WTK + [ck] + (["m%d" % p] if k else []), ["w%d" % p],
-          tt(w[p][:, :], wi, T.MM[:, H * p:H * p + H], OP.mult) if k else cp(w[p][:, :], wi))
-        PE(["w%d" % p, "BM"], [PK0[p]], mm(P[:, 0:512], z("BM"), w[p][:, 0:512], True, True),
-           mm(P[:, 512:768], z("BM"), w[p][:, 512:768], True, True))
-        PE(["x%d" % p, "cb%d" % CA], [LK[p]],
-           *[mm(LP[p][:, 0:48], comb(CA, i), x[p][:, i:H:16], i == 0, False) for i in range(16)])
-        S(["w%d" % p], ["n%d" % p], ac(n[p][:, :], w[p][:, :], AF.Relu, bias=-1.0))
-        PE(["x%d" % p, "n%d" % p, "R15", "LT"], [PK0[p], PK2[p]],
-           mm(P[:, 768:1024], z("R15"), x[p][:, 0:256], True, False), mm(P[:, 768:1024], z("LT"), n[p][:, 0:256], False, True),
-           mm(P[:, 1024:1536], z("R15"), x[p][:, 256:768], True, False), mm(P[:, 1024:1536], z("LT"), n[p][:, 256:768], False, True))
-
-    def p2(p, idx, k):
-        off, ck = lists(p, idx)
-        P, s = PX[p], k % SP
-        vk = "vv%d" % (0 if k == 0 else 1 if k < 4 else 2)
-        V([vk, PK0[p]], ["Y%d" % p], tt(Y[p][:, :], T.VV[:, k * 1536 + H * p:k * 1536 + H * p + H], P[:, 0:768], OP.mult))
-        V(["Y%d" % p, PK0[p], PK2[p]], ["k%d" % p], tt(cond[p][:, :], P[:, 768:1536], Y[p][:, :], OP.is_le))
-        V(DTK + [ck, "k%d" % p], ["X%d" % p], tt(X[p][:, :], T.DT[:, 0:2304].indirect(off), cond[p][:, :], OP.mult))
-
-        def esc_list():
-            if s == SP - 1:
-                PE(["k%d" % p, "cb%d" % CE], [PK2[p]],
-                   *[mm(P[:, 1024:1072], comb(CE, i), cond[p][:, i:H:16], i == 0, i == 15) for i in range(16)])
-            elif p == 0:
-                PE(["k0", "cb%d" % CE], [PK2[0]],
-                   *[mm(P[:, 1024:1032], comb(CE, i), cond[0][:, i:128:16], i == 0, i == 15) for i in range(16)])
-                S([PK2[0]], ["HT"], ac(z("HT", s + 2, 40, 5), P[:, 1024:1032], AF.Copy))
-
-        def marks():
-            if k == RO * SP - 1:
-                return
-            f = []
-            for a, b in ((0, 512), (512, 768)):
-                if k:
-                    f.append(mm(P[:, a:b], z("IDN"), T.MM[:, H * p + a:H * p + b], True, False))
-                f += [mm(P[:, a:b], z("NI"), w[p][:, a:b], k == 0, False), mm(P[:, a:b], z("ESC"), cond[p][:, a:b], False, True)]
-            PE(["w%d" % p, "k%d" % p, "IDN", "NI", "ESC"] + (["m%d" % p] if k else []), [PK0[p]], *f)
-            S([PK0[p]], ["m%d" % p],
-              ac(T.MM[:, H * p:H * p + H], P[:, 0:768], AF.Sigmoid, bias=8064.0 if k else 8320.0, scale=256.0))
-
-        def xlist():
-            PE(["X%d" % p, "COMBX"], [LK[p]],
-               *[mm(LP[p][:, 0:48], combx(i), X[p][:, i:H:16], False, i == 15) for i in range(16)])
-        if s < SP - 1:
-            marks()
-            xlist()
-            esc_list()
-            return None
-        esc_list()
-        xlist()
-        return marks
-
-    def v5(p, idx, rnd):
-        off, ck = lists(p, idx)
-        if rnd == 0:
-            V([LK[p]], [ck], cp(off, LP[p][:, 0:48]))
+        if k:
+            V(WTK + [ck, "m%d" % p], ["w%d" % p], tt(w[p][:, :], wi, T.MM[:, H * p:H * p + H], OP.mult))
         else:
-            t = z("CIT", 48 * p, 48 * p + 48)
-            V([LK[p]], ["cit%d" % p], cp(t, LP[p][:, 0:48]))
-            V(["cit%d" % p], ["cit%d" % p], ts(t, t, 4095, BA))
-            V(["cit%d" % p], [ck], cp(off, t))
+            op("vs"[p], WTK + [ck], ["w%d" % p], ac(w[p][:, :], wi, AF.Copy) if p else cp(w[p][:, :], wi))
+
+    def s1(p):
+        L, sp = LP[p], str(p)
+        PE(["w" + sp, "cb%d" % C1], [LK[p]],
+           *group(*[(L[:, 0:64], comb(C1, a), w[p][:, c0:c1:st]) for a, (c0, c1, st) in enumerate(ROWS)]))
+        S([LK[p]], ["a16" + sp], ac(zs("a16", p), L[:, 0:64], AF.Identity, bias=B0 + 0.48, scale=1.003))
+        S(["a16" + sp], ["a1" + sp], ac(zs("a1", p), zs("a16", p), AF.Identity, bias=-1.0625 * B0, scale=1.0625))
+        PE(["w" + sp, "NLT"], [PK[p]], *[mm(o, l, r, True, False) for o, l, r in halves(PX[p], z("NLT"), w[p])])
+        PE(["a16" + sp, "RT" + sp, "ID16", "TU"], [LK[p]], *group(
+            (L[:, 64:128], z("ID16"), zs("a16", p)),
+            *[(L[:, 64 + r:128:st], turn(*BACK[j]), z("RT", 48 * p + c0, 48 * p + c1)) for j, (_, _, (r, st), (c0, c1)) in enumerate(TURN)]))
+
+    def s2(p, idx, k):
+        L, sp, s = LP[p], str(p), k % SP
+        v = T.VL[:, 128 * k + 64 * p:128 * k + 64 * p + 64]
+        V([LK[p], "a1" + sp], ["tq" + sp], tt(L[:, 0:64], zs("a1", p), L[:, 0:64], OP.subtract))
+        V([LK[p], "tq" + sp, "VL%d" % (k // SP)], ["y" + sp], tt(zs("y", p), L[:, 0:64], v, OP.mult))
+        V(["y" + sp], ["UU" + sp], ts(zs("UU", p), zs("y", p), B0 - 255.0 / 512, OP.add))
+        V([LK[p], "UU" + sp], ["eb" + sp], tt(zs("eb", p), zs("UU", p), L[:, 64:128], OP.is_lt))
+
+        def xo():
+            PE(["eb" + sp, "C16" + sp, "ID16", "TU"], [LK[p]], *group(
+                (L[:, 128:176], z("ID16"), zs("C16", p, 48)),
+                *[(L[:, 128 + c0:128 + c1], turn(m, sh), zs("eb", p, 64, r, st)) for m, sh, (r, st), (c0, c1) in TURN]))
+
+        def flags():
+            if s == SP - 1:
+                S([LK[p], "EB"], ["EB" + sp], ac(z("EB", 16 + 48 * p, 64 + 48 * p), L[:, 128:176], AF.Sigmoid, bias=-256 * 1151.5, scale=256.0))
+            if p == 0:
+                S([LK[0], "HT"], ["E8" if s == SP - 1 else "HT"], ac(z("E8") if s == SP - 1 else z("HT", s + 2, 40, 5), L[:, 128:136],
+                                                                     AF.Sigmoid, bias=256 * 1151.5, scale=-256.0))
+                S(["C160", "DL"], ["DL"], ac(z("DL", s + 1, 40, 5), z("C16", 0, 8), AF.Identity, bias=1024.0))
+        first = s == SP - 1 and p == 1
+        if first:
+            xo()
+            flags()
+        PE(["UU" + sp, "BC"], [PK[p]], *spread(PX[p], "UU", p, True))
+        if not first:
+            xo()
+
+        def compare():
+            S([PK[p], "KB"], ["k" + sp], ac(cond[p][:, :], PX[p][:, 0:H], AF.Sigmoid, bias=z("KB"), scale=-4096.0))
+            if not first:
+                flags()
+        return compare
+
+    def marks_sum(p, k):
+        if k < RO * SP - 1:
+            PE(["w%d" % p, "N16", "eb%d" % p, "BC"], ["#M"], *([mm(o, l, r, True, False) for o, l, r in halves(PM, z("N16"), w[p])]
+                                                               + spread(PM, "eb", p, True)))
+
+    def marks(p, k):
+        if k < RO * SP - 1:
+            S(["#M"], ["m%d" % p], ac(T.MM[:, H * p:H * p + H], PM[:, 0:H], AF.Sigmoid, bias=-128.0, scale=2.0 ** 32))
+
+    def shown(p, rnd):
+        off, ck = lists(p, 5 * rnd + SP - 1)
+        S(AFK + [ck], ["A2%d" % p], ac(T.A2[:, H * p:H * p + H], T.AUF[:, 0:2048 + 128 * rnd].indirect(off), AF.Copy))
+
+    def s3a(p):
+        V([LK[p]], ["XL%d" % p], ts(zs("XL", p, 48), LP[p][:, 128:176], 1024.0, OP.add))
+
+    def s3(p, rnd):
+        sp = str(p)
+        V(DTK + ["XL" + sp, "k" + sp], ["X" + sp], tt(X[p][:, :], T.DT[:, 0:OD + 2048 + 128 * rnd].indirect(zs("XL", p, 48)), cond[p][:, :], OP.mult))
+        PE(["X" + sp, "COMBX"], [LK[p]], *group(*[(LP[p][:, 192:240], T.COMBX[:, 15 - i:143 - i], X[p][:, i:H:16]) for i in range(16)]))
+
+    def s4(p, idx, rnd):
+        off, ck = lists(p, idx)
+        P, sp, last = LP[p][:, 192:240], str(p), idx % 5 == SP
+        if rnd == 0:
+            if p == 0 or not last:
+                V([LK[p]], [ck], ts(off, P, 1024.0, OP.add))
+            S([LK[p]], ["C16" + sp], ac(zs("C16", p, 48), P, AF.Copy))
+        else:
+            V([LK[p]], ["rr" + sp], ts(zs("rr", p, 48), P, M35, OP.add, -M35, OP.add))
+            V([LK[p], "rr" + sp], ["C16" + sp], tt(zs("C16", p, 48), P, zs("rr", p, 48), OP.subtract))
+            if p == 0 or not last:
+                V(["C16" + sp], [ck], ts(off, zs("C16", p, 48), 1024.0, OP.add))
+        if last:
+            S(["C16" + sp], ["CLF" + sp], ac(zs("CLF", p, 48), zs("C16", p, 48), AF.Identity, bias=1024.0))
+        else:
+            root(p)
 
     nxt = T.cores[(rank + 1) % len(T.cores)]
     rid, pid = topo.addr(nxt, core)
     rmask, ne = topo.mask(core, nxt), len(topo.engines(core, nxt))
+    suffix_copy = lambda: V(["#LB"], ["FL"], cp(z("FL"), LB[:, 256:384]))
+    fill = {0: [lambda: pointers(2), early_c, lambda: pointers(3), late_0], 1: [late_b], 2: [suffix_copy, late_b2], 3: [late_c],
+            4: [late_d], 5: [late_e]}
+    fill_t = {0: lambda: (differences(2), differences(3), late_a()), 1: lambda: (suffix_list(0), suffix_list(1))}
 
     for rnd in range(RO):
-        base = 5 * rnd
-        for s in range(SP):
+        base, i4 = 5 * rnd, 5 * rnd + SP
+        DUM = "DUM%d" % rnd
+        for n in range(2 * SP):
+            p, s = n % 2, n // 2
             k, idx = rnd * SP + s, base + s
-            for p in (0, 1):
-                if s:
-                    v5(p, idx, rnd)
-                p1(p, idx, k)
-                drain(7 if k and p else 0)
-            if k == 0:
-                late_a()
-            V(["c%d_0" % idx], ["DL"], cp(z("DL", s + 1, 40, 5), T.CL[:, idx * 96:idx * 96 + 8]))
-            for p in (0, 1):
-                mk = p2(p, idx, k)
-                if mk and p == 0:
-                    mk()
-                drain(4 if p == 0 else 0)
-            if k == SP:
-                zeros()
-        drain(len(todo))
-        i4 = base + SP
-        LA, LB = T.LAp, T.LBp
+            if k == 0 and n == 0:
+                s0(0, idx, k)
+                s0(1, idx, k)
+                early_b()
+            elif k:
+                s0(p, idx, k)
+            s1(p)
+            if n:
+                marks(1 - p, rnd * SP + (n - 1) // 2)
+                s3a(1 - p)
+                s3(1 - p, rnd)
+            if s == SP - 1:
+                shown(p, rnd)
+            elif n:
+                drain(1 if n < 3 else 2)
+            if n == 0:
+                for f in fill.pop(8 * rnd + n, []):
+                    f()
+            compare = s2(p, idx, k)
+            for f in fill.pop(8 * rnd + n, []):
+                f()
+            if n:
+                s4(1 - p, base + (n + 1) // 2, rnd)
+            if n == 0:
+                fill_t.pop(8 * rnd + n, lambda: None)()
+            compare()
+            if n < 2 * SP - 1:
+                marks_sum(p, k)
+            fill_t.pop(8 * rnd + n, lambda: None)()
+            drain(1 if n < 5 else len(todo) if n == 5 else 0)
         nl = T.CL[:, i4 * 96:i4 * 96 + 8]
         nk = "c%d_0" % i4
-        V([PK2[0]], ["E16a"], cp(z("E16", 0, 48), T.PA[:, 1024:1072]))
-        v5(0, i4, rnd)
-        V([PK2[1]], ["E16b"], cp(z("E16", 48, 96), T.PB[:, 1024:1072]))
-        v5(1, i4, rnd)
-        PE(["E16a", "E16b", "LTB", "NI2K", "BM"], ["#LA"], mm(LA[:, 128:224], z("LTB"), z("E16"), True, False),
-           mm(LA[:, 128:224], z("NI2K"), z("E16"), False, True), mm(LA[:, 256:352], z("BM"), z("E16"), True, True))
-        off, ck = lists(0, i4)
-        S(AUXK + [ck], ["A20"], ac(T.A2[:, 0:H], T.AUX[:, 0:2304].indirect(off), AF.Copy))
-        mk()
-        off, ck = lists(1, i4)
-        S(AUXK + [ck], ["A21"], ac(T.A2[:, H:1536], T.AUX[:, 0:2304].indirect(off), AF.Copy))
-        DUM = "DUM%d" % rnd
+        V(["EB0", "EB1", "JQ", "QB"], ["QB1"], tt(z("QB", 16, 112), z("EB", 16, 112), z("JQ"), OP.mult))
+        PE(["EB0", "EB1", "EB", "QB", "QB1", "NLT", "NUT", "ID16", "NI16"], ["#LA"], *group(
+            (LA[:, 256:352], z("NLT"), z("EB", 16, 112)), (LA[:, 256:352], z("NUT"), z("EB", 15, 111)),
+            (LA[:, 256:352], z("ID16"), z("QB", 16, 112)), (LA[:, 256:352], z("NI16"), z("QB", 15, 111))))
+        marks_sum(1, rnd * SP + SP - 1)
+        s3a(1)
         t2("hd", "HT", "DL", OP.mult)
-        V(["HT", "E16a"], ["CAND"], tt(z("CAND", 0, 8), z("HT", 4, 40, 5), z("E16", 0, 8), OP.is_gt),
-          tt(z("CAND", 8, 16), z("HT", 4, 40, 5), z("E16", 0, 8), OP.is_gt))
+        V(["HT", "EB0"], ["CAND"], tt(z("CAND", 0, 8), z("HT", 4, 40, 5), z("EB", 16, 24), OP.mult),
+          tt(z("CAND", 8, 16), z("HT", 4, 40, 5), z("EB", 16, 24), OP.mult))
         t2("d1", "DL", "hd", OP.subtract)
-        V(["#LA", "Z96", "CS"], ["CS1"],
-          lambda e: e.tensor_tensor_scan(z("CS", 1, 97), LA[:, 256:352], z("Z96"), 0.0, OP.add, OP.add))
-        V(["#LA", "CS", "CS1"], ["CNT"], tt(z("CNT"), LA[:, 128:224], z("CS", 0, 96), OP.add))
-        tz("OKT", "CNT", -1663.5, OP.is_le)
-        t2("TT", "CNT", "J2", OP.subtract)
-        t2("TT2", "TT", "OKT", OP.mult)
-        t2("POSF", "TT2", "J3", OP.add)
+        V(["#LA", "D1"], ["POSF"],
+          lambda e: e.tensor_tensor_scan(z("POSF"), LA[:, 256:352], z("D1"), 0.0, OP.add, OP.add))
+        V(["HT", "d1"], ["FS"], lambda e: e.tensor_tensor_scan(z("FS"), z("HT"), z("d1"), 0.0, OP.mult, OP.add))
         V(["POSF"], ["POS"], cp(z("POS"), z("POSF")))
         S(["LBB", "POS", "SW"], ["SW"], ac(T.SW[:, :].indirect(z("POS", 48, 96)), T.LBB[:, :], AF.Sigmoid))
-        V(LBK + ["POS", "VW"], ["VW"], cp(T.VW[:, :].indirect(z("POS", 0, 48)), T.LBA[:, :]))
-        PE(["VW", "cb%d" % CSA], ["#LA"],
-           *[mm(LA[:, 384:408], comb(CSA, i), T.VW[:, i:384:16], i == 0, False) for i in range(16)])
-        S(["SW"], ["SWb"], ac(z("SWb"), T.SW[:, 0:384], AF.Copy))
-        PE(["SWb", "cb%d" % CSB], ["#LA"],
-           *[mm(LA[:, 384:408], comb(CSB, i), z("SWb", i, 384, 16), False, i == 15) for i in range(16)])
-        V(["HT", "d1"], ["FS"], lambda e: e.tensor_tensor_scan(z("FS"), z("HT"), z("d1"), 0.0, OP.mult, OP.add))
         V(["FS", "DL", DUM], ["KT"], tt(z("KT", 0, 8), z("FS", 3, 40, 5), z(DUM, 0, 8), OP.subtract),
           tt(z("KT", 8, 16), z("DL", 4, 40, 5), z(DUM, 0, 8), OP.subtract))
         t2("KT2", "KT", "CAND", OP.mult)
         t2("KK", "KT2", DUM, OP.add)
         V(["KK"], ["FK"], cp(z("FK"), z("KK")))
-        S(AUXK + ["FK"], ["XF"], ac(z("XF"), T.AUX[:, :].indirect(z("FK")), AF.Copy))
-        SND, RCV = T["SND%d" % rnd], T["RCV%d" % rnd]
-        sk, rk = "SND%d" % rnd, "RCV%d" % rnd
-        V(["#LA"], ["LNE"], ts(z("LNE"), LA[:, 384:408], -2048.0, OP.add, 0.0, OP.max))
-        V(["#LA"], ["T1"], ts(z("T1"), LA[:, 384:408], 2047.5, OP.is_ge))
-        V(["#LA"], [sk + "b"], ts(SND[:, 384:408], LA[:, 384:408], 2047.5, OP.is_ge))
-        S(["A20", "A21", "LNE"], [sk + "a"], ac(SND[:, 0:384], T.A2[:, :].indirect(z("LNE")), AF.Copy))
-        width = 408
-        if rnd == 0:
-            V(["m0", "m1", "LNE"], [sk + "c"], cp(SND[:, 408:792], T.MM[:, 0:1536].indirect(z("LNE"))))
-            width = 792
-        do_waits("q", [sk + c for c in "abc"[:2 if rnd else 3]], [])
-        g.remote_dma(RCV[:, 0:width], SND[:, 0:width], T.sem["arr%d" % rnd], T.sem["snt%d" % rnd], pid, rid, rmask)
-        used["snt%d" % rnd] = ne
-        used["arr%d" % rnd] = ne
-        record(("rem%d" % rnd, "arr%d" % rnd, ne, {}), [], [rk])
-        V(["#LA", "JD2"], ["LNF"], tt(z("LNF"), LA[:, 384:408], z("JD2"), OP.subtract))
-        S(WTK + [nk], ["ug"], ac(z("ug"), T.WT[:, 0:2304].indirect(nl), AF.Copy))
-        t2("PRE", "LNF", "T1", OP.mult)
-
+        V(AUXK + ["FK"], ["XF"], cp(z("XF"), T.AUX[:, :].indirect(z("FK"))))
+        V(LBK + ["POS", "VW"], ["VW"], cp(T.VW[:, :].indirect(z("POS", 0, 48)), T.LBA[:, 0:H]))
+        oh = LB[:, 256:384]
+        PE(["k0", "BID"], ["#LB"], mm(oh, z("BID"), cond[0][:, 0:128], True, True))
         for h in (0, 1):
             f = []
             xf = z("XF", 128 * h, 128 * h + 128)
             for gg in range(8):
                 o = PX[h][:, 128 * gg:128 * gg + 128]
-                f += [mm(o, T.SELK[:, 128 * gg:128 * gg + 128], xf, True, False),
-                      mm(o, xf, T.NSELK[:, 128 * gg:128 * gg + 128], False, False), mm(o, z("IDN"), z("TRI"), False, True)]
-            PE(["XF", "IDN", "TRI"] + [c + "SELK%d" % i for i in range(8) for c in ("", "N")], [PK0[h]], *f)
-        V(["#A0"], ["EQF"], ts(T.EQF[:, :], T.PA[:, 0:1024], 0.0, OP.is_equal))
-        S(["#B0"], ["ABD"], ac(T.ABD[:, :], T.PB[:, 0:1024], AF.Abs))
+                f += group((o, T.SELK[:, 128 * gg:128 * gg + 128], xf), (o, xf, T.NSELK[:, 128 * gg:128 * gg + 128]), (o, z("IDN"), z("TRI")))
+            PE(["XF", "IDN", "TRI", "SELK", "NSELK"], [PK[h]], *f)
+        S(["SW"], ["SWb"], ac(z("SWb"), T.SW[:, 0:384], AF.Copy))
+        sl = LA[:, 352:376]
+        PE(["VW", "SWb", "cb%d" % CSA, "cb%d" % CSB], ["#LA"], *group(
+            *(combed(sl, CSA, lambda i, n, st: T.VW[:, i:n:st], 384) + combed(sl, CSB, lambda i, n, st: z("SWb", i, n, st), 384))))
+        marks(1, rnd * SP + SP - 1)
+        s3(1, rnd)
+        SND, RCV = T["SND%d" % rnd], T["RCV%d" % rnd]
+        sk, rk = "SND%d" % rnd, "RCV%d" % rnd
+        V(["#LA"], ["LNE"], ts(z("LNE"), sl, 1536.0, OP.add))
+        S(["A20", "A21", "A2z", "LNE"], [sk + "a"], ac(SND[:, 0:384], T.A2[:, :].indirect(z("LNE")), AF.Copy))
+        if rnd == 0:
+            V(["#LA", sk + "z"], [sk + "b"], ts(SND[:, 400:424], sl, -0.5, OP.is_lt))
+            V(["m0", "m1", "mz", "LNE"], [sk + "c"], cp(SND[:, 432:816], T.MM[:, 0:1552].indirect(z("LNE"))))
+        do_waits("q", [sk + c for c in "azbc"[:2 if rnd else 4]], [])
+        g.remote_dma(RCV[:, :], SND[:, :], T.sem["arr%d" % rnd], T.sem["snt%d" % rnd], pid, rid, rmask)
+        used["snt%d" % rnd] = ne
+        used["arr%d" % rnd] = ne
+        record(("rem%d" % rnd, "arr%d" % rnd, ne, {}), [], [rk])
+        V(["#A"], ["EQF"], ts(T.EQF[:, :], T.PA[:, :], 0.0, OP.is_equal))
+        S(["#B"], ["ABD"], ac(T.ABD[:, :], T.PB[:, :], AF.Abs))
         S(["ABD"], ["EQD"], ac(T.EQD[:, :], T.ABD[:, :], AF.Relu, bias=1.0, scale=-1.0))
-        oh = LB[:, 256:384]
-        PE(["k0", "BID", "E0", "ONES"], ["#LB"], mm(oh, z("BID"), cond[0][:, 0:128], True, False), mm(oh, z("E0"), z("ONES"), False, True))
+        s4(1, i4, rnd)
+        S(WTK + [nk], ["ug"], ac(z("ug"), T.WT[:, 0:2304].indirect(nl), AF.Identity, bias=128.3, scale=0.5))
 
         def dup(h, EQ, ek):
-            o = PX[h][:, 1024:1152]
-            PE([ek, "OB", "XF", "CANDM"], [PK2[h]],
-               *([mm(o, z("OB", 112 - 16 * gg, 240 - 16 * gg), EQ[:, 128 * gg:128 * gg + 128], gg == 0, False) for gg in range(8)]
-                 + [mm(o, z("CANDM"), z("XF", 128 * h, 128 * h + 128), False, True)]))
+            o = LP[h][:, 384:512]
+            PE([ek, "OB", "XF", "CANDM"], [LK[h]], *group(
+                *([(o, z("OB", 112 - 16 * gg, 240 - 16 * gg), EQ[:, 128 * gg:128 * gg + 128]) for gg in range(8)]
+                  + [(o, z("CANDM"), z("XF", 128 * h, 128 * h + 128))])))
 
         def winners(h):
-            P = PX[h]
-            V([PK2[h]], ["AR%d" % h], ts(z("AR", 128 * h, 128 * h + 128), P[:, 1024:1152], -0.5, OP.is_lt))
-            PE(["AR%d" % h, "cb%d" % C0], [PK2[h]],
-               *[mm(P[:, 1280:1288], comb(C0, i), z("AR", 128 * h + i, 128 * h + 128, 16), i == 0, i == 15) for i in range(16)])
+            V([LK[h]], ["AR%d" % h], ts(z("AR", 128 * h, 128 * h + 128), LP[h][:, 384:512], -0.5, OP.is_lt))
+            PE(["AR%d" % h, "cb%d" % C0], [LK[h]],
+               *group(*combed(LP[h][:, 240:248], C0, lambda i, n, st: z("AR", 128 * h + i, 128 * h + n, st), 128)))
 
         def offsets(h, o1, o2, off):
-            V([PK2[h], "KT2"], [o1], tt(z(o1), PX[h][:, 1280:1288], z("KT2", 8 * h, 8 * h + 8), OP.mult))
+            V([LK[h], "KT2"], [o1], tt(z(o1), LP[h][:, 240:248], z("KT2", 8 * h, 8 * h + 8), OP.mult))
             V([o1, DUM], [o2], tt(z(o2), z(o1), z(DUM, 0, 8), OP.add))
             V([o2], [off], cp(z(off), z(o2)))
         dup(0, T.EQF, "EQF")
+        tz("POG", "POSF", 384.0, OP.min)
+        if rnd == 0:
+            V(["#LA"], ["T1"], ts(z("T1"), sl, -0.5, OP.is_lt))
+            V(["#LA", "JL"], ["LNF"], tt(z("LNF"), sl, z("JL", 0, 24), OP.subtract))
         winners(0)
         V(["#LB", "AR0"], ["OA"], tt(z("OA"), oh, z("AR", 0, 128), OP.mult))
         S(["OA"], ["nOA"], ac(z("nOA"), z("OA"), AF.Identity, bias=1.0, scale=-1.0))
-        scaled("OA2", "OA", 2.0, "OA")
+        scaled("OA2", "OA", 15.0 / 16, "OA")
+        if rnd == 0:
+            t2("PRE", "LNF", "T1", OP.mult)
+            tz("u2", "ug", -128.0625, OP.add, -TINY, OP.max)
+        else:
+            tz("u2", "ug", -128.0, OP.add)
+        wc = 2048 + 128 * rnd
+        V(["u2", "AR0"], ["WTn"], tt(T.WT[:, wc:wc + 128], z("u2"), z("AR", 0, 128), OP.mult))
         offsets(0, "AO", "AO2", "OFF")
         dup(1, T.EQD, "EQD")
-        wc = 2048 + 128 * rnd
-        tz("i_u", "ug", 0.53, OP.mult, 0.45, OP.add)
         V(WTK + ["OFF", "nOA"], ["tg"], tt(z("tg"), T.WT[:, :].indirect(z("OFF")), z("nOA"), OP.mult))
         winners(1)
         if rnd == 0:
-            V(STK + ["OFF", "nOA"], ["tS"], tt(z("tS"), T.ST[:, :].indirect(z("OFF")), z("nOA"), OP.mult))
-            t2("qS", "OA", "WR", OP.mult)
-            V(STK + [nk], ["Sc"], cp(z("Sc"), T.ST[:, 0:2304].indirect(nl)))
-            S(AUXK + [nk], ["XC"], ac(z("XC"), T.AUX[:, 0:2304].indirect(nl), AF.Copy))
-            o = T.PA[:, 1408:1536]
-            PE(["SH16", "tS", "qS", "XF", "cb%d" % CF], ["#A2"], mm(o, z("SH16"), z("tS"), True, False),
-               mm(o, z("SH16"), z("qS"), False, False), mm(o, comb(CF, 15), z("XF", 0, 128), False, True))
-            PE(["OA", "cb%d" % C0], ["#A0"], mm(T.PA[:, 0:128], comb(C0, 0), z("OA"), True, False),
-               mm(T.PA[:, 0:128], comb(C0, 1), z("OA"), False, True))
-            o = T.PB[:, 0:128]
-            PE(AUXK + ["XF", "N01", "cb%d" % C7, "cb%d" % C8], ["#B0"], mm(o, comb(C7, 0), T.AUX[:, 2048:2176], True, False),
-               mm(o, comb(C8, 1), T.AUX[:, 2048:2176], False, False), mm(o, z("N01"), z("XF", 0, 128), False, True))
-            o = T.PB[:, 1408:1536]
-            PE(["SH16", "Sc", "XC", "cb%d" % CID], ["#B2"], mm(o, z("SH16"), z("Sc"), True, False),
-               mm(o, comb(CID, 15), z("XC"), False, True))
-            S(["#A2"], ["xs"], ac(z("xs"), T.PA[:, 1408:1536], AF.Copy))
-            S(["#A0"], ["FLs"], ac(z("FLs"), T.PA[:, 0:128], AF.Copy))
-            S(["#B2"], DTK, ac(T.DT[:, 2048:2176], o, AF.Copy))
-            scaled("xt", "XC", *late["keep"])
+            S(AUXK + [nk], ["AFn"], ac(T.AUF[:, 2048:OD], T.AUX[:, 0:2048].indirect(nl), AF.Copy))
+            S(DTK + [nk], ["DTn"], ac(T.DT[:, OD + 2048:OD + OD], T.DT[:, OD:OD + 2048].indirect(nl), AF.Copy))
+            PE(["AFn", "cb%d" % CID], ["#B"], mm(T.PB[:, 0:128], comb(CID, 15), T.AUF[:, 2048:OD], True, True))
+            S(["#B", "X1"], ["DFn"], ac(T.DT[:, 2048:OD], T.PB[:, 0:128], AF.Copy))
+            for j in range(4):
+                plain_pointers(j)
+            targets(1)
         V(["tg", "OA2", "OFF"], WTK, tt(T.WT[:, :].indirect(z("OFF")), z("tg"), z("OA2"), OP.add))
         V(["#LB", "AR1"], ["OBm"], tt(z("OBm"), oh, z("AR", 128, 256), OP.mult))
-        PE(["OBm", "ID2"], ["#LA"], mm(LA[:, 256:384], z("ID2"), z("OBm"), True, True))
         offsets(1, "BO", "BO2", "OFD")
-        if rnd == 0:
-            tz("i_k", "xs", 1.0 / 4096, OP.mult)
-            V(["FLs", "#B0"], ["fd"], tt(z("fd"), z("FLs"), T.PB[:, 0:128], OP.mult))
-            tz("kk", "i_k", -4096.0, OP.mult)
         V(WTK + ["OFD", "OBm"], ["s1"], tt(z("s1"), T.WT[:, :].indirect(z("OFD")), z("OBm"), OP.add))
         if rnd == 0:
-            V(["XF", "fd", "OFF"], AUXK, tt(T.AUX[:, :].indirect(z("OFF")), z("XF", 0, 128), z("fd"), OP.add))
-        V(["s1", "#LA"], ["s2"], tt(z("s2"), z("s1"), LA[:, 256:384], OP.max))
-        if rnd == 0:
-            V(["kk", "xs", "OFF"], DTK, tt(T.DT[:, :].indirect(z("OFF")), z("kk"), z("xs"), OP.add))
-        tz("s3", "s2", 16.0, OP.min)
-        if rnd == 0:
-            V(["xt"] + AUXK, AUXK, tt(T.AUX[:, 2048:2176], z("xt"), T.AUX[:, 2048:2176], OP.add))
+            tz("s2", "s1", 15.0, OP.min, 128.0, OP.add)
+            tz("s3", "s2", -128.0625, OP.add, -TINY, OP.max)
+        else:
+            tz("s3", "s1", 15.0, OP.min)
         V(["s3", "OFD"], WTK, cp(T.WT[:, :].indirect(z("OFD")), z("s3")))
-        V(["i_u", "AR0"], WTK, tt(T.WT[:, wc:wc + 128], z("i_u"), z("AR", 0, 128), OP.mult))
-        V([nk, "c%d_1" % i4], ["CLF"], cp(z("CLF"), T.CL[:, i4 * 96:i4 * 96 + 96]))
+
+        def new_pointers():
+            V(STK + ["OFF", "nOA"], ["tS"], tt(z("tS"), T.ST[:, :].indirect(z("OFF")), z("nOA"), OP.mult))
+            t2("qS", "OA", "WR", OP.mult)
+            o = T.PB[:, 0:128]
+            PE(["SH16", "tS", "qS"], ["#B"], *group((o, z("SH16"), z("tS")), (o, z("SH16"), z("qS"))))
+            S(["#B"], ["xs"], ac(z("xs"), o, AF.Copy))
+            tz("kk", "xs", M35, OP.add, -M35, OP.add)
+            V(["kk", "xs", "OFF"], DTK, tt(T.DT[:, OD:OD + NW].indirect(z("OFF")), z("xs"), z("kk"), OP.subtract))
 
         def counts_out(a, b, q):
-            V(WTK, ["yn%d" % a], ts(T.YN[:, a:b], T.WT[:, a:b], -1.0, OP.add, 0.0, OP.max))
+            V(WTK, ["yn%d" % a], ts(T.YN[:, a:b], T.WT[:, a:b], M23, OP.add, -M23, OP.add))
             dma(q, ["yn%d" % a], [], (T.yn[:, a:b], T.YN[:, a:b]))
-        if rnd == RO - 1:
-            counts_out(0, 1152, "s")
-        V([rk, "PRE"], ["RX1"], tt(z("RX1"), RCV[:, 384:408], z("PRE"), OP.mult))
-        t2("RX2", "RX1", "JD", OP.add)
-        V(["RX2"], ["TO"], cp(z("TO"), z("RX2")))
-        V([rk, "TO", "LW"], ["LW"], cp(T.LW[:, :].indirect(z("TO")), RCV[:, 0:384]))
-        PE(["LW", "cb%d" % CLK], ["#LB"], *[mm(LB[:, 128:224], comb(CLK, i), T.LW[:, i:1536:16], i == 0, i == 15) for i in range(16)])
+
+        def landed(p, e):
+            o, i = T.LW[:, H * p:H * p + H], RCV[:, 0:400].indirect(zs("POG", p, 48))
+            op(e, [rk, "POG"], ["LW%d" % p], ac(o, i, AF.Copy) if e == "s" else cp(o, i))
+
+        def merged(P, pk, a, b, out, ok):
+            V([pk, "CLF0", "CLF1"], ["mx%d" % a], tt(z("mx", a, b), P, z("CLF", a, b), OP.max))
+            V(["mx%d" % a], ["rr%d" % (a // 48)], ts(z("rr", a, b), z("mx", a, b), 4096.0, OP.is_ge, 4096.0, OP.mult))
+            V(["mx%d" % a, "rr%d" % (a // 48)], [ok], tt(out, z("mx", a, b), z("rr", a, b), OP.subtract))
         if rnd == 0:
-            V([rk, "TO", "m0", "m1"], ["m0", "m1"], cp(T.MM[:, :].indirect(z("TO")), RCV[:, 408:792]))
+            new_pointers()
+            zeros()
+            landed(0, "s")
+            landed(1, "s")
+            V([rk, "PRE"], ["RX1"], tt(z("RX1"), RCV[:, 400:424], z("PRE"), OP.mult))
+            t2("RX2", "RX1", "JD", OP.add)
+            V(["RX2"], ["TO"], cp(z("TO"), z("RX2")))
+            V([rk, "TO", "m0", "m1", "mz"], ["m0", "m1", "mz"], cp(T.MM[:, :].indirect(z("TO")), RCV[:, 432:816]))
+            for p in (0, 1):
+                P = LP[p][:, 192:240]
+                PE(["LW%d" % p, "cb%d" % CLK], [LK[p]], *group(*combed(P, CLK, lambda i, n, st: T.LW[:, H * p + i:H * p + n:st], H)))
+
+            def hopped(p):
+                off, ck = lists(p, SP + 1)
+                merged(LP[p][:, 192:240], LK[p], 48 * p, 48 * p + 48, zs("cc", p, 48), "cc%d" % p)
+                V(["cc%d" % p], [ck], cp(off, zs("cc", p, 48)))
+                S(["cc%d" % p], ["C16%d" % p], ac(zs("C16", p, 48), zs("cc", p, 48), AF.Identity, bias=-1024.0))
+                root(p)
+
+            def carried():
+                hopped(1)
+                V(["FS"], ["DL"], cp(z("DL", 0, 40, 5), z("FS", 4, 40, 5)))
+                V(["HF", "E8"], ["HT"], tt(z("HT", 1, 40, 5), z("E8"), z("HF"), OP.subtract))
+            hopped(0)
+            S(["#LA"], ["HF"], ac(z("HF"), LA[:, 192:200], AF.Sigmoid, bias=-2048.0))
+            fill[8] = [carried]
         else:
-            counts_out(1152, 2304, "s")
-        V(["#LB", "CLF"], ["cit0", "cit1"], tt(z("CIT"), LB[:, 128:224], z("CLF"), OP.max))
-        V(["cit0", "cit1"], ["cit0", "cit1"], ts(z("CIT"), z("CIT"), 4095, BA))
-        if rnd < RO - 1:
-            V(["cit0", "cit1"], ["c%d_0" % (i4 + 1), "c%d_1" % (i4 + 1)], cp(T.CL[:, (i4 + 1) * 96:(i4 + 2) * 96], z("CIT")))
-            V(["#LB"], ["HF"], ts(z("HF"), LB[:, 128:136], 4095.5, OP.is_ge))
-            V(["FS"], ["DL"], cp(z("DL", 0, 40, 5), z("FS", 4, 40, 5)))
-            V(["HF", "E16a"], ["HT"], tt(z("HT", 1, 40, 5), z("E16", 0, 8), z("HF"), OP.subtract))
-        else:
-            V(["cit0", "cit1"], ["YC"], cp(z("YC"), z("CIT")))
+            counts_out(0, 1152, "s")
+            counts_out(1152, 2304, "y")
+            landed(0, "v")
+            landed(1, "s")
+            PE(["LW0", "LW1", "cb%d" % CLK], ["#LB"], *group(*combed(LB[:, 0:96], CLK, lambda i, n, st: T.LW[:, i:n:st], 1536)))
+            merged(LB[:, 0:96], "#LB", 0, 96, z("YC"), "YC")
             dma("y", ["YC"], [], (T.yc[:, :], z("YC")))
 
     for q in ("v", "s", "t", "q"):

@@ -6,6 +6,7 @@ RO, SP = 2, 4
 NW = 2560
 OD = 2176
 H = 768
+VS = 896
 B0 = 1280.0
 TINY = 2.0 ** -20
 M23, M35 = 1.5 * 2 ** 23, 1.5 * 2 ** 35
@@ -14,6 +15,8 @@ ROWS = [(a, 512, 8) for a in range(8)] + [(512 + a, H, 4) for a in range(4)]
 TURN = [("lo", 8 * r, (r, 2), (0, 32)) for r in range(2)] + [("q2", 4 * r - 8, (r, 4), (32, 48)) for r in range(4)]
 BACK = [("lo", 0), ("hi", -8), ("q0", 8), ("q1", 4), ("q2", 0), ("q3", -4)]
 MASKS = {"lo": (0, 8), "hi": (8, 16), "q0": (0, 4), "q1": (4, 8), "q2": (8, 12), "q3": (12, 16)}
+C1, C0, CID, CLK, CSA, CSB = range(6)
+WEIGHTS = {CID: {4: -1024 - 4128, 7: 32, 8: 1}, CLK: {2: 32, 3: 1, 4: -32}, CSA: {15: -1536}, CSB: {15: VS - 1536}}
 SCRATCH = {}
 WHERE = {}
 
@@ -32,28 +35,26 @@ def pool(buf, dtype, **kw):
 
 
 sb(I32, tabI=2048, CI=2048, CPI=416, CPL=288, BI=640)
-sb(F32, YB=2048, ST=NW, DT=OD + NW, LBB=H, SW=4608)
-sb(B16, WT=NW, AUX=NW, AUF=OD, VV=12288, VL=1024, w0=H, w1=H, k0=H, k1=H, MM=1920, YN=2304, BB=640, LBA=1024,
-   VW=4608, A2=1552, SND0=816, SND1=400, RCV0=816, RCV1=400, LW=1536, SELK=1024, NSELK=1024, EQF=1024, EQD=1024, ABD=1024,
+sb(F32, YB=2048, ST=NW, DT=OD + NW, LBB=1536 - VS, SW=4352)
+sb(B16, WT=NW, AUX=NW, AUF=OD, VV=12288, VL=1024, w0=H, w1=H, k0=H, k1=H, MM=1920, YN=NW, BB=640, LBA=1024,
+   VW=4864, A2=1552, SND0=816, SND1=400, RCV0=816, RCV1=400, LW=1536, SELK=1024, NSELK=1024, TRW=1024, EQ0=1024, EQ1=1024,
    COMB=864)
 sb(F16, X0=H, X1=H, COMBX=144, SH=2048, BC=1536, FB=2048, TU=960)
 sb(U16, CL=960)
-pool("zi", I32, CXI=96, i_rm=16, i_pc=16, i_g8=8, i_bm=128, i_dp=160, i_sf=144, i_wr=128, i_jc=64)
-pool("zf", F32, RM=16, PC=1, G8=8, JI=96, JL=96, JQ=96, JD=24, DUM0=16, DUM1=16, CLF=96, YC=96, HT=40, FC=128,
-     DL=40, hd=40, d1=40, FS=40, KT=16, KT2=16, KK=16, CAND=16, D1=96, POSF=96, PRE=24, E8=8, MK=8, KB=1,
-     LNF=24, T1=24, RX1=24, RX2=24, AO=8, AO2=8, BO=8, BO2=8, HF=8, xs=128, kk=128, COLS=64, ZF=384,
-     a1=128, y=128, mx=96, rr=96, cc=96)
+pool("zi", I32, CXI=96, i_rm=16, i_pc=16, i_g8=8, i_bm=128, i_dp=160, i_sf=144, i_wr=128, i_jc=64, mx=96, cc=96)
+pool("zf", F32, RM=16, PC=1, G8=8, JI=96, JL=96, JQ=96, DUM0=16, DUM1=16, CLF=96, YC=96, HT=40, FC=128,
+     DL=40, hd=40, d1=40, FS=40, KK=16, CAND=8, ND=8, N2=8, D1=96, POSF=96, PJ=48, TF=48, E8=8, MK=8, KB=1, CB=1,
+     LNF=24, T1=24, HF=8, xs=128, kk=128, ZF=384, rr=96, xb=48, qa=48, W16=64, WM=64, WC=4, TWO=16, Z16=16)
 pool("zb", B16, BM=128, IDN=128, NLT=128, NUT=128, N16=128, TRI=128, CANDM=128, BID=128, U1=128, U2=128, LTu=128, LTB=128,
-     SELV=144, OB=240, SWb=384, EB=112, HB=288, LB=288, XF=256, AR=256, OA=128, nOA=128, OA2=128, OBm=128, tg=128,
-     s1=128, s2=128, s3=128, ug=128, u2=128, ZB=384)
-pool("zh", F16, SH16=128, ID16=128, NI16=128, IDW=160, SELH=144, WR=128, tS=128, qS=128, QB=112, C16=96, RT=96, a16=128,
-     UU=128, eb=128, FH=128)
+     SELV=144, OB=240, SWb=384, EB=112, HB=288, LB=288, XF=256, XD=256, ZW=256, AR=256, OA=128, nOA=128, OBm=128, gF=128,
+     hF=128, hh=128, m1=128, s1=128, s2=128, s3=128, ug=128, u2=128, ZB=384)
+pool("zh", F16, SH16=128, ID16=128, NI16=128, IDW=160, SELH=144, WR=128, tS=128, qS=128, QB=112, C16=96, RT=96, D0=512,
+     SC=512, eb=128, FH=128, DU=16)
 pool("zu", U16, POS=96, POG=96, LNE=24, TO=24, FK=16, OFF=8, OFD=8, XL=96, FL=128)
 for nm, nc in (("PA", 1024), ("PB", 1024), ("PM", 1024), ("LA", 512), ("LB", 512)):
     SCRATCH[nm] = ("psum", [128, nc], F32)
 
 SEMAPHORES = ["v", "s", "t", "q", "arr0", "arr1", "snt0", "snt1"] + ["d%d" % i for i in range(60)]
-C1, CID, CSA, CSB, CLK, C0 = range(6)
 
 
 def rank_program(g, core, T, topo):
@@ -142,6 +143,12 @@ def rank_program(g, core, T, topo):
     def mm(out, l, r, st, sp):
         return lambda e: e.matmul(out, l, r, st, sp)
 
+    def scan(out, d0, d1, first, o0):
+        return lambda e: e.tensor_tensor_scan(out, d0, d1, first, o0, OP.add)
+
+    def rowsum(out, a):
+        return lambda e: e.tensor_reduce(out, a, AxisListType.X, OP.add)
+
     def group(*terms):
         return [mm(o, l, r, j == 0, j == len(terms) - 1) for j, (o, l, r) in enumerate(terms)]
 
@@ -178,20 +185,37 @@ def rank_program(g, core, T, topo):
         o = 160 * list(MASKS).index(mask) + 16 - shift
         return T.TU[:, o:o + 128]
 
+    def zs(name, p, n=64, a=0, st=1):
+        return z(name, n * p + a, n * p + n, st)
+
+    spare = {"v": [], "s": []}
+
+    def later(q, ns, f, *a):
+        spare[q].append((ns, lambda: f(*a)))
+
+    def spend(q, ns):
+        while spare[q] and spare[q][0][0] <= ns:
+            c, f = spare[q].pop(0)
+            f()
+            ns -= c
+
     def tab_load(k, q):
         dma(q, [], ["tab%d" % k], (T.tabI[:, 512 * k:512 * k + 512], T.tab[:, 512 * k:512 * k + 512]))
     tab_load(0, "s")
     dma("y", [], ["CXI"], (z("CXI"), T.cx[:, :]))
     tab_load(1, "y")
     dma("s", [], ["vv0"], (T.VV[0:8, 0:6144], T.vv[:, 0:6144]))
+    dma("y", [], ["cpF"], (T.CPI[:, 288:416], T.suf[:, :]))
     tab_load(2, "s")
     tab_load(3, "y")
-    dma("y", [], ["cpF"], (T.CPI[:, 288:416], T.suf[:, :]))
     dma("y", [], ["cpL"], (T.CPI[:, 0:128], T.lnk[:, :]))
     dma("y", [], ["vv1"], (T.VV[0:8, 6144:12288], T.vv[:, 6144:12288]))
 
     def iota(tile, key, pattern, base, cm, **kw):
         op("q", [], [key], lambda e: e.iota(tile, pattern, base, cm, **kw))
+
+    def select(tile, pattern, test, fill, base, cm):
+        op("q", [tile], [tile], lambda e: e.affine_select(T[tile][:, :], T[tile][:, :], pattern, test, fill, base, cm))
     fl = {"allow_small_or_imprecise_dtypes": True}
     iota(z("i_rm"), "i_rm", [[-1, 16]], 0, 1)
     iota(z("i_g8"), "i_g8", [[-16, 8]], 0, 1)
@@ -206,89 +230,71 @@ def rank_program(g, core, T, topo):
     iota(z("JI"), "JI", [[16, 96]], 0, 0, **fl)
     iota(z("i_wr"), "i_wr", [[1, 128]], 0, 0)
     iota(T.LBA[:, :], "LBA", [[0, 1024]], 1, 0, **fl)
-    iota(T.ST[:, 2048:NW], "STz", [[0, 512]], 0, 0, **fl)
+    iota(z("ZB"), "ZB", [[0, 384]], 0, 0, **fl)
+    iota(z("ZF"), "ZF", [[0, 384]], 0, 0, **fl)
     for tile, sg in (("SELK", 1.0), ("NSELK", -1.0)):
         iota(T[tile][:, :], tile, [[0, 1024]], 0, 0, **fl)
         for r, wt in ((7, 32.0), (8, 1.0)):
-            op("q", [tile], [tile], lambda e, tile=tile, r=r, c=sg * wt: e.affine_select(
-                T[tile][:, :], T[tile][:, :], [[-16, 8], [0, 128]], OP.not_equal, c, -r, 1))
+            select(tile, [[-16, 8], [0, 128]], OP.not_equal, sg * wt, -r, 1)
+    iota(T.TRW[:, :], "TRW", [[0, 1024]], 0, 0, **fl)
+    select("TRW", [[0, 8], [1, 128]], OP.is_gt, 8192.0, 0, -1)
+    iota(T.ST[:, 2048:NW], "STz", [[0, 512]], 0, 0, **fl)
+    iota(T.YN[:, 2304:NW], "YNz", [[0, 256]], 0, 0, **fl)
 
     SR, BA = OP.logical_shift_right, OP.bitwise_and
     dp = z("i_dp", 16, 144)
-    V([], ["AUX"], ms(T.AUX[:, :], 0.0))
+    V([], ["w0"], ms(w[0][:, :], 0.0))
     tz("i_rm", "i_rm", 15, BA)
     tz("i_g8", "i_g8", 4, OP.arith_shift_right)
+    V([], ["COMBX"], ms(T.COMBX[:, :], 0.0))
     tz("i_bm", "i_bm", 4, OP.arith_shift_right)
     tz("RM", "i_rm", 0.0, OP.is_equal)
+    V([], ["COMB"], ms(T.COMB[:, :], 0.0))
+    V(["RM"], ["CB"], tt(z("CB"), RMc(4), RMc(9), OP.add))
     tz("G8", "i_g8", 0.0, OP.is_equal)
     tz("BM", "i_bm", 0.0, OP.is_equal)
-    V([], ["COMB"], ms(T.COMB[:, :], 0.0))
-    tz("SELV", "i_sf", 0.0, OP.is_equal, 1.0 / 16, OP.mult)
     for name, c, o in (("U1", -1.0, OP.is_equal), ("IDN", 0.0, OP.is_equal), ("LTu", 0.0, OP.is_ge), ("ID16", 0.0, OP.is_equal)):
         V(["i_dp"], [name], ts(z(name), dp, c, o))
-    V([], ["COMBX"], ms(T.COMBX[:, :], 0.0))
+    tz("SELV", "i_sf", 0.0, OP.is_equal, 1.0 / 16, OP.mult)
     t2("U1", "U1", "BM", OP.mult)
-    V(["G8", "COMB"], ["cb%d" % C1], cp(T.COMB[:, C1 * 144 + 15:C1 * 144 + 143:16], z("G8")))
-    t2("SH16", "IDN", "U1", OP.subtract)
+    V(["G8", "COMB"], ["cb%d" % C1], ts(T.COMB[:, C1 * 144 + 15:C1 * 144 + 143:16], z("G8"), -1.0, OP.mult))
     V(["G8", "COMBX"], ["COMBX"], cp(T.COMBX[:, 15:143:16], z("G8")))
-    t2("LTB", "LTu", "BM", OP.mult)
-    V([], ["WTz"], ms(T.WT[:, 2048:NW], 0.0))
     tz("IDW", "i_dp", 0.0, OP.is_equal, float(OD), OP.mult)
-    for j, (a, b) in enumerate(MASKS.values()):
-        V(["RM"], ["mk%d" % j], lambda e, j=j, a=a, b=b: e.tensor_reduce(z("MK", j, j + 1), z("RM", a, b), AxisListType.X, OP.add))
+    t2("SH16", "IDN", "U1", OP.subtract)
+    t2("LTB", "LTu", "BM", OP.mult)
+    V(["RM"], ["MK"], *[rowsum(z("MK", j, j + 1), z("RM", a, b)) for j, (a, b) in enumerate(MASKS.values())])
 
-    def early_a():
-        V(["CXI"], ["c0_0", "c0_1"], cp(T.CL[:, 0:96], z("CXI")))
-        V(["CXI"], ["C160", "C161"], ts(z("C16"), z("CXI"), -1024.0, OP.add))
-
-    def early_b():
-        V(["cpF"], ["FC"], ts(z("FC"), T.CPI[:, 288:416], -1024.0, OP.add))
-        dma("y", ["FC", "DF"], ["DF"], (T.DT[15:128:16, 0:2048], z("FC")))
-        V(["IDW"] + ["mk%d" % j for j in range(6)], ["TU"],
-          *[ts(T.TU[:, 160 * j:160 * j + 160], z("IDW"), z("MK", j, j + 1), OP.mult) for j in range(6)])
-
-    def early_c():
-        V(["BM", "RM"], ["BC"], *[ts(T.BC[:, 128 * a:128 * a + 128], z("BM"), RMc(a), OP.mult) for a in range(12)])
-    ncol = [0]
-
-    def column(terms):
-        prev, key = None, None
-        for r, wt in terms:
-            c = ncol[0]
-            ncol[0] += 1
-            out = z("COLS", c, c + 1)
-            kw = {"bias": prev} if key else {}
-            S(["RM"] + ([key] if key else []), ["col%d" % c], ac(out, RMc(r), AF.Identity, scale=float(wt), **kw))
-            prev, key = out, "col%d" % c
-        return prev, key
-
-    def make_comb(v, col, key):
-        S([key, "G8", "COMB"], ["cb%d" % v], ac(T.COMB[:, v * 144 + 15:v * 144 + 143:16], z("G8"), AF.Copy, scale=col))
+    def scan_constants():
+        V([], ["D00", "D01"], ms(z("D0", 0, 512, 4), 0.0), ms(z("D0", 2, 512, 4), 1.0))
+        for p in (0, 1):
+            V([LK[p]], ["D1%d" % p], ms(LP[p][:, 0:256:4], 1.0625), ms(LP[p][:, 1:256:4], -1.0625 * B0),
+              ms(LP[p][:, 3:256:4], B0 - 255.0 / 512))
+    V([], ["WTz"], ms(T.WT[:, 2048:NW], 0.0))
 
     def scaled(out, a, col, key):
         S([a, key], [out], ac(z(out), z(a), AF.Copy, scale=col))
 
     def root(p):
-        S(["C16%d" % p], ["RT%d" % p], ac(z("RT", 48 * p, 48 * p + 48), z("C16", 48 * p, 48 * p + 48), AF.Sigmoid,
-                                             bias=-256 * 1023.5, scale=-256.0))
+        S(["C16%d" % p], ["RT%d" % p], ac(zs("RT", p, 48), zs("C16", p, 48), AF.Sigmoid, bias=-256 * 1023.5, scale=-256.0))
 
     S(["RM"], ["KB"], ac(z("KB"), RMc(15), AF.Identity, bias=4096 * B0 - 128, scale=1e9))
-    colB, kB = column([(4, 1), (9, 1)])
-    S(["AUX", kB], ["AUX"], ac(T.AUX[:, 0:2304], T.AUX[:, 0:2304], AF.Identity, bias=colB))
-    S(["AUX", "RM"], ["AUX"], ac(T.AUX[:, 2304:NW], T.AUX[:, 2304:NW], AF.Identity, bias=RMc(4)))
+    S(["w0", "CB", "RM"], ["AUX"], *([ac(T.AUX[:, a:a + H], w[0][:, :], AF.Identity, bias=z("CB")) for a in range(0, 2304, H)]
+                                     + [ac(T.AUX[:, 2304:NW], w[0][:, 0:256], AF.Identity, bias=RMc(4))]))
 
-    def targets(rnd):
+    def targets(rnd, P, pk, h0, h1):
         o = WHERE["SELV"][1]
-        for hs in range(8):
+        for hs in range(h0, h1):
             b = (8 * rnd + hs) * H
-            PE(["vv%d" % rnd, "SELV"], ["#M"], *group(*[(PM[:, 64 * hs:64 * hs + 64], T.zb[0:8, o + 15 - a:o + 143 - a],
-                                                         T.VV[0:8, b + c0:b + c1:st]) for a, (c0, c1, st) in enumerate(ROWS)]))
-        S(["#M"], ["VL%d" % rnd], ac(T.VL[:, 512 * rnd:512 * rnd + 512], PM[:, 0:512], AF.Copy))
+            PE(["vv%d" % rnd, "SELV"], [pk], *group(*[(P[:, 64 * hs:64 * hs + 64], T.zb[0:8, o + 15 - a:o + 143 - a],
+                                                       T.VV[0:8, b + c0:b + c1:st]) for a, (c0, c1, st) in enumerate(ROWS)]))
+
+    def targets_out(rnd, P, pk):
+        S([pk], ["VL%d" % rnd], ac(T.VL[:, 512 * rnd:512 * rnd + 512], P[:, 0:512], AF.Copy))
 
     def counts(k):
         a, b = 512 * k, 512 * k + 512
         V(["tab%d" % k], ["ci%d" % k], ts(T.CI[:, a:b], T.tabI[:, a:b], 15, BA))
-        V(["ci%d" % k], ["wt%d" % k], ts(T.WT[:, a:b], T.CI[:, a:b], -1.0 / 16, OP.add, -TINY, OP.max))
+        return lambda: V(["ci%d" % k], ["wt%d" % k], ts(T.WT[:, a:b], T.CI[:, a:b], -1.0 / 16, OP.add, -TINY, OP.max))
 
     def pointers(k):
         a, b = 512 * k, 512 * k + 512
@@ -300,125 +306,119 @@ def rank_program(g, core, T, topo):
         P, pk = ((T.PA, "#A"), (T.PB, "#B"), (PM, "#M"), (PM, "#M"))[k]
         PE(["sh%d" % k, "SH16"], [pk], mm(P[:, 0:512], z("SH16"), T.SH[:, a:b], True, True))
         S([pk], ["dt%d" % k], ac(T.DT[:, OD + a:OD + b], P[:, 0:512], AF.Copy))
-    counts(0)
-    early_a()
+    rest = counts(0)
+    V(["CXI"], ["C160", "C161"], ts(z("C16"), z("CXI"), -1024.0, OP.add))
+    V(["CXI"], ["c0_0", "c0_1"], cp(T.CL[:, 0:96], z("CXI")))
+    rest()
     root(0)
     root(1)
+    pointers(0)
+    V(["IDW", "MK"], ["TU"], *[ts(T.TU[:, 160 * j:160 * j + 160], z("IDW"), z("MK", j, j + 1), OP.mult) for j in range(6)])
+    rest = counts(1)
+    pointers(1)
+    rest()
     scaled("NLT", "LTB", -1.0, "LTB")
     scaled("N16", "IDN", -1.0 / 16, "IDN")
-    counts(1)
-    pointers(0)
-    counts(2)
-    pointers(1)
-    targets(0)
+    V(["cpF"], ["FC"], ts(z("FC"), T.CPI[:, 288:416], -1024.0, OP.add))
+    V(["cpF"], ["FH"], cp(z("FH"), T.CPI[:, 288:416]))
+    dma("y", ["FC", "DF"], ["DF"], (T.DT[15:128:16, 0:2048], z("FC")))
+    dma("y", ["FH"], ["FB"], (T.FB[0:8, :], z("FH")))
+    targets(0, PM, "#M", 0, 8)
     differences(0)
     differences(1)
-    counts(3)
+    targets_out(0, PM, "#M")
+    rest = counts(2)
+    pointers(2)
+    rest()
+    differences(2)
+    rest = counts(3)
+    scan_constants()
+    rest()
     WTK = ["WT", "WTz", "WTn"] + ["wt%d" % k for k in range(4)]
+    YNK = ["YN", "YNz", "YNn"] + ["yn%d" % k for k in range(9)]
     DTK = ["DT", "DF", "DTn", "DFn"] + ["dt%d" % k for k in range(4)]
     STK = ["STz"] + ["st%d" % k for k in range(4)]
     AFK = ["AFn"] + ["af%d" % k for k in range(8)]
+    LBK = ["LBA"] + ["lb%d" % i for i in range(10)]
+
+    def first_gap():
+        V(["tab3"], ["yb3"], ts(T.YB[:, 1536:2048], T.tabI[:, 1536:2048], -7.5, OP.add, 201326592.0, OP.add))
+        V(["BM", "RM"], ["BC"], *[ts(T.BC[:, 128 * a:128 * a + 128], z("BM"), RMc(a), OP.mult) for a in range(12)])
+        tz("SELH", "i_sf", 0.0, OP.is_equal)
+
+    def last_differences():
+        S(["yb3"], ["sh3"], ac(T.SH[:, 1536:2048], T.YB[:, 1536:2048], AF.Identity, bias=-12583936.0, scale=0.0625))
+        differences(3)
+
+    def suffix_list():
+        o = WHERE["SELH"][1]
+        PE(["FB", "SELH"], ["#M"], *group(*[(PM[:, 512:640], T.zh[0:8, o + 15 - i:o + 143 - i], T.FB[0:8, i:2048:16]) for i in range(16)]))
+        V(["#M"], ["FL"], cp(z("FL"), PM[:, 512:640]))
 
     def zeros():
         dma("y", ["ZB", "VW"], ["VW"], (T.VW[:, 0:384], z("ZB")))
         dma("y", ["ZF", "SW"], ["SW"], (T.SW[:, 0:384], z("ZF")))
 
-    def late_a():
-        b32 = 129.0 - 31.0 / 64
-        V(["cpj"], ["cpj"], ts(T.CPI[:, 128:256], T.CPI[:, 128:256], 2047, BA))
-        V(["cpk"], ["cpk"], ts(T.CPI[:, 256:288], T.CPI[:, 256:288], 511, BA))
-        tz("i_jc", "i_jc", 1023, BA)
-        V(["cpL", "cpj"], ["HBa"], ts(z("HB", 0, 256), T.CPI[:, 0:256], 1.0 / 32, OP.mult, b32, OP.add))
-        V(["cpL", "cpj", "cpk"], ["cpl"], ts(T.CPL[:, :], T.CPI[:, 0:288], 31, BA))
-        V(["cpk"], ["HBb"], ts(z("HB", 256, 288), T.CPI[:, 256:288], 1.0 / 32, OP.mult, b32 + 64.0, OP.add))
-        V(["cpl"], ["LB"], cp(z("LB"), T.CPL[:, :]))
+    b32 = 129.0 - 31.0 / 64
+
+    def aux_rows():
         for j, (r, key, t, a) in enumerate(((2, "HBa", "HB", 0), (3, "LB", "LB", 0), (7, "HBa", "HB", 128), (8, "LB", "LB", 128))):
             dma("y", [key, "AUX"], ["ar%d" % j], (T.AUX[r:128:16, 0:2048], z(t, a, a + 128)))
         dma("y", ["HBb", "AUX"], ["ar4"], (T.AUX[7:128:16, 2048:NW], z("HB", 256, 288)))
         dma("y", ["LB", "AUX"], ["ar5"], (T.AUX[8:128:16, 2048:NW], z("LB", 256, 288)))
-
-    def late_0():
-        V(["cpF"], ["FH"], cp(z("FH"), T.CPI[:, 288:416]))
-        dma("y", ["FH"], ["FB"], (T.FB[0:8, :], z("FH")))
-        tz("i_pc", "i_pc", 15, BA)
-        V([], ["DL"], ms(z("DL"), 0.0))
-        V([], ["HT"], ms(z("HT"), 0.0))
-        V(["i_pc"], ["PC"], cp(z("PC"), z("i_pc", 0, 1)))
-        tz("SELH", "i_sf", 0.0, OP.is_equal)
-
-    def suffix_list(j):
-        o = WHERE["SELH"][1]
-        P = LB[:, 256 + 64 * j:320 + 64 * j]
-        PE(["FB", "SELH"], ["#LB"], *group(*[(P, T.zh[0:8, o + 15 - i:o + 143 - i], T.FB[0:8, 1024 * j + i:1024 * j + 1024:16])
-                                             for i in range(16)]))
-
-    def late_b():
-        V(["i_jc"], ["BI"], *[ts(T.BI[:, 64 * i:64 * i + 64], z("i_jc"), i, SR, 1, BA) for i in range(10)])
-
-    def late_b2():
-        V(["BI"], ["BB"], cp(T.BB[:, :], T.BI[:, :]))
-        for i in range(10):
-            dma("y", ["BB", "LBA"], ["lb%d" % i], (T.LBA[i:128:16, :], T.BB[:, 64 * i:64 * i + 64]))
-
-    def late_c():
-        V([], ["ZB"], ms(z("ZB"), 0.0))
-        V([], ["ZF"], ms(z("ZF"), 0.0))
         zeros()
-        V([], ["OB"], ms(z("OB"), 0.0))
-        V([], ["EB"], ms(z("EB", 0, 16), 0.0))
-        V([], ["QB"], ms(z("QB", 0, 16), 0.0))
-        V([], ["D1"], ms(z("D1"), 16.0))
-        V([], ["A2z"], ms(T.A2[:, 1536:1552], 0.0))
-        V([], ["mz"], ms(T.MM[:, 1536:1552], 0.0))
 
-    def late_d():
-        V([], ["SND0z"], ms(T.SND0[:, 384:432], 0.0))
-        V([], ["SND1z"], ms(T.SND1[:, 384:400], 0.0))
-        V(["i_dp"], ["TRI"], ts(z("TRI"), dp, 0.0, OP.is_le, 8192.0, OP.mult))
-        V(["OB"], ["OB"], ms(z("OB", 112, 128), 1.0))
-        V(["PC", "D1"], ["D1"], cp(z("D1", 0, 1), z("PC")))
+    def lane_bits():
+        for i in range(10):
+            dma("y", ["BB%d" % (i // 5), "LBA"], ["lb%d" % i], (T.LBA[i:128:16, :], T.BB[:, 64 * i:64 * i + 64]))
 
-    def late_e():
-        V(["i_dp"], ["U2"], ts(z("U2"), dp, 1.0, OP.is_equal))
-        tz("WR", "i_wr", 1024.0, OP.add)
-        t2("U2", "U2", "BM", OP.mult)
-        t2("NUT", "LTB", "BM", OP.subtract)
-        t2("BID", "IDN", "U2", OP.subtract)
+    def fills(key, *pairs):
+        V([key], [key], *[ms(a, c) for a, c in pairs])
+    for ns, R, W, f in (
+            (110, ["cpj"], ["cpj"], ts(T.CPI[:, 128:256], T.CPI[:, 128:256], 2047, BA)),
+            (60, ["cpk"], ["cpk"], ts(T.CPI[:, 256:288], T.CPI[:, 256:288], 511, BA)),
+            (60, ["i_pc"], ["i_pc"], ts(z("i_pc"), z("i_pc"), 15, BA)),
+            (60, ["i_jc"], ["i_jc"], ts(z("i_jc"), z("i_jc"), 1023, BA)),
+            (60, [], ["DL"], ms(z("DL"), 0.0)),
+            (60, [], ["HT"], ms(z("HT"), 0.0)),
+            (240, ["cpL", "cpj", "cpk"], ["cpl"], ts(T.CPL[:, :], T.CPI[:, 0:288], 31, BA)),
+            (220, ["cpL", "cpj"], ["HBa"], ts(z("HB", 0, 256), T.CPI[:, 0:256], 1.0 / 32, OP.mult, b32, OP.add)),
+            (60, ["cpk"], ["HBb"], ts(z("HB", 256, 288), T.CPI[:, 256:288], 1.0 / 32, OP.mult, b32 + 64.0, OP.add)),
+            (60, ["i_pc"], ["PC"], cp(z("PC"), z("i_pc", 0, 1))),
+            (240, ["cpl"], ["LB"], cp(z("LB"), T.CPL[:, :]))):
+        later("v", ns, V, R, W, f)
+    later("v", 0, aux_rows)
+    for i in range(10):
+        later("v", 60, V, ["i_jc"], ["BI%d" % i], ts(T.BI[:, 64 * i:64 * i + 64], z("i_jc"), i, SR, 1, BA))
+    later("v", 180, lambda: (V([], ["W16"], ms(z("W16"), 0.0)), V([], ["TWO"], ms(z("TWO"), 2.0)), V([], ["Z16"], ms(z("Z16"), 0.0))))
+    for j in range(2):
+        later("v", 270, V, ["BI%d" % i for i in range(5 * j, 5 * j + 5)], ["BB%d" % j],
+              cp(T.BB[:, 320 * j:320 * j + 320], T.BI[:, 320 * j:320 * j + 320]))
+    later("v", 0, lane_bits)
+    for j in (2, 3):
+        later("v", 60, V, ["W16", "TWO", "Z16"], ["W%d" % j], scan(z("W16", 16 * j, 16 * j + 10), z("TWO", 0, 10), z("Z16", 0, 10), 0.5, OP.mult))
+    for j, wts in enumerate(WEIGHTS.values()):
+        later("v", 60 * len(wts), V, ["W16"], ["Wr%d" % j], *[ms(z("W16", 16 * j + r, 16 * j + r + 1), float(c)) for r, c in wts.items()])
+    later("v", 100, V, [], ["OB"], ms(z("OB"), 0.0))
+    later("v", 120, lambda: (V([], ["EB"], ms(z("EB", 0, 16), 0.0)), V([], ["QB"], ms(z("QB", 0, 16), 0.0))))
+    for j in range(4):
+        later("v", 60, V, ["RM", "W2", "W3", "Wr%d" % j], ["WM%d" % j], tt(z("WM", 16 * j, 16 * j + 16), z("W16", 16 * j, 16 * j + 16), z("RM"), OP.mult))
+    later("v", 80, V, [], ["D1"], ms(z("D1"), 16.0))
+    later("v", 120, lambda: (V([], ["A2z"], ms(T.A2[:, 1536:1552], 0.0)), V([], ["mz"], ms(T.MM[:, 1536:1552], 0.0))))
+    for j in range(4):
+        later("v", 60, V, ["WM%d" % j], ["WC%d" % j], rowsum(z("WC", j, j + 1), z("WM", 16 * j, 16 * j + 16)))
+    later("v", 120, lambda: (V([], ["SND0z"], ms(T.SND0[:, 384:432], 0.0)), V([], ["SND1z"], ms(T.SND1[:, 384:400], 0.0))))
+    later("v", 120, lambda: (fills("OB", (z("OB", 112, 128), -1.0)), V(["PC", "D1"], ["D1"], cp(z("D1", 0, 1), z("PC")))))
+    for j, v in enumerate(WEIGHTS):
+        later("v", 60, V, ["WC%d" % j, "G8", "COMB"], ["cb%d" % v], ts(T.COMB[:, v * 144 + 15:v * 144 + 143:16], z("G8"), z("WC", j, j + 1), OP.mult))
+    later("v", 110, V, ["i_dp"], ["U2"], ts(z("U2"), dp, 1.0, OP.is_equal))
+    later("v", 110, tz, "WR", "i_wr", 1024.0, OP.add)
+    later("v", 220, t2, "NUT", "LTB", "BM", OP.subtract)
+    later("v", 220, t2, "U2", "U2", "BM", OP.mult)
+    later("v", 220, t2, "BID", "IDN", "U2", OP.subtract)
 
-    todo = []
-
-    def drain(m):
-        for _ in range(min(m, len(todo))):
-            todo.pop(0)()
-
-    def later(f, *a):
-        todo.append(lambda: f(*a))
-
-    def shifted(out, a, na, c, o=0, i=0, scale=1.0):
-        S([a, "PC"], [out], ac(z(out, o, o + na), z(a, i, i + na), AF.Identity, bias=c, scale=scale))
-
-    def later_comb(v, terms):
-        later(lambda: make_comb(v, *column(terms)))
-
-    def slot_combs():
-        sa = column([(i, 1 << i) for i in range(10)] + [(15, -1536)])
-        make_comb(CSA, *sa)
-        c = ncol[0]
-        ncol[0] += 1
-        S(["RM", sa[1]], ["colx"], ac(z("COLS", c, c + 1), RMc(15), AF.Identity, bias=sa[0], scale=768.0))
-        make_comb(CSB, z("COLS", c, c + 1), "colx")
-
-    def smalls():
-        shifted("JL", "JI", 96, z("PC"))
-        for p in (0, 1):
-            shifted("JQ", "JL", 48, 1536.0, 48 * p, 0, 2.0)
-        shifted("JD", "JL", 24, 1536.0)
-        for t in range(2):
-            shifted("DUM%d" % t, "JL", 8, 2304.0 + 128 * t)
-            shifted("DUM%d" % t, "JL", 8, 2304.0 + 128 * t, 8)
-        scaled("NI16", "IDN", -1.0, "IDN")
-
-    LBK = ["LBA"] + ["lb%d" % i for i in range(10)]
+    def shifted(out, a, na, c, o=0, scale=1.0, st=1):
+        S([a, "PC"], [out], ac(z(out, o, o + na * st, st), z(a, 0, na), AF.Identity, bias=c, scale=scale))
 
     def plain_pointers(k):
         S(["yb%d" % k], ["st%d" % k], ac(T.ST[:, 512 * k:512 * k + 512], T.YB[:, 512 * k:512 * k + 512], AF.Identity,
@@ -426,29 +426,32 @@ def rank_program(g, core, T, topo):
 
     def suffix_aux(k):
         S(AUXK + ["FL"], ["af%d" % k], ac(T.AUF[:, 256 * k:256 * k + 256], T.AUX[:, 0:2048].indirect(z("FL", 16 * k, 16 * k + 16)), AF.Copy))
-    later(smalls)
-    later(lambda: (scaled("CANDM", "BM", *column([(9, -1)])), make_comb(CLK, *column([(2, 32), (3, 1), (4, -32)])),
-                   make_comb(C0, RMc(0), "RM")))
-    later(slot_combs)
-    later_comb(CID, [(4, -1024 - 4128), (7, 32), (8, 1)])
+    later("s", 80, shifted, "JL", "JI", 96, z("PC"))
+    later("s", 110, scaled, "NI16", "IDN", -1.0, "IDN")
+    later("s", 110, scaled, "CANDM", "BM", RMc(9), "RM")
+    later("s", 60, S, ["RM", "G8", "COMB"], ["cb%d" % C0], ac(T.COMB[:, C0 * 144 + 15:C0 * 144 + 143:16], z("G8"), AF.Copy, scale=RMc(0)))
+    later("s", 60, shifted, "JQ", "JL", VS // 16, 1536.0 / OD, 0, 2.0 / OD)
+    later("s", 60, shifted, "PJ", "JL", 24, 1536.0, 1, 1.0, 2)
+    later("s", 60, shifted, "DUM0", "JL", 8, 2304.0)
+    later("s", 60, shifted, "DUM1", "JL", 8, 2432.0)
+    later("s", 60, shifted, "JQ", "JL", 96 - VS // 16, 1536.0 / OD, VS // 16, 2.0 / OD)
+    later("s", 60, shifted, "DU", "JL", 16, 256.0)
+    for k in range(4):
+        later("s", 430, plain_pointers, k)
     for k in range(8):
-        later(suffix_aux, k)
-    later(lambda: S(LBK, ["LBB"], ac(T.LBB[:, :], T.LBA[:, 0:H], AF.Identity, bias=-200.0, scale=400.0)))
+        later("s", 300, suffix_aux, k)
+    later("s", 900, S, LBK, ["LBB"], ac(T.LBB[:, :], T.LBA[:, 0:1536 - VS], AF.Identity, bias=-200.0, scale=400.0))
 
     def lists(p, idx):
         return T.CL[:, idx * 96 + 48 * p:idx * 96 + 48 * p + 48], "c%d_%d" % (idx, p)
 
-    def zs(name, p, n=64, a=0, st=1):
-        return z(name, n * p + a, n * p + n, st)
-
     def halves(P, l, src):
-        return [(P[:, 0:512], l, src[:, 0:512]), (P[:, 512:H], l, src[:, 512:H])]
+        return [mm(P[:, 0:512], l, src[:, 0:512], True, False), mm(P[:, 512:H], l, src[:, 512:H], True, False)]
 
-    def spread(P, src, p, close):
-        return [mm(P[:, c0:c1:st], T.BC[:, 128 * a:128 * a + 128], zs(src, p), False, close and a in (7, 11))
-                for a, (c0, c1, st) in enumerate(ROWS)]
+    def spread(P, src):
+        return [mm(P[:, c0:c1:st], T.BC[:, 128 * a:128 * a + 128], src, False, a in (7, 11)) for a, (c0, c1, st) in enumerate(ROWS)]
 
-    def s0(p, idx, k):
+    def gather_counts(p, idx, k):
         off, ck = lists(p, idx)
         wi = T.WT[:, 0:2304].indirect(off)
         if k:
@@ -456,55 +459,50 @@ def rank_program(g, core, T, topo):
         else:
             op("vs"[p], WTK + [ck], ["w%d" % p], ac(w[p][:, :], wi, AF.Copy) if p else cp(w[p][:, :], wi))
 
-    def s1(p):
+    def sums(p, k):
         L, sp = LP[p], str(p)
+        S(["VL%d" % (k // SP)], ["D0v" + sp], ac(zs("D0", p, 256, 3, 4), T.VL[:, 128 * k + 64 * p:128 * k + 64 * p + 64], AF.Copy))
         PE(["w" + sp, "cb%d" % C1], [LK[p]],
-           *group(*[(L[:, 0:64], comb(C1, a), w[p][:, c0:c1:st]) for a, (c0, c1, st) in enumerate(ROWS)]))
-        S([LK[p]], ["a16" + sp], ac(zs("a16", p), L[:, 0:64], AF.Identity, bias=B0 + 0.48, scale=1.003))
-        S(["a16" + sp], ["a1" + sp], ac(zs("a1", p), zs("a16", p), AF.Identity, bias=-1.0625 * B0, scale=1.0625))
-        PE(["w" + sp, "NLT"], [PK[p]], *[mm(o, l, r, True, False) for o, l, r in halves(PX[p], z("NLT"), w[p])])
-        PE(["a16" + sp, "RT" + sp, "ID16", "TU"], [LK[p]], *group(
-            (L[:, 64:128], z("ID16"), zs("a16", p)),
-            *[(L[:, 64 + r:128:st], turn(*BACK[j]), z("RT", 48 * p + c0, 48 * p + c1)) for j, (_, _, (r, st), (c0, c1)) in enumerate(TURN)]))
+           *group(*[(L[:, 2:256:4], comb(C1, a), w[p][:, c0:c1:st]) for a, (c0, c1, st) in enumerate(ROWS)]))
+        S([LK[p]], ["D0a" + sp], ac(zs("D0", p, 256, 1, 4), L[:, 2:256:4], AF.Identity, bias=B0 + 0.48, scale=-1.003))
+        PE(["w" + sp, "NLT"], [PK[p]], *halves(PX[p], z("NLT"), w[p]))
+        PE(["D0a" + sp, "ID16"], [PK[1 - p]], mm(PX[1 - p][:, H:H + 64], z("ID16"), zs("D0", p, 256, 1, 4), False, True))
 
-    def s2(p, idx, k):
-        L, sp, s = LP[p], str(p), k % SP
-        v = T.VL[:, 128 * k + 64 * p:128 * k + 64 * p + 64]
-        V([LK[p], "a1" + sp], ["tq" + sp], tt(L[:, 0:64], zs("a1", p), L[:, 0:64], OP.subtract))
-        V([LK[p], "tq" + sp, "VL%d" % (k // SP)], ["y" + sp], tt(zs("y", p), L[:, 0:64], v, OP.mult))
-        V(["y" + sp], ["UU" + sp], ts(zs("UU", p), zs("y", p), B0 - 255.0 / 512, OP.add))
-        V([LK[p], "UU" + sp], ["eb" + sp], tt(zs("eb", p), zs("UU", p), L[:, 64:128], OP.is_lt))
+    def roots(p):
+        A = PX[1 - p]
+        PE(["D0%d" % p, "RT%d" % p, "ID16", "TU"], [PK[1 - p]], mm(A[:, H:H + 64], z("ID16"), zs("D0", p, 256, 0, 4), True, False),
+           *[mm(A[:, H + r:H + 64:st], turn(*BACK[j]), z("RT", 48 * p + c0, 48 * p + c1), False, False)
+             for j, (_, _, (r, st), (c0, c1)) in enumerate(TURN)])
 
-        def xo():
-            PE(["eb" + sp, "C16" + sp, "ID16", "TU"], [LK[p]], *group(
-                (L[:, 128:176], z("ID16"), zs("C16", p, 48)),
-                *[(L[:, 128 + c0:128 + c1], turn(m, sh), zs("eb", p, 64, r, st)) for m, sh, (r, st), (c0, c1) in TURN]))
+    def floor_vt(p):
+        sp = str(p)
+        V([LK[p], "D0" + sp, "D0a" + sp, "D0v" + sp, "D1" + sp], ["SC" + sp], scan(zs("SC", p, 256), zs("D0", p, 256), LP[p][:, 0:256], 0.0, OP.mult))
 
-        def flags():
-            if s == SP - 1:
-                S([LK[p], "EB"], ["EB" + sp], ac(z("EB", 16 + 48 * p, 64 + 48 * p), L[:, 128:176], AF.Sigmoid, bias=-256 * 1151.5, scale=256.0))
-            if p == 0:
-                S([LK[0], "HT"], ["E8" if s == SP - 1 else "HT"], ac(z("E8") if s == SP - 1 else z("HT", s + 2, 40, 5), L[:, 128:136],
-                                                                     AF.Sigmoid, bias=256 * 1151.5, scale=-256.0))
-                S(["C160", "DL"], ["DL"], ac(z("DL", s + 1, 40, 5), z("C16", 0, 8), AF.Identity, bias=1024.0))
-        first = s == SP - 1 and p == 1
-        if first:
-            xo()
-            flags()
-        PE(["UU" + sp, "BC"], [PK[p]], *spread(PX[p], "UU", p, True))
-        if not first:
-            xo()
+    def stays(p):
+        V([PK[1 - p], "SC%d" % p], ["eb%d" % p], tt(zs("eb", p), zs("SC", p, 256, 3, 4), PX[1 - p][:, H:H + 64], OP.is_lt))
 
-        def compare():
-            S([PK[p], "KB"], ["k" + sp], ac(cond[p][:, :], PX[p][:, 0:H], AF.Sigmoid, bias=z("KB"), scale=-4096.0))
-            if not first:
-                flags()
-        return compare
+    def turned(p):
+        return [(LP[p][:, 320 + c0:320 + c1], turn(m, sh), zs("eb", p, 64, r, st)) for m, sh, (r, st), (c0, c1) in TURN]
+
+    def window(p):
+        PE(["eb%d" % p, "C16%d" % p, "ID16", "TU"], [LK[p]], *group((LP[p][:, 320:368], z("ID16"), zs("C16", p, 48)), *turned(p)))
+
+    def bound(p):
+        PE(["SC%d" % p, "BC"], [PK[p]], *spread(PX[p], zs("SC", p, 256, 3, 4)))
+
+    def compare(p):
+        S([PK[p], "KB"], ["k%d" % p], ac(cond[p][:, :], PX[p][:, 0:H], AF.Sigmoid, bias=z("KB"), scale=-4096.0))
+
+    def history(s):
+        if s == SP - 1:
+            S(["#LA", "EB"], ["EB0"], ac(z("EB", 16, 64), LA[:, 320:368], AF.Sigmoid, bias=-256 * 1151.5, scale=256.0))
+        S(["#LA", "HT"], ["E8" if s == SP - 1 else "HT"], ac(z("E8") if s == SP - 1 else z("HT", s + 2, 40, 5), LA[:, 320:328],
+                                                             AF.Sigmoid, bias=256 * 1151.5, scale=-256.0))
+        S(["C160", "DL"], ["DL"], ac(z("DL", s + 1, 40, 5), z("C16", 0, 8), AF.Identity, bias=1024.0))
 
     def marks_sum(p, k):
         if k < RO * SP - 1:
-            PE(["w%d" % p, "N16", "eb%d" % p, "BC"], ["#M"], *([mm(o, l, r, True, False) for o, l, r in halves(PM, z("N16"), w[p])]
-                                                               + spread(PM, "eb", p, True)))
+            PE(["w%d" % p, "N16", "eb%d" % p, "BC"], ["#M"], *(halves(PM, z("N16"), w[p]) + spread(PM, zs("eb", p))))
 
     def marks(p, k):
         if k < RO * SP - 1:
@@ -514,24 +512,26 @@ def rank_program(g, core, T, topo):
         off, ck = lists(p, 5 * rnd + SP - 1)
         S(AFK + [ck], ["A2%d" % p], ac(T.A2[:, H * p:H * p + H], T.AUF[:, 0:2048 + 128 * rnd].indirect(off), AF.Copy))
 
-    def s3a(p):
-        V([LK[p]], ["XL%d" % p], ts(zs("XL", p, 48), LP[p][:, 128:176], 1024.0, OP.add))
+    def window_offsets(p):
+        V([LK[p]], ["XL%d" % p], ts(zs("XL", p, 48), LP[p][:, 320:368], 1024.0, OP.add))
 
-    def s3(p, rnd):
+    def gather_next(p, rnd):
         sp = str(p)
         V(DTK + ["XL" + sp, "k" + sp], ["X" + sp], tt(X[p][:, :], T.DT[:, 0:OD + 2048 + 128 * rnd].indirect(zs("XL", p, 48)), cond[p][:, :], OP.mult))
-        PE(["X" + sp, "COMBX"], [LK[p]], *group(*[(LP[p][:, 192:240], T.COMBX[:, 15 - i:143 - i], X[p][:, i:H:16]) for i in range(16)]))
+        PE(["X" + sp, "COMBX"], [LK[p]], *group(*[(LP[p][:, 368:416], T.COMBX[:, 15 - i:143 - i], X[p][:, i:H:16]) for i in range(16)]))
 
-    def s4(p, idx, rnd):
+    def next_list(p, idx, rnd, gap):
         off, ck = lists(p, idx)
-        P, sp, last = LP[p][:, 192:240], str(p), idx % 5 == SP
+        P, sp, last = LP[p][:, 368:416], str(p), idx % 5 == SP
         if rnd == 0:
             if p == 0 or not last:
                 V([LK[p]], [ck], ts(off, P, 1024.0, OP.add))
             S([LK[p]], ["C16" + sp], ac(zs("C16", p, 48), P, AF.Copy))
         else:
             V([LK[p]], ["rr" + sp], ts(zs("rr", p, 48), P, M35, OP.add, -M35, OP.add))
+            gap()
             V([LK[p], "rr" + sp], ["C16" + sp], tt(zs("C16", p, 48), P, zs("rr", p, 48), OP.subtract))
+            gap()
             if p == 0 or not last:
                 V(["C16" + sp], [ck], ts(off, zs("C16", p, 48), 1024.0, OP.add))
         if last:
@@ -542,214 +542,267 @@ def rank_program(g, core, T, topo):
     nxt = T.cores[(rank + 1) % len(T.cores)]
     rid, pid = topo.addr(nxt, core)
     rmask, ne = topo.mask(core, nxt), len(topo.engines(core, nxt))
-    suffix_copy = lambda: V(["#LB"], ["FL"], cp(z("FL"), LB[:, 256:384]))
-    fill = {0: [lambda: pointers(2), early_c, lambda: pointers(3), late_0], 1: [late_b], 2: [suffix_copy, late_b2], 3: [late_c],
-            4: [late_d], 5: [late_e]}
-    fill_t = {0: lambda: (differences(2), differences(3), late_a()), 1: lambda: (suffix_list(0), suffix_list(1))}
+    gap = lambda: spend("v", 200)
 
     for rnd in range(RO):
-        base, i4 = 5 * rnd, 5 * rnd + SP
+        base, i4, k3 = 5 * rnd, 5 * rnd + SP, SP * rnd + SP - 1
         DUM = "DUM%d" % rnd
+        TB, TBK, TBn, one = (T.WT, WTK, "WTn", 15.0 / 16) if rnd == 0 else (T.YN, YNK, "YNn", 1.0)
         for n in range(2 * SP):
-            p, s = n % 2, n // 2
+            p, s, o = n % 2, n // 2, 1 - n % 2
             k, idx = rnd * SP + s, base + s
             if k == 0 and n == 0:
-                s0(0, idx, k)
-                s0(1, idx, k)
-                early_b()
+                gather_counts(0, idx, k)
+                gather_counts(1, idx, k)
+                first_gap()
             elif k:
-                s0(p, idx, k)
-            s1(p)
+                gather_counts(p, idx, k)
+            roots(p)
+            sums(p, k)
             if n:
-                marks(1 - p, rnd * SP + (n - 1) // 2)
-                s3a(1 - p)
-                s3(1 - p, rnd)
+                marks(o, rnd * SP + (n - 1) // 2)
+                gather_next(o, rnd)
+                spend("v", 300)
+            else:
+                spend("v", 900 * rnd)
             if s == SP - 1:
                 shown(p, rnd)
             elif n:
-                drain(1 if n < 3 else 2)
+                spend("s", 900)
+            if k == 0 and n == 0:
+                last_differences()
+            floor_vt(p)
+            gap()
+            if n == 2 * SP - 1:
+                break
+            bound(p)
             if n == 0:
-                for f in fill.pop(8 * rnd + n, []):
-                    f()
-            compare = s2(p, idx, k)
-            for f in fill.pop(8 * rnd + n, []):
-                f()
-            if n:
-                s4(1 - p, base + (n + 1) // 2, rnd)
-            if n == 0:
-                fill_t.pop(8 * rnd + n, lambda: None)()
-            compare()
-            if n < 2 * SP - 1:
-                marks_sum(p, k)
-            fill_t.pop(8 * rnd + n, lambda: None)()
-            drain(1 if n < 5 else len(todo) if n == 5 else 0)
+                stays(p)
+                spend("v", 1000)
+            else:
+                stays(p)
+                spend("v", 400)
+                next_list(o, base + (n + 1) // 2, rnd, gap)
+            window(p)
+            window_offsets(p)
+            if k == 0 and n == 0:
+                suffix_list()
+            compare(p)
+            if p == 0:
+                history(s)
+            marks_sum(p, k)
+            spend("s", 900)
+            if n == 5:
+                spend("v", 9000)
+                spend("s", 9000)
+            if n == 6:
+                for ns, R, W, f in (
+                        (70, ["HT", "DL"], ["hd"], tt(z("hd"), z("HT"), z("DL"), OP.mult)),
+                        (60, ["HT", "EB0"], ["CAND"], tt(z("CAND"), z("HT", 4, 40, 5), z("EB", 16, 24), OP.mult)),
+                        (70, ["EB0", "JQ", "QB"], ["QB0"], tt(z("qa"), z("EB", 16, 64), z("JQ", 0, 48), OP.mult)),
+                        (190, ["DL", "hd"], ["d1"], tt(z("d1"), z("DL"), z("hd"), OP.subtract)),
+                        (10, ["CAND", DUM], ["N2"], tt(z("N2"), z("CAND"), z(DUM, 0, 8), OP.mult)),
+                        (190, ["HT", "d1"], ["FS"], scan(z("FS"), z("HT"), z("d1"), 0.0, OP.mult)),
+                        (10, ["N2", DUM], ["ND"], tt(z("ND"), z(DUM, 0, 8), z("N2"), OP.subtract)),
+                        (0, ["QB0", "QB"], ["QBa"], ts(z("QB", 16, 64), z("qa"), float(OD), OP.mult))):
+                    later("v", ns, V, R, W, f)
         nl = T.CL[:, i4 * 96:i4 * 96 + 8]
         nk = "c%d_0" % i4
-        V(["EB0", "EB1", "JQ", "QB"], ["QB1"], tt(z("QB", 16, 112), z("EB", 16, 112), z("JQ"), OP.mult))
-        PE(["EB0", "EB1", "EB", "QB", "QB1", "NLT", "NUT", "ID16", "NI16"], ["#LA"], *group(
-            (LA[:, 256:352], z("NLT"), z("EB", 16, 112)), (LA[:, 256:352], z("NUT"), z("EB", 15, 111)),
-            (LA[:, 256:352], z("ID16"), z("QB", 16, 112)), (LA[:, 256:352], z("NI16"), z("QB", 15, 111))))
-        marks_sum(1, rnd * SP + SP - 1)
-        s3a(1)
-        t2("hd", "HT", "DL", OP.mult)
-        V(["HT", "EB0"], ["CAND"], tt(z("CAND", 0, 8), z("HT", 4, 40, 5), z("EB", 16, 24), OP.mult),
-          tt(z("CAND", 8, 16), z("HT", 4, 40, 5), z("EB", 16, 24), OP.mult))
-        t2("d1", "DL", "hd", OP.subtract)
-        V(["#LA", "D1"], ["POSF"],
-          lambda e: e.tensor_tensor_scan(z("POSF"), LA[:, 256:352], z("D1"), 0.0, OP.add, OP.add))
-        V(["HT", "d1"], ["FS"], lambda e: e.tensor_tensor_scan(z("FS"), z("HT"), z("d1"), 0.0, OP.mult, OP.add))
-        V(["POSF"], ["POS"], cp(z("POS"), z("POSF")))
-        S(["LBB", "POS", "SW"], ["SW"], ac(T.SW[:, :].indirect(z("POS", 48, 96)), T.LBB[:, :], AF.Sigmoid))
-        V(["FS", "DL", DUM], ["KT"], tt(z("KT", 0, 8), z("FS", 3, 40, 5), z(DUM, 0, 8), OP.subtract),
-          tt(z("KT", 8, 16), z("DL", 4, 40, 5), z(DUM, 0, 8), OP.subtract))
-        t2("KT2", "KT", "CAND", OP.mult)
-        t2("KK", "KT2", DUM, OP.add)
+        spend("v", 9000)
+        stays(1)
+        tu = turned(1)
+        PE(["eb1", "TU"], ["#LB"], *(group(*tu[:2]) + group(*tu[2:])))
+        bound(1)
+        V(["FS", "DL", "ND"], ["KK"], tt(z("KK", 0, 8), z("FS", 3, 40, 5), z("ND"), OP.max), tt(z("KK", 8, 16), z("DL", 4, 40, 5), z("ND"), OP.max))
+        next_list(0, i4, rnd, lambda: None)
         V(["KK"], ["FK"], cp(z("FK"), z("KK")))
+        V(["#LB", "JQ", "QB"], ["QB1"], tt(z("QB", 64, 112), LB[:, 320:368], z("JQ", 48, 96), OP.mult))
+        S(["#LB", "EB"], ["EB1"], ac(z("EB", 64, 112), LB[:, 320:368], AF.Copy, scale=1.0 / OD))
         V(AUXK + ["FK"], ["XF"], cp(z("XF"), T.AUX[:, :].indirect(z("FK"))))
-        V(LBK + ["POS", "VW"], ["VW"], cp(T.VW[:, :].indirect(z("POS", 0, 48)), T.LBA[:, 0:H]))
-        oh = LB[:, 256:384]
-        PE(["k0", "BID"], ["#LB"], mm(oh, z("BID"), cond[0][:, 0:128], True, True))
-        for h in (0, 1):
-            f = []
-            xf = z("XF", 128 * h, 128 * h + 128)
+        rk_ = LA[:, 416:512]
+        PE(["EB0", "EB1", "EB", "QB", "QBa", "QB1", "NLT", "NUT", "ID16", "NI16"], ["#LA"], *group(
+            (rk_, z("ID16"), z("QB", 16, 112)), (rk_, z("NI16"), z("QB", 15, 111)),
+            (rk_, z("NLT"), z("EB", 16, 112)), (rk_, z("NUT"), z("EB", 15, 111))))
+        compare(1)
+        V(["#LB", "C161"], ["xb"], tt(z("xb"), LB[:, 320:368], zs("C16", 1, 48), OP.add))
+        V(["#LA", "D1"], ["POSF"], scan(z("POSF"), rk_, z("D1"), 0.0, OP.add))
+        V(["xb"], ["XL1"], ts(zs("XL", 1, 48), z("xb"), 1024.0, OP.add))
+        V(["POSF"], ["POS"], cp(z("POS"), z("POSF")))
+
+        def pairs(h):
+            f, xf = [], z("XF", 128 * h, 128 * h + 128)
             for gg in range(8):
                 o = PX[h][:, 128 * gg:128 * gg + 128]
-                f += group((o, T.SELK[:, 128 * gg:128 * gg + 128], xf), (o, xf, T.NSELK[:, 128 * gg:128 * gg + 128]), (o, z("IDN"), z("TRI")))
-            PE(["XF", "IDN", "TRI", "SELK", "NSELK"], [PK[h]], *f)
+                f += group((o, T.SELK[:, 128 * gg:128 * gg + 128], xf), (o, xf, T.NSELK[:, 128 * gg:128 * gg + 128]))
+            PE(["XF", "SELK", "NSELK"], [PK[h]], *f)
+
+        def equal(h):
+            V([PK[h], "TRW"], ["EQ%d" % h], tt(T["EQ%d" % h][:, :], PX[h][:, :], T.TRW[:, :], OP.is_equal))
+        pairs(0)
+        oh = LA[:, 256:384]
+        PE(["k0", "BID"], ["#LA"], mm(oh, z("BID"), cond[0][:, 0:128], True, True))
+        marks_sum(1, k3)
+        pairs(1)
+        V(LBK + ["POS", "VW"], ["VW"], cp(T.VW[:, :].indirect(z("POS", 0, VS // 16)), T.LBA[:, 0:VS]))
+        S(["LBB", "POS", "SW"], ["SW"], ac(T.SW[:, :].indirect(z("POS", VS // 16, 96)), T.LBB[:, :], AF.Sigmoid))
         S(["SW"], ["SWb"], ac(z("SWb"), T.SW[:, 0:384], AF.Copy))
-        sl = LA[:, 352:376]
-        PE(["VW", "SWb", "cb%d" % CSA, "cb%d" % CSB], ["#LA"], *group(
+        sl = LB[:, 416:440]
+        PE(["VW", "SWb", "cb%d" % CSA, "cb%d" % CSB], ["#LB"], *group(
             *(combed(sl, CSA, lambda i, n, st: T.VW[:, i:n:st], 384) + combed(sl, CSB, lambda i, n, st: z("SWb", i, n, st), 384))))
-        marks(1, rnd * SP + SP - 1)
-        s3(1, rnd)
+        marks(1, k3)
+        equal(0)
+        V(TBK + ["FK"], ["hF"], ts(z("hF"), TB[:, :].indirect(z("FK", 0, 8)), -1.0, OP.mult, one, OP.add))
+        V(TBK + ["FK"], ["gF"], cp(z("gF"), TB[:, :].indirect(z("FK", 0, 8))))
         SND, RCV = T["SND%d" % rnd], T["RCV%d" % rnd]
         sk, rk = "SND%d" % rnd, "RCV%d" % rnd
-        V(["#LA"], ["LNE"], ts(z("LNE"), sl, 1536.0, OP.add))
+        V(["#LB"], ["LNE"], ts(z("LNE"), sl, 1536.0, OP.add))
         S(["A20", "A21", "A2z", "LNE"], [sk + "a"], ac(SND[:, 0:384], T.A2[:, :].indirect(z("LNE")), AF.Copy))
         if rnd == 0:
-            V(["#LA", sk + "z"], [sk + "b"], ts(SND[:, 400:424], sl, -0.5, OP.is_lt))
+            V(["#LB", sk + "z"], [sk + "b"], ts(SND[:, 385:432:2], sl, -0.5, OP.is_lt))
             V(["m0", "m1", "mz", "LNE"], [sk + "c"], cp(SND[:, 432:816], T.MM[:, 0:1552].indirect(z("LNE"))))
         do_waits("q", [sk + c for c in "azbc"[:2 if rnd else 4]], [])
         g.remote_dma(RCV[:, :], SND[:, :], T.sem["arr%d" % rnd], T.sem["snt%d" % rnd], pid, rid, rmask)
         used["snt%d" % rnd] = ne
         used["arr%d" % rnd] = ne
         record(("rem%d" % rnd, "arr%d" % rnd, ne, {}), [], [rk])
-        V(["#A"], ["EQF"], ts(T.EQF[:, :], T.PA[:, :], 0.0, OP.is_equal))
-        S(["#B"], ["ABD"], ac(T.ABD[:, :], T.PB[:, :], AF.Abs))
-        S(["ABD"], ["EQD"], ac(T.EQD[:, :], T.ABD[:, :], AF.Relu, bias=1.0, scale=-1.0))
-        s4(1, i4, rnd)
-        S(WTK + [nk], ["ug"], ac(z("ug"), T.WT[:, 0:2304].indirect(nl), AF.Identity, bias=128.3, scale=0.5))
 
-        def dup(h, EQ, ek):
-            o = LP[h][:, 384:512]
-            PE([ek, "OB", "XF", "CANDM"], [LK[h]], *group(
+        def dup(h):
+            o, EQ = PM[:, 128 * h:128 * h + 128], T["EQ%d" % h]
+            PE(["EQ%d" % h, "OB", "XF", "CANDM"], ["#M"], *group(
                 *([(o, z("OB", 112 - 16 * gg, 240 - 16 * gg), EQ[:, 128 * gg:128 * gg + 128]) for gg in range(8)]
                   + [(o, z("CANDM"), z("XF", 128 * h, 128 * h + 128))])))
 
         def winners(h):
-            V([LK[h]], ["AR%d" % h], ts(z("AR", 128 * h, 128 * h + 128), LP[h][:, 384:512], -0.5, OP.is_lt))
-            PE(["AR%d" % h, "cb%d" % C0], [LK[h]],
-               *group(*combed(LP[h][:, 240:248], C0, lambda i, n, st: z("AR", 128 * h + i, 128 * h + n, st), 128)))
+            V(["#M"], ["AR%d" % h], ts(zs("AR", h, 128), PM[:, 128 * h:128 * h + 128], 0.5, OP.is_gt))
 
-        def offsets(h, o1, o2, off):
-            V([LK[h], "KT2"], [o1], tt(z(o1), LP[h][:, 240:248], z("KT2", 8 * h, 8 * h + 8), OP.mult))
-            V([o1, DUM], [o2], tt(z(o2), z(o1), z(DUM, 0, 8), OP.add))
-            V([o2], [off], cp(z(off), z(o2)))
-        dup(0, T.EQF, "EQF")
-        tz("POG", "POSF", 384.0, OP.min)
-        if rnd == 0:
-            V(["#LA"], ["T1"], ts(z("T1"), sl, -0.5, OP.is_lt))
-            V(["#LA", "JL"], ["LNF"], tt(z("LNF"), sl, z("JL", 0, 24), OP.subtract))
-        winners(0)
-        V(["#LB", "AR0"], ["OA"], tt(z("OA"), oh, z("AR", 0, 128), OP.mult))
-        S(["OA"], ["nOA"], ac(z("nOA"), z("OA"), AF.Identity, bias=1.0, scale=-1.0))
-        scaled("OA2", "OA", 15.0 / 16, "OA")
-        if rnd == 0:
-            t2("PRE", "LNF", "T1", OP.mult)
-            tz("u2", "ug", -128.0625, OP.add, -TINY, OP.max)
-        else:
-            tz("u2", "ug", -128.0, OP.add)
-        wc = 2048 + 128 * rnd
-        V(["u2", "AR0"], ["WTn"], tt(T.WT[:, wc:wc + 128], z("u2"), z("AR", 0, 128), OP.mult))
-        offsets(0, "AO", "AO2", "OFF")
-        dup(1, T.EQD, "EQD")
-        V(WTK + ["OFF", "nOA"], ["tg"], tt(z("tg"), T.WT[:, :].indirect(z("OFF")), z("nOA"), OP.mult))
-        winners(1)
-        if rnd == 0:
-            S(AUXK + [nk], ["AFn"], ac(T.AUF[:, 2048:OD], T.AUX[:, 0:2048].indirect(nl), AF.Copy))
-            S(DTK + [nk], ["DTn"], ac(T.DT[:, OD + 2048:OD + OD], T.DT[:, OD:OD + 2048].indirect(nl), AF.Copy))
-            PE(["AFn", "cb%d" % CID], ["#B"], mm(T.PB[:, 0:128], comb(CID, 15), T.AUF[:, 2048:OD], True, True))
-            S(["#B", "X1"], ["DFn"], ac(T.DT[:, 2048:OD], T.PB[:, 0:128], AF.Copy))
-            for j in range(4):
-                plain_pointers(j)
-            targets(1)
-        V(["tg", "OA2", "OFF"], WTK, tt(T.WT[:, :].indirect(z("OFF")), z("tg"), z("OA2"), OP.add))
-        V(["#LB", "AR1"], ["OBm"], tt(z("OBm"), oh, z("AR", 128, 256), OP.mult))
-        offsets(1, "BO", "BO2", "OFD")
-        V(WTK + ["OFD", "OBm"], ["s1"], tt(z("s1"), T.WT[:, :].indirect(z("OFD")), z("OBm"), OP.add))
-        if rnd == 0:
-            tz("s2", "s1", 15.0, OP.min, 128.0, OP.add)
-            tz("s3", "s2", -128.0625, OP.add, -TINY, OP.max)
-        else:
-            tz("s3", "s1", 15.0, OP.min)
-        V(["s3", "OFD"], WTK, cp(T.WT[:, :].indirect(z("OFD")), z("s3")))
+        def keys(h):
+            V(["AR%d" % h, "XD%d" % h], ["ZW%d" % h], tt(zs("ZW", h, 128), zs("AR", h, 128), zs("XD", h, 128), OP.mult))
+            o = PM[:, 256 + 8 * h:264 + 8 * h]
+            PE(["ZW%d" % h, "cb%d" % CID, "ID16", "DU"], ["#M"], *group(
+                (o, z("ID16"), z("DU", 8 * rnd, 8 * rnd + 8)), *combed(o, CID, lambda i, n, st: z("ZW", 128 * h + i, 128 * h + n, st), 128)))
 
-        def new_pointers():
-            V(STK + ["OFF", "nOA"], ["tS"], tt(z("tS"), T.ST[:, :].indirect(z("OFF")), z("nOA"), OP.mult))
-            t2("qS", "OA", "WR", OP.mult)
-            o = T.PB[:, 0:128]
-            PE(["SH16", "tS", "qS"], ["#B"], *group((o, z("SH16"), z("tS")), (o, z("SH16"), z("qS"))))
-            S(["#B"], ["xs"], ac(z("xs"), o, AF.Copy))
-            tz("kk", "xs", M35, OP.add, -M35, OP.add)
-            V(["kk", "xs", "OFF"], DTK, tt(T.DT[:, OD:OD + NW].indirect(z("OFF")), z("xs"), z("kk"), OP.subtract))
-
-        def counts_out(a, b, q):
-            V(WTK, ["yn%d" % a], ts(T.YN[:, a:b], T.WT[:, a:b], M23, OP.add, -M23, OP.add))
-            dma(q, ["yn%d" % a], [], (T.yn[:, a:b], T.YN[:, a:b]))
+        def offsets(h):
+            V(["#M"], ["OF%d" % h], ts(z(("OFF", "OFD")[h]), PM[:, 256 + 8 * h:264 + 8 * h], 2048.0, OP.add))
 
         def landed(p, e):
             o, i = T.LW[:, H * p:H * p + H], RCV[:, 0:400].indirect(zs("POG", p, 48))
             op(e, [rk, "POG"], ["LW%d" % p], ac(o, i, AF.Copy) if e == "s" else cp(o, i))
 
-        def merged(P, pk, a, b, out, ok):
-            V([pk, "CLF0", "CLF1"], ["mx%d" % a], tt(z("mx", a, b), P, z("CLF", a, b), OP.max))
-            V(["mx%d" % a], ["rr%d" % (a // 48)], ts(z("rr", a, b), z("mx", a, b), 4096.0, OP.is_ge, 4096.0, OP.mult))
-            V(["mx%d" % a, "rr%d" % (a // 48)], [ok], tt(out, z("mx", a, b), z("rr", a, b), OP.subtract))
+        def shown_list(p, P):
+            PE(["LW%d" % p, "cb%d" % CLK], [LK[p]], *group(*combed(P, CLK, lambda i, n, st: T.LW[:, H * p + i:H * p + n:st], H)))
+
+        def next_targets(a, b):
+            if rnd == 0:
+                targets(1, T.PA, "#A", a, b)
+        dup(0)
+        next_targets(0, 2)
+        S(WTK + [nk], ["ug"], ac(z("ug"), T.WT[:, 0:2304].indirect(nl), AF.Identity, bias=128.3, scale=0.5))
         if rnd == 0:
-            new_pointers()
+            S(AUXK + [nk], ["AFn"], ac(T.AUF[:, 2048:OD], T.AUX[:, 0:2048].indirect(nl), AF.Copy))
+            S(DTK + [nk], ["DTn"], ac(T.DT[:, OD + 2048:OD + OD], T.DT[:, OD:OD + 2048].indirect(nl), AF.Copy))
+            later("v", 60, V, ["#LB"], ["T1"], ts(z("T1"), sl, -0.5, OP.is_lt))
+            later("v", 60, V, ["#LB", "JL"], ["LNF"], tt(z("LNF"), sl, z("JL", 0, 24), OP.subtract))
+            later("v", 200, V, ["LNF", "T1", "PJ"], ["PJ"], tt(z("PJ", 0, 48, 2), z("LNF"), z("T1"), OP.mult))
+        dm = T.AUX[:, 2304 + 128 * rnd:2432 + 128 * rnd]
+        if rnd:
+            equal(1)
+        V(["XF"] + AUXK, ["XD0"], tt(zs("XD", 0, 128), zs("XF", 0, 128), dm, OP.subtract))
+        winners(0)
+        V(["#LA", "hF"], ["hh"], tt(z("hh"), oh, z("hF"), OP.mult))
+        keys(0)
+        if rnd == 0:
+            equal(1)
+        else:
+            gather_next(1, rnd)
+        V(["AR0", "hh"], ["m1"], tt(z("m1"), zs("AR", 0, 128), z("hh"), OP.mult))
+        offsets(0)
+        dup(1)
+        next_targets(2, 5)
+        V(["XF"] + AUXK, ["XD1"], tt(zs("XD", 1, 128), zs("XF", 1, 128), dm, OP.subtract))
+        V(["gF", "m1", "OF0"], TBK, tt(TB[:, :].indirect(z("OFF")), z("gF"), z("m1"), OP.add))
+        if rnd == 0:
+            V(["#LA", "AR0"], ["OA"], tt(z("OA"), oh, zs("AR", 0, 128), OP.mult))
+            S(["OA"], ["nOA"], ac(z("nOA"), z("OA"), AF.Identity, bias=1.0, scale=-1.0))
+        gap()
+        winners(1)
+        gap()
+        V(["#LA", "AR1"], ["OBm"], tt(z("OBm"), oh, zs("AR", 1, 128), OP.mult))
+        keys(1)
+        if rnd:
+            next_list(1, i4, rnd, gap)
+        if rnd == 0:
+            tz("u2", "ug", -128.0625, OP.add, -TINY, OP.max)
+        else:
+            tz("u2", "ug", -128.0, OP.add)
+        V(TBK + ["FK", "OBm"], ["s1"], tt(z("s1"), TB[:, :].indirect(z("FK", 8, 16)), z("OBm"), OP.add))
+        if rnd == 0:
+            t2("qS", "OA", "WR", OP.mult)
+            tz("s2", "s1", 15.0, OP.min, 128.0, OP.add)
+            V(STK + ["FK", "nOA"], ["tS"], tt(z("tS"), T.ST[:, :].indirect(z("FK", 0, 8)), z("nOA"), OP.mult))
+            PE(["SH16", "tS", "qS", "AFn", "cb%d" % CID], ["#B"], *(group((T.PB[:, 0:128], z("SH16"), z("tS")), (T.PB[:, 0:128], z("SH16"), z("qS")))
+                                                                    + group((T.PB[:, 128:256], comb(CID, 15), T.AUF[:, 2048:OD]))))
+            S(["#B"], ["xs"], ac(z("xs"), T.PB[:, 0:128], AF.Copy))
+            tz("s3", "s2", -128.0625, OP.add, -TINY, OP.max)
+        else:
+            tz("POG", "POSF", 384.0, OP.min)
+            landed(0, "s")
+            tz("s3", "s1", 15.0, OP.min)
+        wc = 2048 + 128 * rnd
+        V(["u2", "AR0"], [TBn], tt(TB[:, wc:wc + 128], z("u2"), zs("AR", 0, 128), OP.mult))
+        offsets(1)
+        if rnd == 0:
+            gather_next(1, rnd)
+            next_targets(5, 8)
+        V(["s3", "OF1"], TBK, cp(TB[:, :].indirect(z("OFD")), z("s3")))
+        if rnd:
+            for a, q in ((0, "y"), (1152, "y")):
+                dma(q, YNK, [], (T.yn[:, a:a + 1152], T.YN[:, a:a + 1152]))
+
+        def merged(P, pk, a, b):
+            V([pk, "CLF0", "CLF1"], ["mx%d" % a], tt(z("mx", a, b), P, z("CLF", a, b), OP.max))
+            gap()
+            V(["mx%d" % a], ["cc%d" % a], ts(z("cc", a, b), z("mx", a, b), 4095, BA))
+            gap()
+        if rnd == 0:
+            S(["#B", "X1"], ["DFn"], ac(T.DT[:, 2048:OD], T.PB[:, 128:256], AF.Copy))
+            next_list(1, i4, rnd, gap)
+            tz("kk", "xs", M35, OP.add, -M35, OP.add)
+            tz("POG", "POSF", 384.0, OP.min)
+            V(["FS"], ["DL"], cp(z("DL", 0, 40, 5), z("FS", 4, 40, 5)))
+            V(["kk", "xs", "OF0"], DTK, tt(T.DT[:, OD:OD + NW].indirect(z("OFF")), z("xs"), z("kk"), OP.subtract))
             zeros()
             landed(0, "s")
+            targets_out(1, T.PA, "#A")
             landed(1, "s")
-            V([rk, "PRE"], ["RX1"], tt(z("RX1"), RCV[:, 400:424], z("PRE"), OP.mult))
-            t2("RX2", "RX1", "JD", OP.add)
-            V(["RX2"], ["TO"], cp(z("TO"), z("RX2")))
+            V([rk, "PJ"], ["TF"], scan(z("TF"), RCV[:, 384:432], z("PJ"), 0.0, OP.mult))
+            V(["TF"], ["TO"], cp(z("TO"), z("TF", 1, 48, 2)))
             V([rk, "TO", "m0", "m1", "mz"], ["m0", "m1", "mz"], cp(T.MM[:, :].indirect(z("TO")), RCV[:, 432:816]))
             for p in (0, 1):
-                P = LP[p][:, 192:240]
-                PE(["LW%d" % p, "cb%d" % CLK], [LK[p]], *group(*combed(P, CLK, lambda i, n, st: T.LW[:, H * p + i:H * p + n:st], H)))
+                shown_list(p, LP[p][:, 368:416])
 
             def hopped(p):
                 off, ck = lists(p, SP + 1)
-                merged(LP[p][:, 192:240], LK[p], 48 * p, 48 * p + 48, zs("cc", p, 48), "cc%d" % p)
-                V(["cc%d" % p], [ck], cp(off, zs("cc", p, 48)))
-                S(["cc%d" % p], ["C16%d" % p], ac(zs("C16", p, 48), zs("cc", p, 48), AF.Identity, bias=-1024.0))
+                V(["cc%d" % (48 * p)], [ck], cp(off, zs("cc", p, 48)))
+                V(["cc%d" % (48 * p)], ["C16%d" % p], ts(zs("C16", p, 48), zs("cc", p, 48), -1024.0, OP.add))
                 root(p)
-
-            def carried():
-                hopped(1)
-                V(["FS"], ["DL"], cp(z("DL", 0, 40, 5), z("FS", 4, 40, 5)))
-                V(["HF", "E8"], ["HT"], tt(z("HT", 1, 40, 5), z("E8"), z("HF"), OP.subtract))
+            merged(LA[:, 368:416], "#LA", 0, 48)
             hopped(0)
-            S(["#LA"], ["HF"], ac(z("HF"), LA[:, 192:200], AF.Sigmoid, bias=-2048.0))
-            fill[8] = [carried]
+            S(["#LA"], ["HF"], ac(z("HF"), LA[:, 368:376], AF.Sigmoid, bias=-2048.0))
+            later("v", 260, V, ["#LB", "CLF1"], ["mx48"], tt(z("mx", 48, 96), LB[:, 368:416], z("CLF", 48, 96), OP.max))
+            later("v", 60, V, ["HF", "E8"], ["HT"], tt(z("HT", 1, 40, 5), z("E8"), z("HF"), OP.subtract))
+            later("v", 260, V, ["mx48"], ["cc48"], ts(z("cc", 48, 96), z("mx", 48, 96), 4095, BA))
+            later("v", 120, hopped, 1)
+            for j in range(9):
+                later("v", 190, V, WTK, ["yn%d" % j], ts(T.YN[:, 256 * j:256 * j + 256], T.WT[:, 256 * j:256 * j + 256], M23, OP.add, -M23, OP.add))
         else:
-            counts_out(0, 1152, "s")
-            counts_out(1152, 2304, "y")
-            landed(0, "v")
-            landed(1, "s")
-            PE(["LW0", "LW1", "cb%d" % CLK], ["#LB"], *group(*combed(LB[:, 0:96], CLK, lambda i, n, st: T.LW[:, i:n:st], 1536)))
-            merged(LB[:, 0:96], "#LB", 0, 96, z("YC"), "YC")
-            dma("y", ["YC"], [], (T.yc[:, :], z("YC")))
+            landed(1, "v")
+            for p in (0, 1):
+                shown_list(p, LP[p][:, 448:496])
+            for p in (0, 1):
+                V([LK[p], "CLF%d" % p], ["mx%d" % p], tt(zs("mx", p, 48), LP[p][:, 448:496], zs("CLF", p, 48), OP.max))
+            V(["mx0", "mx1"], ["cc0"], ts(z("cc"), z("mx"), 4095, BA))
+            V(["cc0"], ["YC"], cp(z("YC"), z("cc")))
+            dma("s", ["YC"], [], (T.yc[:, :], z("YC")))
 
     for q in ("v", "s", "t", "q"):
         g.wait_ge(T.sem[q], cnt[q])

@@ -6,7 +6,7 @@ RO, SP = 2, 4
 NW = 2560
 OD = 2176
 H = 768
-VS = 896
+OW = NW
 B0 = 1280.0
 TINY = 2.0 ** -20
 M23, M35 = 1.5 * 2 ** 23, 1.5 * 2 ** 35
@@ -16,7 +16,7 @@ TURN = [("lo", 8 * r, (r, 2), (0, 32)) for r in range(2)] + [("q2", 4 * r - 8, (
 BACK = [("lo", 0), ("hi", -8), ("q0", 8), ("q1", 4), ("q2", 0), ("q3", -4)]
 MASKS = {"lo": (0, 8), "hi": (8, 16), "q0": (0, 4), "q1": (4, 8), "q2": (8, 12), "q3": (12, 16)}
 C1, C0, CID, CLK, CSA, CSB = range(6)
-WEIGHTS = {CID: {4: -1024 - 4128, 7: 32, 8: 1}, CLK: {2: 32, 3: 1, 4: -32}, CSA: {15: -1536}, CSB: {15: VS - 1536}}
+WEIGHTS = {CID: {4: -1024 - 4128, 7: 32, 8: 1}, CLK: {2: 32, 3: 1, 4: 2 * OW - 4128}, CSA: {15: -1536}, CSB: {15: H - 1536}}
 SCRATCH = {}
 WHERE = {}
 
@@ -35,22 +35,22 @@ def pool(buf, dtype, **kw):
 
 
 sb(I32, tabI=2048, CI=2048, CPI=416, CPL=288, BI=640)
-sb(F32, YB=2048, ST=NW, DT=OD + NW, LBB=1536 - VS, SW=4352)
-sb(B16, WT=NW, AUX=NW, AUF=OD, VV=12288, VL=1024, w0=H, w1=H, k0=H, k1=H, MM=1920, YN=NW, BB=640, LBA=1024,
-   VW=4864, A2=1552, SND0=816, SND1=400, RCV0=816, RCV1=400, LW=1536, SELK=1024, NSELK=1024, TRW=1024, EQ0=1024, EQ1=1024,
+sb(F32, YB=2048, ST=NW, DT=OD + NW, LBB=H, SW=4608)
+sb(B16, WT=3 * NW, AUX=NW, AUF=OD, VV=12288, VL=1024, w0=H, w1=H, k0=H, k1=H, MM=1920, YN=NW, BB=640, LBA=1024,
+   VW=4608, A2=1552, SND0=816, SND1=400, RCV0=816, RCV1=400, LW=1536, SELK=1024, NSELK=1024, TRW=1024, EQ0=1024, EQ1=1024,
    COMB=864)
 sb(F16, X0=H, X1=H, COMBX=144, SH=2048, BC=1536, FB=2048, TU=960)
 sb(U16, CL=960)
-pool("zi", I32, CXI=96, i_rm=16, i_pc=16, i_g8=8, i_bm=128, i_dp=160, i_sf=144, i_wr=128, i_jc=64, mx=96, cc=96)
+pool("zi", I32, CXI=96, i_rm=16, i_pc=16, i_g8=8, i_bm=128, i_dp=160, i_sf=144, i_wr=128, i_jc=64)
 pool("zf", F32, RM=16, PC=1, G8=8, JI=96, JL=96, JQ=96, DUM0=16, DUM1=16, CLF=96, YC=96, HT=40, FC=128,
      DL=40, hd=40, d1=40, FS=40, KK=16, CAND=8, ND=8, N2=8, D1=96, POSF=96, PJ=48, TF=48, E8=8, MK=8, KB=1, CB=1,
-     LNF=24, T1=24, HF=8, xs=128, kk=128, ZF=384, rr=96, xb=48, qa=48, W16=64, WM=64, WC=4, TWO=16, Z16=16)
-pool("zb", B16, BM=128, IDN=128, NLT=128, NUT=128, N16=128, TRI=128, CANDM=128, BID=128, U1=128, U2=128, LTu=128, LTB=128,
+     LNF=24, T1=24, HF=8, xs=128, kk=128, ZF=384, rr=96, xb=48, mx=96, k1=128, XW=96, W16=64, WM=64, WC=4, TWO=16, Z16=16)
+pool("zb", B16, BM=128, IDN=128, NLT=128, NUT=128, N16=128, NI=128, JW=96, CANDM=128, BID=128, U1=128, U2=128, LTu=128, LTB=128,
      SELV=144, OB=240, SWb=384, EB=112, HB=288, LB=288, XF=256, XD=256, ZW=256, AR=256, OA=128, nOA=128, OBm=128, gF=128,
      hF=128, hh=128, m1=128, s1=128, s2=128, s3=128, ug=128, u2=128, ZB=384)
-pool("zh", F16, SH16=128, ID16=128, NI16=128, IDW=160, SELH=144, WR=128, tS=128, qS=128, QB=112, C16=96, RT=96, D0=512,
+pool("zh", F16, SH16=128, ID16=128, NI16=128, IDW=160, SELH=144, WR=128, tS=128, qS=128, QB=112, C4=96, RT=96, D0=512,
      SC=512, eb=128, FH=128, DU=16)
-pool("zu", U16, POS=96, POG=96, LNE=24, TO=24, FK=16, OFF=8, OFD=8, XL=96, FL=128)
+pool("zu", U16, POS=96, POG=96, LNE=24, TO=24, FK=16, OFF=8, OFD=8, XL=96, FL=128, CC=96, NL=8)
 for nm, nc in (("PA", 1024), ("PB", 1024), ("PM", 1024), ("LA", 512), ("LB", 512)):
     SCRATCH[nm] = ("psum", [128, nc], F32)
 
@@ -168,6 +168,7 @@ def rank_program(g, core, T, topo):
         V([a, b], [out], tt(z(out), z(a), z(b), o))
 
     PX, LP, PK, LK = [T.PA, T.PB], [T.LA, T.LB], ["#A", "#B"], ["#LA", "#LB"]
+    MK, BK = ["#M", "#N"], [["#A", "#A1"], ["#B", "#B1"]]
     LA, LB, PM = T.LA, T.LB, T.PM
     w, cond, X = ([T["%s%d" % (a, p)] for p in (0, 1)] for a in ("w", "k", "X"))
     AUXK = ["AUX"] + ["ar%d" % i for i in range(6)]
@@ -188,6 +189,12 @@ def rank_program(g, core, T, topo):
     def zs(name, p, n=64, a=0, st=1):
         return z(name, n * p + a, n * p + n, st)
 
+    def wt(a, b):
+        return T.WT[:, OW + a:OW + b]
+
+    def cm(p, n=48):
+        return z("C4", 48 * p, 48 * p + n)
+
     spare = {"v": [], "s": []}
 
     def later(q, ns, f, *a):
@@ -202,10 +209,10 @@ def rank_program(g, core, T, topo):
     def tab_load(k, q):
         dma(q, [], ["tab%d" % k], (T.tabI[:, 512 * k:512 * k + 512], T.tab[:, 512 * k:512 * k + 512]))
     tab_load(0, "s")
-    dma("y", [], ["CXI"], (z("CXI"), T.cx[:, :]))
-    tab_load(1, "y")
-    dma("s", [], ["vv0"], (T.VV[0:8, 0:6144], T.vv[:, 0:6144]))
     dma("y", [], ["cpF"], (T.CPI[:, 288:416], T.suf[:, :]))
+    dma("s", [], ["vv0"], (T.VV[0:8, 0:6144], T.vv[:, 0:6144]))
+    tab_load(1, "y")
+    dma("y", [], ["CXI"], (z("CXI"), T.cx[:, :]))
     tab_load(2, "s")
     tab_load(3, "y")
     dma("y", [], ["cpL"], (T.CPI[:, 0:128], T.lnk[:, :]))
@@ -229,13 +236,26 @@ def rank_program(g, core, T, topo):
     iota(z("i_jc"), "i_jc", [[1, 64]], 0, 64)
     iota(z("JI"), "JI", [[16, 96]], 0, 0, **fl)
     iota(z("i_wr"), "i_wr", [[1, 128]], 0, 0)
-    iota(T.LBA[:, :], "LBA", [[0, 1024]], 1, 0, **fl)
-    iota(z("ZB"), "ZB", [[0, 384]], 0, 0, **fl)
-    iota(z("ZF"), "ZF", [[0, 384]], 0, 0, **fl)
+
+    def fill(tile, key, n, c):
+        iota(tile, key, [[0, n]], c, 0, **fl)
+    for name, c in (("DL", 0), ("HT", 0), ("W16", 0), ("TWO", 2), ("Z16", 0)):
+        fill(z(name), name, WHERE[name][2], c)
+    for j, wts in enumerate(WEIGHTS.values()):
+        for r, c in wts.items():
+            fill(z("W16", 16 * j + r, 16 * j + r + 1), "W16", 1, c)
+    fill(T.LBA[:, :], "LBA", 1024, 1)
+    for i in range(6):
+        iota(T.BB[:, 64 * i:64 * i + 64], "bb%d" % i, [[0, 32 >> i], [1, 2], [0, 1 << i]], 0, 0, **fl)
+    for name, c in (("ZB", 0), ("ZF", 0), ("D1", 16), ("OB", 0)):
+        fill(z(name), name, WHERE[name][2], c)
+    for tile, key, n, c in ((z("EB", 0, 16), "EB", 16, 0), (T.A2[:, 1536:1552], "A2z", 16, 0), (T.MM[:, 1536:1552], "mz", 16, 0),
+                            (T.SND0[:, 384:432], "SND0z", 48, 0), (T.SND1[:, 384:400], "SND1z", 16, 0), (z("OB", 112, 128), "OB", 16, -1)):
+        fill(tile, key, n, c)
     for tile, sg in (("SELK", 1.0), ("NSELK", -1.0)):
         iota(T[tile][:, :], tile, [[0, 1024]], 0, 0, **fl)
-        for r, wt in ((7, 32.0), (8, 1.0)):
-            select(tile, [[-16, 8], [0, 128]], OP.not_equal, sg * wt, -r, 1)
+        for r, c in ((7, 32.0), (8, 1.0)):
+            select(tile, [[-16, 8], [0, 128]], OP.not_equal, sg * c, -r, 1)
     iota(T.TRW[:, :], "TRW", [[0, 1024]], 0, 0, **fl)
     select("TRW", [[0, 8], [1, 128]], OP.is_gt, 8192.0, 0, -1)
     iota(T.ST[:, 2048:NW], "STz", [[0, 512]], 0, 0, **fl)
@@ -253,7 +273,7 @@ def rank_program(g, core, T, topo):
     V(["RM"], ["CB"], tt(z("CB"), RMc(4), RMc(9), OP.add))
     tz("G8", "i_g8", 0.0, OP.is_equal)
     tz("BM", "i_bm", 0.0, OP.is_equal)
-    for name, c, o in (("U1", -1.0, OP.is_equal), ("IDN", 0.0, OP.is_equal), ("LTu", 0.0, OP.is_ge), ("ID16", 0.0, OP.is_equal)):
+    for name, c, o in (("U1", -1.0, OP.is_equal), ("IDN", 0.0, OP.is_equal), ("LTu", 0.0, OP.is_ge)):
         V(["i_dp"], [name], ts(z(name), dp, c, o))
     tz("SELV", "i_sf", 0.0, OP.is_equal, 1.0 / 16, OP.mult)
     t2("U1", "U1", "BM", OP.mult)
@@ -264,22 +284,25 @@ def rank_program(g, core, T, topo):
     t2("LTB", "LTu", "BM", OP.mult)
     V(["RM"], ["MK"], *[rowsum(z("MK", j, j + 1), z("RM", a, b)) for j, (a, b) in enumerate(MASKS.values())])
 
-    def scan_constants():
-        V([], ["D00", "D01"], ms(z("D0", 0, 512, 4), 0.0), ms(z("D0", 2, 512, 4), 1.0))
-        for p in (0, 1):
-            V([LK[p]], ["D1%d" % p], ms(LP[p][:, 0:256:4], 1.0625), ms(LP[p][:, 1:256:4], -1.0625 * B0),
-              ms(LP[p][:, 3:256:4], B0 - 255.0 / 512))
-    V([], ["WTz"], ms(T.WT[:, 2048:NW], 0.0))
+    tz("SELH", "i_sf", 0.0, OP.is_equal)
+
+    def const(out, n, c):
+        return ac(out, w[0][:, 0:n], AF.Identity, bias=c)
+    S(["w0"], ["D00", "D01", "WTz"], const(z("D0", 0, 512, 4), 128, 0.0), const(z("D0", 2, 512, 4), 128, 1.0), const(wt(2048, NW), 512, 0.0))
+    for p in (0, 1):
+        S(["w0", LK[p]], ["D1%d" % p], const(LP[p][:, 0:256:4], 64, 1.0625), const(LP[p][:, 1:256:4], 64, -1.0625 * B0),
+          const(LP[p][:, 3:256:4], 64, B0 - 255.0 / 512))
 
     def scaled(out, a, col, key):
         S([a, key], [out], ac(z(out), z(a), AF.Copy, scale=col))
 
     def root(p):
-        S(["C16%d" % p], ["RT%d" % p], ac(zs("RT", p, 48), zs("C16", p, 48), AF.Sigmoid, bias=-256 * 1023.5, scale=-256.0))
+        S(["C%d" % p], ["RT%d" % p], ac(zs("RT", p, 48), cm(p), AF.Sigmoid, bias=-256 * 1023.5, scale=-256.0))
 
     S(["RM"], ["KB"], ac(z("KB"), RMc(15), AF.Identity, bias=4096 * B0 - 128, scale=1e9))
-    S(["w0", "CB", "RM"], ["AUX"], *([ac(T.AUX[:, a:a + H], w[0][:, :], AF.Identity, bias=z("CB")) for a in range(0, 2304, H)]
-                                     + [ac(T.AUX[:, 2304:NW], w[0][:, 0:256], AF.Identity, bias=RMc(4))]))
+    S(["IDN"], ["ID16"], ac(z("ID16"), z("IDN"), AF.Sigmoid, bias=-128.0, scale=256.0))
+    S(["w0", "CB", "RM"], ["AUX"], *([const(T.AUX[:, a:a + H], H, z("CB")) for a in range(0, 2304, H)]
+                                     + [const(T.AUX[:, 2304:NW], 256, RMc(4))]))
 
     def targets(rnd, P, pk, h0, h1):
         o = WHERE["SELV"][1]
@@ -294,7 +317,7 @@ def rank_program(g, core, T, topo):
     def counts(k):
         a, b = 512 * k, 512 * k + 512
         V(["tab%d" % k], ["ci%d" % k], ts(T.CI[:, a:b], T.tabI[:, a:b], 15, BA))
-        return lambda: V(["ci%d" % k], ["wt%d" % k], ts(T.WT[:, a:b], T.CI[:, a:b], -1.0 / 16, OP.add, -TINY, OP.max))
+        return lambda: V(["ci%d" % k], ["wt%d" % k], ts(wt(a, b), T.CI[:, a:b], -1.0 / 16, OP.add, -TINY, OP.max))
 
     def pointers(k):
         a, b = 512 * k, 512 * k + 512
@@ -307,22 +330,22 @@ def rank_program(g, core, T, topo):
         PE(["sh%d" % k, "SH16"], [pk], mm(P[:, 0:512], z("SH16"), T.SH[:, a:b], True, True))
         S([pk], ["dt%d" % k], ac(T.DT[:, OD + a:OD + b], P[:, 0:512], AF.Copy))
     rest = counts(0)
-    V(["CXI"], ["C160", "C161"], ts(z("C16"), z("CXI"), -1024.0, OP.add))
-    V(["CXI"], ["c0_0", "c0_1"], cp(T.CL[:, 0:96], z("CXI")))
+    V(["cpF"], ["FH"], cp(z("FH"), T.CPI[:, 288:416]))
+    V(["cpF"], ["FC"], ts(z("FC"), T.CPI[:, 288:416], -1024.0, OP.add))
+    dma("y", ["FH"], ["FB"], (T.FB[0:8, :], z("FH")))
+    dma("y", ["FC", "DF"], ["DF"], (T.DT[15:128:16, 0:2048], z("FC")))
     rest()
-    root(0)
-    root(1)
     pointers(0)
     V(["IDW", "MK"], ["TU"], *[ts(T.TU[:, 160 * j:160 * j + 160], z("IDW"), z("MK", j, j + 1), OP.mult) for j in range(6)])
     rest = counts(1)
     pointers(1)
     rest()
+    V(["CXI"], ["C0", "C1"], ts(z("C4"), z("CXI"), -1024.0, OP.add))
+    V(["CXI"], ["c0_0", "c0_1"], cp(T.CL[:, 0:96], z("CXI")))
+    root(0)
+    root(1)
     scaled("NLT", "LTB", -1.0, "LTB")
     scaled("N16", "IDN", -1.0 / 16, "IDN")
-    V(["cpF"], ["FC"], ts(z("FC"), T.CPI[:, 288:416], -1024.0, OP.add))
-    V(["cpF"], ["FH"], cp(z("FH"), T.CPI[:, 288:416]))
-    dma("y", ["FC", "DF"], ["DF"], (T.DT[15:128:16, 0:2048], z("FC")))
-    dma("y", ["FH"], ["FB"], (T.FB[0:8, :], z("FH")))
     targets(0, PM, "#M", 0, 8)
     differences(0)
     differences(1)
@@ -331,8 +354,10 @@ def rank_program(g, core, T, topo):
     pointers(2)
     rest()
     differences(2)
+    o = WHERE["SELH"][1]
+    PE(["FB", "SELH"], ["#N"], *group(*[(PM[:, 640:768], T.zh[0:8, o + 15 - i:o + 143 - i], T.FB[0:8, i:2048:16]) for i in range(16)]))
     rest = counts(3)
-    scan_constants()
+    V(["BM", "RM"], ["BC0"], *[ts(T.BC[:, 128 * a:128 * a + 128], z("BM"), RMc(a), OP.mult) for a in range(3)])
     rest()
     WTK = ["WT", "WTz", "WTn"] + ["wt%d" % k for k in range(4)]
     YNK = ["YN", "YNz", "YNn"] + ["yn%d" % k for k in range(9)]
@@ -343,17 +368,10 @@ def rank_program(g, core, T, topo):
 
     def first_gap():
         V(["tab3"], ["yb3"], ts(T.YB[:, 1536:2048], T.tabI[:, 1536:2048], -7.5, OP.add, 201326592.0, OP.add))
-        V(["BM", "RM"], ["BC"], *[ts(T.BC[:, 128 * a:128 * a + 128], z("BM"), RMc(a), OP.mult) for a in range(12)])
-        tz("SELH", "i_sf", 0.0, OP.is_equal)
+        V(["BM", "RM", "BC0"], ["BC"], *[ts(T.BC[:, 128 * a:128 * a + 128], z("BM"), RMc(a), OP.mult) for a in range(3, 12)])
 
-    def last_differences():
+    def last_pointers():
         S(["yb3"], ["sh3"], ac(T.SH[:, 1536:2048], T.YB[:, 1536:2048], AF.Identity, bias=-12583936.0, scale=0.0625))
-        differences(3)
-
-    def suffix_list():
-        o = WHERE["SELH"][1]
-        PE(["FB", "SELH"], ["#M"], *group(*[(PM[:, 512:640], T.zh[0:8, o + 15 - i:o + 143 - i], T.FB[0:8, i:2048:16]) for i in range(16)]))
-        V(["#M"], ["FL"], cp(z("FL"), PM[:, 512:640]))
 
     def zeros():
         dma("y", ["ZB", "VW"], ["VW"], (T.VW[:, 0:384], z("ZB")))
@@ -370,52 +388,38 @@ def rank_program(g, core, T, topo):
 
     def lane_bits():
         for i in range(10):
-            dma("y", ["BB%d" % (i // 5), "LBA"], ["lb%d" % i], (T.LBA[i:128:16, :], T.BB[:, 64 * i:64 * i + 64]))
+            dma("y", ["BB1" if i > 5 else "bb%d" % i, "LBA"], ["lb%d" % i], (T.LBA[i:128:16, :], T.BB[:, 64 * i:64 * i + 64]))
 
-    def fills(key, *pairs):
-        V([key], [key], *[ms(a, c) for a, c in pairs])
     for ns, R, W, f in (
+            (60, ["i_pc"], ["i_pc"], ts(z("i_pc"), z("i_pc"), 15, BA)),
             (110, ["cpj"], ["cpj"], ts(T.CPI[:, 128:256], T.CPI[:, 128:256], 2047, BA)),
             (60, ["cpk"], ["cpk"], ts(T.CPI[:, 256:288], T.CPI[:, 256:288], 511, BA)),
-            (60, ["i_pc"], ["i_pc"], ts(z("i_pc"), z("i_pc"), 15, BA)),
-            (60, ["i_jc"], ["i_jc"], ts(z("i_jc"), z("i_jc"), 1023, BA)),
-            (60, [], ["DL"], ms(z("DL"), 0.0)),
-            (60, [], ["HT"], ms(z("HT"), 0.0)),
+            (60, ["i_pc"], ["PC"], cp(z("PC"), z("i_pc", 0, 1))),
             (240, ["cpL", "cpj", "cpk"], ["cpl"], ts(T.CPL[:, :], T.CPI[:, 0:288], 31, BA)),
             (220, ["cpL", "cpj"], ["HBa"], ts(z("HB", 0, 256), T.CPI[:, 0:256], 1.0 / 32, OP.mult, b32, OP.add)),
             (60, ["cpk"], ["HBb"], ts(z("HB", 256, 288), T.CPI[:, 256:288], 1.0 / 32, OP.mult, b32 + 64.0, OP.add)),
-            (60, ["i_pc"], ["PC"], cp(z("PC"), z("i_pc", 0, 1))),
             (240, ["cpl"], ["LB"], cp(z("LB"), T.CPL[:, :]))):
         later("v", ns, V, R, W, f)
     later("v", 0, aux_rows)
-    for i in range(10):
-        later("v", 60, V, ["i_jc"], ["BI%d" % i], ts(T.BI[:, 64 * i:64 * i + 64], z("i_jc"), i, SR, 1, BA))
-    later("v", 180, lambda: (V([], ["W16"], ms(z("W16"), 0.0)), V([], ["TWO"], ms(z("TWO"), 2.0)), V([], ["Z16"], ms(z("Z16"), 0.0))))
-    for j in range(2):
-        later("v", 270, V, ["BI%d" % i for i in range(5 * j, 5 * j + 5)], ["BB%d" % j],
-              cp(T.BB[:, 320 * j:320 * j + 320], T.BI[:, 320 * j:320 * j + 320]))
-    later("v", 0, lane_bits)
+    for i in range(4):
+        later("v", 60, V, ["i_jc"], ["BI%d" % i], ts(T.BI[:, 64 * i:64 * i + 64], z("i_jc"), 6 + i, SR, 1, BA))
     for j in (2, 3):
         later("v", 60, V, ["W16", "TWO", "Z16"], ["W%d" % j], scan(z("W16", 16 * j, 16 * j + 10), z("TWO", 0, 10), z("Z16", 0, 10), 0.5, OP.mult))
-    for j, wts in enumerate(WEIGHTS.values()):
-        later("v", 60 * len(wts), V, ["W16"], ["Wr%d" % j], *[ms(z("W16", 16 * j + r, 16 * j + r + 1), float(c)) for r, c in wts.items()])
-    later("v", 100, V, [], ["OB"], ms(z("OB"), 0.0))
-    later("v", 120, lambda: (V([], ["EB"], ms(z("EB", 0, 16), 0.0)), V([], ["QB"], ms(z("QB", 0, 16), 0.0))))
+    later("v", 220, V, ["BI%d" % i for i in range(4)], ["BB1"], cp(T.BB[:, 384:640], T.BI[:, 0:256]))
+    later("v", 0, lane_bits)
     for j in range(4):
-        later("v", 60, V, ["RM", "W2", "W3", "Wr%d" % j], ["WM%d" % j], tt(z("WM", 16 * j, 16 * j + 16), z("W16", 16 * j, 16 * j + 16), z("RM"), OP.mult))
-    later("v", 80, V, [], ["D1"], ms(z("D1"), 16.0))
-    later("v", 120, lambda: (V([], ["A2z"], ms(T.A2[:, 1536:1552], 0.0)), V([], ["mz"], ms(T.MM[:, 1536:1552], 0.0))))
+        later("v", 60, V, ["RM", "W2", "W3", "W16"], ["WM%d" % j], tt(z("WM", 16 * j, 16 * j + 16), z("W16", 16 * j, 16 * j + 16), z("RM"), OP.mult))
+    later("v", 60, V, [], ["QB"], ms(z("QB", 0, 16), 0.0))
+    later("v", 200, t2, "NUT", "LTB", "BM", OP.subtract)
     for j in range(4):
         later("v", 60, V, ["WM%d" % j], ["WC%d" % j], rowsum(z("WC", j, j + 1), z("WM", 16 * j, 16 * j + 16)))
-    later("v", 120, lambda: (V([], ["SND0z"], ms(T.SND0[:, 384:432], 0.0)), V([], ["SND1z"], ms(T.SND1[:, 384:400], 0.0))))
-    later("v", 120, lambda: (fills("OB", (z("OB", 112, 128), -1.0)), V(["PC", "D1"], ["D1"], cp(z("D1", 0, 1), z("PC")))))
+    later("v", 60, V, ["PC", "D1"], ["D1"], cp(z("D1", 0, 1), z("PC")))
+    later("v", 110, V, ["i_dp"], ["U2"], ts(z("U2"), dp, 1.0, OP.is_equal))
     for j, v in enumerate(WEIGHTS):
         later("v", 60, V, ["WC%d" % j, "G8", "COMB"], ["cb%d" % v], ts(T.COMB[:, v * 144 + 15:v * 144 + 143:16], z("G8"), z("WC", j, j + 1), OP.mult))
-    later("v", 110, V, ["i_dp"], ["U2"], ts(z("U2"), dp, 1.0, OP.is_equal))
+    later("v", 200, t2, "U2", "U2", "BM", OP.mult)
     later("v", 110, tz, "WR", "i_wr", 1024.0, OP.add)
-    later("v", 220, t2, "NUT", "LTB", "BM", OP.subtract)
-    later("v", 220, t2, "U2", "U2", "BM", OP.mult)
-    later("v", 220, t2, "BID", "IDN", "U2", OP.subtract)
+    later("v", 200, t2, "BID", "IDN", "U2", OP.subtract)
 
     def shifted(out, a, na, c, o=0, scale=1.0, st=1):
         S([a, "PC"], [out], ac(z(out, o, o + na * st, st), z(a, 0, na), AF.Identity, bias=c, scale=scale))
@@ -428,19 +432,18 @@ def rank_program(g, core, T, topo):
         S(AUXK + ["FL"], ["af%d" % k], ac(T.AUF[:, 256 * k:256 * k + 256], T.AUX[:, 0:2048].indirect(z("FL", 16 * k, 16 * k + 16)), AF.Copy))
     later("s", 80, shifted, "JL", "JI", 96, z("PC"))
     later("s", 110, scaled, "NI16", "IDN", -1.0, "IDN")
+    later("s", 110, scaled, "NI", "IDN", -1.0, "IDN")
     later("s", 110, scaled, "CANDM", "BM", RMc(9), "RM")
     later("s", 60, S, ["RM", "G8", "COMB"], ["cb%d" % C0], ac(T.COMB[:, C0 * 144 + 15:C0 * 144 + 143:16], z("G8"), AF.Copy, scale=RMc(0)))
-    later("s", 60, shifted, "JQ", "JL", VS // 16, 1536.0 / OD, 0, 2.0 / OD)
+    later("s", 60, shifted, "JQ", "JL", 48, 1536.0, 0, 2.0)
     later("s", 60, shifted, "PJ", "JL", 24, 1536.0, 1, 1.0, 2)
     later("s", 60, shifted, "DUM0", "JL", 8, 2304.0)
     later("s", 60, shifted, "DUM1", "JL", 8, 2432.0)
-    later("s", 60, shifted, "JQ", "JL", 96 - VS // 16, 1536.0 / OD, VS // 16, 2.0 / OD)
+    later("s", 60, shifted, "JQ", "JL", 48, 1536.0 / OD, 48, 2.0 / OD)
     later("s", 60, shifted, "DU", "JL", 16, 256.0)
-    for k in range(4):
-        later("s", 430, plain_pointers, k)
     for k in range(8):
-        later("s", 300, suffix_aux, k)
-    later("s", 900, S, LBK, ["LBB"], ac(T.LBB[:, :], T.LBA[:, 0:1536 - VS], AF.Identity, bias=-200.0, scale=400.0))
+        later("s", 400, suffix_aux, k)
+    later("s", 700, S, LBK, ["LBB"], ac(T.LBB[:, :], T.LBA[:, 0:H], AF.Identity, bias=-200.0, scale=400.0))
 
     def lists(p, idx):
         return T.CL[:, idx * 96 + 48 * p:idx * 96 + 48 * p + 48], "c%d_%d" % (idx, p)
@@ -451,91 +454,120 @@ def rank_program(g, core, T, topo):
     def spread(P, src):
         return [mm(P[:, c0:c1:st], T.BC[:, 128 * a:128 * a + 128], src, False, a in (7, 11)) for a, (c0, c1, st) in enumerate(ROWS)]
 
-    def gather_counts(p, idx, k):
-        off, ck = lists(p, idx)
-        wi = T.WT[:, 0:2304].indirect(off)
-        if k:
-            V(WTK + [ck, "m%d" % p], ["w%d" % p], tt(w[p][:, :], wi, T.MM[:, H * p:H * p + H], OP.mult))
-        else:
-            op("vs"[p], WTK + [ck], ["w%d" % p], ac(w[p][:, :], wi, AF.Copy) if p else cp(w[p][:, :], wi))
+    PART = ((0, 512), (512, H))
 
-    def sums(p, k):
-        L, sp = LP[p], str(p)
-        S(["VL%d" % (k // SP)], ["D0v" + sp], ac(zs("D0", p, 256, 3, 4), T.VL[:, 128 * k + 64 * p:128 * k + 64 * p + 64], AF.Copy))
-        PE(["w" + sp, "cb%d" % C1], [LK[p]],
-           *group(*[(L[:, 2:256:4], comb(C1, a), w[p][:, c0:c1:st]) for a, (c0, c1, st) in enumerate(ROWS)]))
-        S([LK[p]], ["D0a" + sp], ac(zs("D0", p, 256, 1, 4), L[:, 2:256:4], AF.Identity, bias=B0 + 0.48, scale=-1.003))
-        PE(["w" + sp, "NLT"], [PK[p]], *halves(PX[p], z("NLT"), w[p]))
-        PE(["D0a" + sp, "ID16"], [PK[1 - p]], mm(PX[1 - p][:, H:H + 64], z("ID16"), zs("D0", p, 256, 1, 4), False, True))
+    def both(key, p):
+        return ["%s%d0" % (key, p), "%s%d1" % (key, p)]
+
+    def gather_counts(p, idx, k, part):
+        a, b = PART[part]
+        off, ck = T.CL[:, idx * 96 + 48 * p + a // 16:idx * 96 + 48 * p + b // 16], "c%d_%d" % (idx, p)
+        wi = (wt(0, 2304) if k <= SP else T.WT[:, 0:2 * OW + OD]).indirect(off)
+        W = ["w%d%d" % (p, part)]
+        if k:
+            V(WTK + (["WTl"] + ["WTh%d" % j for j in range(4)]) * (k > SP) + [ck, "m%d" % p], W, tt(w[p][:, a:b], wi, T.MM[:, H * p + a:H * p + b], OP.mult))
+        else:
+            op("vs"[p], WTK + [ck, "AUX"], W, ac(w[p][:, a:b], wi, AF.Copy) if p else cp(w[p][:, a:b], wi))
+
+    def target(p, k):
+        S(["VL%d" % (k // SP)], ["D0v%d" % p], ac(zs("D0", p, 256, 3, 4), T.VL[:, 128 * k + 64 * p:128 * k + 64 * p + 64], AF.Copy))
+
+    def total(p, part):
+        f = group(*[(LP[p][:, 2:256:4], comb(C1, a), w[p][:, c0:c1:st]) for a, (c0, c1, st) in enumerate(ROWS)])
+        PE(["w%d%d" % (p, part), "cb%d" % C1], [LK[p]], *(f[8:] if part else f[:8]))
+
+    def rounding(p):
+        S([LK[p]], ["D0a%d" % p], ac(zs("D0", p, 256, 1, 4), LP[p][:, 2:256:4], AF.Identity, bias=B0 + 0.48, scale=-1.003))
+
+    def prefix(p):
+        PE(both("w", p) + ["NLT"], BK[p], *halves(PX[p], z("NLT"), w[p]))
 
     def roots(p):
-        A = PX[1 - p]
-        PE(["D0%d" % p, "RT%d" % p, "ID16", "TU"], [PK[1 - p]], mm(A[:, H:H + 64], z("ID16"), zs("D0", p, 256, 0, 4), True, False),
-           *[mm(A[:, H + r:H + 64:st], turn(*BACK[j]), z("RT", 48 * p + c0, 48 * p + c1), False, False)
+        o = 512 * p
+        PE(["D0%d" % p, "RT%d" % p, "ID16", "TU"], [MK[p]], mm(PM[:, o:o + 64], z("ID16"), zs("D0", p, 256, 0, 4), True, False),
+           *[mm(PM[:, o + r:o + 64:st], turn(*BACK[j]), z("RT", 48 * p + c0, 48 * p + c1), False, False)
              for j, (_, _, (r, st), (c0, c1)) in enumerate(TURN)])
+
+    def limit(p):
+        PE(["D0a%d" % p, "ID16"], [MK[p]], mm(PM[:, 512 * p:512 * p + 64], z("ID16"), zs("D0", p, 256, 1, 4), False, True))
 
     def floor_vt(p):
         sp = str(p)
         V([LK[p], "D0" + sp, "D0a" + sp, "D0v" + sp, "D1" + sp], ["SC" + sp], scan(zs("SC", p, 256), zs("D0", p, 256), LP[p][:, 0:256], 0.0, OP.mult))
 
     def stays(p):
-        V([PK[1 - p], "SC%d" % p], ["eb%d" % p], tt(zs("eb", p), zs("SC", p, 256, 3, 4), PX[1 - p][:, H:H + 64], OP.is_lt))
+        V([MK[p], "SC%d" % p], ["eb%d" % p], tt(zs("eb", p), zs("SC", p, 256, 3, 4), PM[:, 512 * p:512 * p + 64], OP.is_lt))
 
     def turned(p):
         return [(LP[p][:, 320 + c0:320 + c1], turn(m, sh), zs("eb", p, 64, r, st)) for m, sh, (r, st), (c0, c1) in TURN]
 
     def window(p):
-        PE(["eb%d" % p, "C16%d" % p, "ID16", "TU"], [LK[p]], *group((LP[p][:, 320:368], z("ID16"), zs("C16", p, 48)), *turned(p)))
+        PE(["eb%d" % p, "C%d" % p, "ID16", "TU"], [LK[p]], *group((LP[p][:, 320:368], z("ID16"), cm(p)), *turned(p)))
 
     def bound(p):
-        PE(["SC%d" % p, "BC"], [PK[p]], *spread(PX[p], zs("SC", p, 256, 3, 4)))
+        f = spread(PX[p], zs("SC", p, 256, 3, 4))
+        PE(["SC%d" % p, "BC"], [BK[p][0]], *f[:8])
+        PE(["SC%d" % p, "BC"], [BK[p][1]], *f[8:])
 
-    def compare(p):
-        S([PK[p], "KB"], ["k%d" % p], ac(cond[p][:, :], PX[p][:, 0:H], AF.Sigmoid, bias=z("KB"), scale=-4096.0))
+    def compare(p, parts=(0, 1)):
+        a, b = PART[parts[0]][0], PART[parts[-1]][1]
+        S([BK[p][j] for j in parts] + ["KB"], ["k%d%d" % (p, j) for j in parts],
+          ac(cond[p][:, a:b], PX[p][:, a:b], AF.Sigmoid, bias=z("KB"), scale=-4096.0))
 
     def history(s):
-        if s == SP - 1:
-            S(["#LA", "EB"], ["EB0"], ac(z("EB", 16, 64), LA[:, 320:368], AF.Sigmoid, bias=-256 * 1151.5, scale=256.0))
         S(["#LA", "HT"], ["E8" if s == SP - 1 else "HT"], ac(z("E8") if s == SP - 1 else z("HT", s + 2, 40, 5), LA[:, 320:328],
                                                              AF.Sigmoid, bias=256 * 1151.5, scale=-256.0))
-        S(["C160", "DL"], ["DL"], ac(z("DL", s + 1, 40, 5), z("C16", 0, 8), AF.Identity, bias=1024.0))
+        S(["C0", "DL"], ["DL"], ac(z("DL", s + 1, 40, 5), cm(0, 8), AF.Identity, bias=1024.0))
+
+    def marks_banks(p, k):
+        return (PM, MK) if p and k % SP == SP - 1 else (PX[p], BK[p])
 
     def marks_sum(p, k):
+        P, pk = marks_banks(p, k)
         if k < RO * SP - 1:
-            PE(["w%d" % p, "N16", "eb%d" % p, "BC"], ["#M"], *(halves(PM, z("N16"), w[p]) + spread(PM, zs("eb", p))))
+            PE(both("w", p) + ["N16", "eb%d" % p, "BC"], pk, *(halves(P, z("N16"), w[p]) + spread(P, zs("eb", p))))
 
     def marks(p, k):
+        P, pk = marks_banks(p, k)
         if k < RO * SP - 1:
-            S(["#M"], ["m%d" % p], ac(T.MM[:, H * p:H * p + H], PM[:, 0:H], AF.Sigmoid, bias=-128.0, scale=2.0 ** 32))
+            S(pk, ["m%d" % p], ac(T.MM[:, H * p:H * p + H], P[:, 0:H], AF.Sigmoid, bias=-128.0, scale=2.0 ** 32))
 
-    def shown(p, rnd):
-        off, ck = lists(p, 5 * rnd + SP - 1)
-        S(AFK + [ck], ["A2%d" % p], ac(T.A2[:, H * p:H * p + H], T.AUF[:, 0:2048 + 128 * rnd].indirect(off), AF.Copy))
+    def shown(p, rnd, q, a=0, b=H):
+        off = T.CL[:, (SP - 1) * 96 + 48 * p + a // 16:(SP - 1) * 96 + 48 * p + b // 16] if rnd == 0 else z("CC", 48 * p + a // 16, 48 * p + b // 16)
+        o, i = T.A2[:, H * p + a:H * p + b], T.AUF[:, 0:2048 + 128 * rnd].indirect(off)
+        op(q, AFK + ["CC%d" % p if rnd else "c%d_%d" % (SP - 1, p)], ["A2%d%d" % (p, a)], ac(o, i, AF.Copy) if q == "s" else cp(o, i))
 
     def window_offsets(p):
         V([LK[p]], ["XL%d" % p], ts(zs("XL", p, 48), LP[p][:, 320:368], 1024.0, OP.add))
 
-    def gather_next(p, rnd):
-        sp = str(p)
-        V(DTK + ["XL" + sp, "k" + sp], ["X" + sp], tt(X[p][:, :], T.DT[:, 0:OD + 2048 + 128 * rnd].indirect(zs("XL", p, 48)), cond[p][:, :], OP.mult))
-        PE(["X" + sp, "COMBX"], [LK[p]], *group(*[(LP[p][:, 368:416], T.COMBX[:, 15 - i:143 - i], X[p][:, i:H:16]) for i in range(16)]))
+    def gather_next(p, rnd, part):
+        a, b = PART[part]
+        off = z("XL", 48 * p + a // 16, 48 * p + b // 16)
+        V(DTK + ["XL%d" % p, "k%d%d" % (p, part)], ["X%d%d" % (p, part)],
+          tt(X[p][:, a:b], T.DT[:, 0:OD + 2048 + 128 * rnd].indirect(off), cond[p][:, a:b], OP.mult))
 
-    def next_list(p, idx, rnd, gap):
+    def next_sum(p):
+        PE(both("X", p) + ["COMBX"], [LK[p]], *group(*[(LP[p][:, 368:416], T.COMBX[:, 15 - i:143 - i], X[p][:, i:H:16]) for i in range(16)]))
+
+    def next_list(p, idx, rnd):
         off, ck = lists(p, idx)
-        P, sp, last = LP[p][:, 368:416], str(p), idx % 5 == SP
-        if rnd == 0:
-            if p == 0 or not last:
-                V([LK[p]], [ck], ts(off, P, 1024.0, OP.add))
-            S([LK[p]], ["C16" + sp], ac(zs("C16", p, 48), P, AF.Copy))
+        V([LK[p]], [ck], ts(off, LP[p][:, 368:416], 1024.0 + OW * rnd, OP.add))
+
+    def settle(p, P, bias, after):
+        S([LK[p]], ["C%d" % p], ac(cm(p), P, AF.Identity, bias=bias))
+        if after is None:
+            S([LK[p]], ["RT%d" % p], ac(zs("RT", p, 48), P, AF.Sigmoid, bias=-256 * (1023.5 + bias), scale=-256.0))
         else:
-            V([LK[p]], ["rr" + sp], ts(zs("rr", p, 48), P, M35, OP.add, -M35, OP.add))
-            gap()
-            V([LK[p], "rr" + sp], ["C16" + sp], tt(zs("C16", p, 48), P, zs("rr", p, 48), OP.subtract))
-            gap()
-            if p == 0 or not last:
-                V(["C16" + sp], [ck], ts(off, zs("C16", p, 48), 1024.0, OP.add))
+            S([LK[p]], ["CLF%d" % p], ac(zs("CLF", p, 48), P, AF.Identity, bias=bias + 1024.0 + after))
+
+    def keep(p):
+        S([LK[p]], ["JW%d" % p], ac(zs("JW", p, 48), LP[p][:, 368:416], AF.Identity, bias=192.0, scale=1.0 / OW))
+        S(["JW%d" % p], ["XW%d" % p], ac(zs("XW", p, 48), zs("JW", p, 48), AF.Identity, bias=-192.0 * OW, scale=float(OW)))
+
+    def unwrap(p, last=False):
+        V([LK[p], "XW%d" % p], ["C%d" % p], tt(cm(p), LP[p][:, 368:416], zs("XW", p, 48), OP.subtract))
         if last:
-            S(["C16" + sp], ["CLF" + sp], ac(zs("CLF", p, 48), zs("C16", p, 48), AF.Identity, bias=1024.0))
+            S(["C%d" % p], ["CLF%d" % p], ac(zs("CLF", p, 48), cm(p), AF.Identity, bias=1024.0))
         else:
             root(p)
 
@@ -547,262 +579,379 @@ def rank_program(g, core, T, topo):
     for rnd in range(RO):
         base, i4, k3 = 5 * rnd, 5 * rnd + SP, SP * rnd + SP - 1
         DUM = "DUM%d" % rnd
-        TB, TBK, TBn, one = (T.WT, WTK, "WTn", 15.0 / 16) if rnd == 0 else (T.YN, YNK, "YNn", 1.0)
-        for n in range(2 * SP):
-            p, s, o = n % 2, n // 2, 1 - n % 2
-            k, idx = rnd * SP + s, base + s
-            if k == 0 and n == 0:
-                gather_counts(0, idx, k)
-                gather_counts(1, idx, k)
+        tb, TBK, TBn, one = (wt, WTK, "WTn", 15.0 / 16) if rnd == 0 else (lambda a, b: T.YN[:, a:b], YNK, "YNn", 1.0)
+        k0 = rnd * SP
+
+        def steps_of_rank(p):
+            o, a = LP[1 - p][:, 440:488], 16 + 48 * p
+            PE(["EB0", "EB%d" % p, "EB", "QB", "QB0", "QB%d" % p, "NLT", "NUT", "ID16", "NI16"], [LK[1 - p]], *group(
+                (o, z("ID16"), z("QB", a, a + 48)), (o, z("NI16"), z("QB", a - 1, a + 47)),
+                (o, z("NLT"), z("EB", a, a + 48)), (o, z("NUT"), z("EB", a - 1, a + 47))))
+
+        def ranks(p):
+            V([LK[1 - p], "D1", "POSF0"], ["POSF%d" % p], scan(zs("POSF", p, 48), LP[1 - p][:, 440:488], zs("D1", p, 48),
+                                                              z("POSF", 47, 48) if p else 0.0, OP.add))
+
+        def places(p):
+            V(["POSF%d" % p], ["POS%d" % p], cp(zs("POS", p, 48), zs("POSF", p, 48)))
+
+        def out_of_psum(p):
+            if rnd:
+                keep(p)
+            else:
+                settle(p, LP[p][:, 368:416], 0.0, None)
+
+        for s in range(SP):
+            k, idx, last = k0 + s, base + s, s == SP - 1
+            gather_counts(0, idx, k, 0)
+            if s and rnd:
+                unwrap(0)
+            if s:
+                next_list(1, idx, rnd)
+            elif rnd:
+                spend("v", 130)
+            total(0, 0)
+            gather_counts(0, idx, k, 1)
+            total(0, 1)
+            if k == SP:
+                spend("v", 60)
+            if k == 0:
+                gather_counts(1, idx, k, 0)
+                gather_counts(1, idx, k, 1)
                 first_gap()
-            elif k:
-                gather_counts(p, idx, k)
-            roots(p)
-            sums(p, k)
-            if n:
-                marks(o, rnd * SP + (n - 1) // 2)
-                gather_next(o, rnd)
-                spend("v", 300)
+            if s:
+                out_of_psum(1)
+            target(0, k)
+            rounding(0)
+            roots(0)
+            prefix(0)
+            limit(0)
+            target(1, k)
+            if last and rnd:
+                V(["C0"], ["CC0"], ts(zs("CC", 0, 48), cm(0), 1024.0, OP.add))
+            if last:
+                while spare["s"] and spare["s"][0][0] <= 400:
+                    spend("s", 400)
+            elif k == 0:
+                last_pointers()
             else:
-                spend("v", 900 * rnd)
-            if s == SP - 1:
-                shown(p, rnd)
-            elif n:
-                spend("s", 900)
-            if k == 0 and n == 0:
-                last_differences()
-            floor_vt(p)
-            gap()
-            if n == 2 * SP - 1:
+                spend("s", 800)
+            if k:
+                gather_counts(1, idx, k, 0)
+            if s and rnd:
+                unwrap(1)
+            floor_vt(0)
+            if k:
+                gather_counts(1, idx, k, 1)
+            total(1, 0)
+            if k == 0:
+                total(1, 1)
+            bound(0)
+            if k:
+                total(1, 1)
+            if not last:
+                compare(0, (0,))
+            rounding(1)
+            if last:
+                shown(0, rnd, "s")
+            stays(0)
+            window(0)
+            if k == 0:
+                differences(3)
+                V(["#N"], ["FL"], cp(z("FL"), PM[:, 640:768]))
+            if last and rnd:
+                V(["C1"], ["CC1"], ts(zs("CC", 1, 48), cm(1), 1024.0, OP.add))
+            if last and rnd == 0:
+                shown(1, rnd, "v", 0, 256)
+            else:
+                spend("v", 500 if k else 900)
+            roots(1)
+            prefix(1)
+            limit(1)
+            floor_vt(1)
+            window_offsets(0)
+            if last:
                 break
-            bound(p)
-            if n == 0:
-                stays(p)
-                spend("v", 1000)
-            else:
-                stays(p)
-                spend("v", 400)
-                next_list(o, base + (n + 1) // 2, rnd, gap)
-            window(p)
-            window_offsets(p)
-            if k == 0 and n == 0:
-                suffix_list()
-            compare(p)
-            if p == 0:
-                history(s)
-            marks_sum(p, k)
-            spend("s", 900)
-            if n == 5:
-                spend("v", 9000)
-                spend("s", 9000)
-            if n == 6:
-                for ns, R, W, f in (
-                        (70, ["HT", "DL"], ["hd"], tt(z("hd"), z("HT"), z("DL"), OP.mult)),
-                        (60, ["HT", "EB0"], ["CAND"], tt(z("CAND"), z("HT", 4, 40, 5), z("EB", 16, 24), OP.mult)),
-                        (70, ["EB0", "JQ", "QB"], ["QB0"], tt(z("qa"), z("EB", 16, 64), z("JQ", 0, 48), OP.mult)),
-                        (190, ["DL", "hd"], ["d1"], tt(z("d1"), z("DL"), z("hd"), OP.subtract)),
-                        (10, ["CAND", DUM], ["N2"], tt(z("N2"), z("CAND"), z(DUM, 0, 8), OP.mult)),
-                        (190, ["HT", "d1"], ["FS"], scan(z("FS"), z("HT"), z("d1"), 0.0, OP.mult)),
-                        (10, ["N2", DUM], ["ND"], tt(z("ND"), z(DUM, 0, 8), z("N2"), OP.subtract)),
-                        (0, ["QB0", "QB"], ["QBa"], ts(z("QB", 16, 64), z("qa"), float(OD), OP.mult))):
-                    later("v", ns, V, R, W, f)
-        nl = T.CL[:, i4 * 96:i4 * 96 + 8]
-        nk = "c%d_0" % i4
-        spend("v", 9000)
+            compare(0, (1,))
+            history(s)
+            spend("s", 400 if k else 500)
+            bound(1)
+            spend("v", 250 if k else 500)
+            stays(1)
+            window(1)
+            marks_sum(0, k)
+            gather_next(0, rnd, 0)
+            window_offsets(1)
+            gather_next(0, rnd, 1)
+            compare(1)
+            next_sum(0)
+            marks(0, k)
+            marks_sum(1, k)
+            gather_next(1, rnd, 0)
+            next_list(0, idx + 1, rnd)
+            gather_next(1, rnd, 1)
+            out_of_psum(0)
+            next_sum(1)
+            marks(1, k)
+            spend("s", 400 if k else 500)
+        nl, nk = z("NL"), "NL"
+        V(["#LA", "EB"], ["EB0"], ts(z("EB", 16, 64), LA[:, 320:368], 1151.5, OP.is_ge))
+        history(SP - 1)
+        compare(0)
+        if rnd:
+            shown(1, rnd, "s", 0, 256)
         stays(1)
+        V(["EB0", "JQ", "QB"], ["QB0"], tt(z("QB", 16, 64), z("EB", 16, 64), z("JQ", 0, 48), OP.mult))
         tu = turned(1)
         PE(["eb1", "TU"], ["#LB"], *(group(*tu[:2]) + group(*tu[2:])))
-        bound(1)
-        V(["FS", "DL", "ND"], ["KK"], tt(z("KK", 0, 8), z("FS", 3, 40, 5), z("ND"), OP.max), tt(z("KK", 8, 16), z("DL", 4, 40, 5), z("ND"), OP.max))
-        next_list(0, i4, rnd, lambda: None)
-        V(["KK"], ["FK"], cp(z("FK"), z("KK")))
+        steps_of_rank(0)
+        spend("s", 9000)
+        V(["HT", "EB0"], ["CAND"], tt(z("CAND"), z("HT", 4, 40, 5), z("EB", 16, 24), OP.mult))
+        t2("hd", "HT", "DL", OP.mult)
+        V(["CAND", DUM], ["N2"], tt(z("N2"), z("CAND"), z(DUM, 0, 8), OP.mult))
+        t2("d1", "DL", "hd", OP.subtract)
+        V(["N2", DUM], ["ND"], tt(z("ND"), z(DUM, 0, 8), z("N2"), OP.subtract))
         V(["#LB", "JQ", "QB"], ["QB1"], tt(z("QB", 64, 112), LB[:, 320:368], z("JQ", 48, 96), OP.mult))
-        S(["#LB", "EB"], ["EB1"], ac(z("EB", 64, 112), LB[:, 320:368], AF.Copy, scale=1.0 / OD))
-        V(AUXK + ["FK"], ["XF"], cp(z("XF"), T.AUX[:, :].indirect(z("FK"))))
-        rk_ = LA[:, 416:512]
-        PE(["EB0", "EB1", "EB", "QB", "QBa", "QB1", "NLT", "NUT", "ID16", "NI16"], ["#LA"], *group(
-            (rk_, z("ID16"), z("QB", 16, 112)), (rk_, z("NI16"), z("QB", 15, 111)),
-            (rk_, z("NLT"), z("EB", 16, 112)), (rk_, z("NUT"), z("EB", 15, 111))))
-        compare(1)
-        V(["#LB", "C161"], ["xb"], tt(z("xb"), LB[:, 320:368], zs("C16", 1, 48), OP.add))
-        V(["#LA", "D1"], ["POSF"], scan(z("POSF"), rk_, z("D1"), 0.0, OP.add))
+        V(["#LB", "EB"], ["EB1"], ts(z("EB", 64, 112), LB[:, 320:368], 1.0 / OD, OP.mult))
+        ranks(0)
+        steps_of_rank(1)
+        V(["#LB", "C1"], ["xb"], tt(z("xb"), LB[:, 320:368], cm(1), OP.add))
+        V(["HT", "d1"], ["FS"], scan(z("FS"), z("HT"), z("d1"), 0.0, OP.mult))
+        places(0)
+        S(["LBB", "POS0", "SW"], ["SW"], ac(T.SW[:, :].indirect(zs("POS", 0, 48)), T.LBB[:, :], AF.Sigmoid))
+        bound(1)
+        ranks(1)
+        V(["FS", "DL", "ND"], ["KK"], tt(z("KK", 0, 8), z("FS", 3, 40, 5), z("ND"), OP.max), tt(z("KK", 8, 16), z("DL", 4, 40, 5), z("ND"), OP.max))
+        places(1)
+        V(["KK"], ["FK"], cp(z("FK"), z("KK")))
         V(["xb"], ["XL1"], ts(zs("XL", 1, 48), z("xb"), 1024.0, OP.add))
-        V(["POSF"], ["POS"], cp(z("POS"), z("POSF")))
+        if rnd:
+            V(AUXK + ["FK"], ["XF"], cp(z("XF"), T.AUX[:, :].indirect(z("FK"))))
+        V(LBK + ["POS1", "VW"], ["VW"], cp(T.VW[:, :].indirect(zs("POS", 1, 48)), T.LBA[:, 0:H]))
+        spend("v", 9000)
+        marks_sum(0, k3)
+        marks_sum(1, k3)
+        S(["SW"], ["SWb"], ac(z("SWb"), T.SW[:, 0:384], AF.Copy))
+        marks(0, k3)
+        marks(1, k3)
+        if rnd:
+            compare(1)
+            shown(1, rnd, "s", 256, H)
+        else:
+            V(AUXK + ["FK"], ["XF"], cp(z("XF"), T.AUX[:, :].indirect(z("FK"))))
+            shown(1, rnd, "v", 256, H)
 
-        def pairs(h):
+        def pairs(h, banks=(0, 1)):
             f, xf = [], z("XF", 128 * h, 128 * h + 128)
-            for gg in range(8):
+            for gg in range(4 * banks[0], 4 * banks[-1] + 4):
                 o = PX[h][:, 128 * gg:128 * gg + 128]
                 f += group((o, T.SELK[:, 128 * gg:128 * gg + 128], xf), (o, xf, T.NSELK[:, 128 * gg:128 * gg + 128]))
-            PE(["XF", "SELK", "NSELK"], [PK[h]], *f)
+            PE(["XF", "SELK", "NSELK"], [BK[h][j] for j in banks], *f)
 
         def equal(h):
-            V([PK[h], "TRW"], ["EQ%d" % h], tt(T["EQ%d" % h][:, :], PX[h][:, :], T.TRW[:, :], OP.is_equal))
-        pairs(0)
-        oh = LA[:, 256:384]
-        PE(["k0", "BID"], ["#LA"], mm(oh, z("BID"), cond[0][:, 0:128], True, True))
-        marks_sum(1, k3)
-        pairs(1)
-        V(LBK + ["POS", "VW"], ["VW"], cp(T.VW[:, :].indirect(z("POS", 0, VS // 16)), T.LBA[:, 0:VS]))
-        S(["LBB", "POS", "SW"], ["SW"], ac(T.SW[:, :].indirect(z("POS", VS // 16, 96)), T.LBB[:, :], AF.Sigmoid))
-        S(["SW"], ["SWb"], ac(z("SWb"), T.SW[:, 0:384], AF.Copy))
+            V(BK[h] + ["TRW"], ["EQ%d" % h], tt(T["EQ%d" % h][:, :], PX[h][:, :], T.TRW[:, :], OP.is_equal))
+
+        def contexts_after(p):
+            next_sum(p)
+            if rnd:
+                keep(p)
+            else:
+                settle(p, LP[p][:, 368:416], 0.0, 0.0)
         sl = LB[:, 416:440]
-        PE(["VW", "SWb", "cb%d" % CSA, "cb%d" % CSB], ["#LB"], *group(
-            *(combed(sl, CSA, lambda i, n, st: T.VW[:, i:n:st], 384) + combed(sl, CSB, lambda i, n, st: z("SWb", i, n, st), 384))))
-        marks(1, k3)
-        equal(0)
-        V(TBK + ["FK"], ["hF"], ts(z("hF"), TB[:, :].indirect(z("FK", 0, 8)), -1.0, OP.mult, one, OP.add))
-        V(TBK + ["FK"], ["gF"], cp(z("gF"), TB[:, :].indirect(z("FK", 0, 8))))
+        if rnd:
+            pairs(0)
+        f = group(*(combed(sl, CSA, lambda i, n, st: z("SWb", i, n, st), 384) + combed(sl, CSB, lambda i, n, st: T.VW[:, i:n:st], 384)))
+        PE(["SWb", "cb%d" % CSA], ["#LB"], *f[:16])
+        PE(["VW", "cb%d" % CSB], ["#LB"], *f[16:])
+        if rnd:
+            equal(0)
+        else:
+            pairs(0)
         SND, RCV = T["SND%d" % rnd], T["RCV%d" % rnd]
         sk, rk = "SND%d" % rnd, "RCV%d" % rnd
         V(["#LB"], ["LNE"], ts(z("LNE"), sl, 1536.0, OP.add))
-        S(["A20", "A21", "A2z", "LNE"], [sk + "a"], ac(SND[:, 0:384], T.A2[:, :].indirect(z("LNE")), AF.Copy))
+        S(["A200", "A210", "A21256", "A2z", "LNE"], [sk + "a"], ac(SND[:, 0:384], T.A2[:, :].indirect(z("LNE")), AF.Copy))
         if rnd == 0:
             V(["#LB", sk + "z"], [sk + "b"], ts(SND[:, 385:432:2], sl, -0.5, OP.is_lt))
             V(["m0", "m1", "mz", "LNE"], [sk + "c"], cp(SND[:, 432:816], T.MM[:, 0:1552].indirect(z("LNE"))))
+            compare(1)
+        oh = PM[:, 512:640]
+        PE(["k00", "BID"], ["#N"], mm(oh, z("BID"), cond[0][:, 0:128], True, True))
+        TB = tb(0, NW)
+        S(TBK + ["FK"], ["hF"], ac(z("hF"), TB.indirect(z("FK", 0, 8)), AF.Identity, bias=one, scale=-1.0))
+        S(TBK + ["FK"], ["gF"], ac(z("gF"), TB.indirect(z("FK", 0, 8)), AF.Copy))
+        if rnd == 0:
+            equal(0)
+            plain_pointers(0)
+            plain_pointers(1)
         do_waits("q", [sk + c for c in "azbc"[:2 if rnd else 4]], [])
         g.remote_dma(RCV[:, :], SND[:, :], T.sem["arr%d" % rnd], T.sem["snt%d" % rnd], pid, rid, rmask)
         used["snt%d" % rnd] = ne
         used["arr%d" % rnd] = ne
         record(("rem%d" % rnd, "arr%d" % rnd, ne, {}), [], [rk])
 
+        PW, WK = [PM, T.PB], ["#M", "#B"]
+        dm = T.AUX[:, 2304 + 128 * rnd:2432 + 128 * rnd]
+
         def dup(h):
-            o, EQ = PM[:, 128 * h:128 * h + 128], T["EQ%d" % h]
-            PE(["EQ%d" % h, "OB", "XF", "CANDM"], ["#M"], *group(
-                *([(o, z("OB", 112 - 16 * gg, 240 - 16 * gg), EQ[:, 128 * gg:128 * gg + 128]) for gg in range(8)]
-                  + [(o, z("CANDM"), z("XF", 128 * h, 128 * h + 128))])))
+            o, EQ, xf = PW[h][:, 0:128], T["EQ%d" % h], zs("XF", h, 128)
+            PE(["EQ%d" % h, "OB", "XF", "CANDM", "IDN", "NI"] + AUXK, [WK[h]], *(
+                group((PW[h][:, 128:256], z("IDN"), xf), (PW[h][:, 128:256], z("NI"), dm))
+                + group((o, z("CANDM"), xf), *[(o, z("OB", 112 - 16 * gg, 240 - 16 * gg), EQ[:, 128 * gg:128 * gg + 128]) for gg in range(8)])))
 
         def winners(h):
-            V(["#M"], ["AR%d" % h], ts(zs("AR", h, 128), PM[:, 128 * h:128 * h + 128], 0.5, OP.is_gt))
+            V([WK[h]], ["AR%d" % h], ts(zs("AR", h, 128), PW[h][:, 0:128], 0.5, OP.is_gt))
 
         def keys(h):
-            V(["AR%d" % h, "XD%d" % h], ["ZW%d" % h], tt(zs("ZW", h, 128), zs("AR", h, 128), zs("XD", h, 128), OP.mult))
-            o = PM[:, 256 + 8 * h:264 + 8 * h]
-            PE(["ZW%d" % h, "cb%d" % CID, "ID16", "DU"], ["#M"], *group(
+            V(["AR%d" % h, WK[h]], ["ZW%d" % h], tt(zs("ZW", h, 128), zs("AR", h, 128), PW[h][:, 128:256], OP.mult))
+            o = PW[h][:, 256:264]
+            PE(["ZW%d" % h, "cb%d" % CID, "ID16", "DU"], [WK[h]], *group(
                 (o, z("ID16"), z("DU", 8 * rnd, 8 * rnd + 8)), *combed(o, CID, lambda i, n, st: z("ZW", 128 * h + i, 128 * h + n, st), 128)))
 
         def offsets(h):
-            V(["#M"], ["OF%d" % h], ts(z(("OFF", "OFD")[h]), PM[:, 256 + 8 * h:264 + 8 * h], 2048.0, OP.add))
+            V([WK[h]], ["OF%d" % h], ts(z(("OFF", "OFD")[h]), PW[h][:, 256:264], 2048.0, OP.add))
 
         def landed(p, e):
             o, i = T.LW[:, H * p:H * p + H], RCV[:, 0:400].indirect(zs("POG", p, 48))
             op(e, [rk, "POG"], ["LW%d" % p], ac(o, i, AF.Copy) if e == "s" else cp(o, i))
 
-        def shown_list(p, P):
-            PE(["LW%d" % p, "cb%d" % CLK], [LK[p]], *group(*combed(P, CLK, lambda i, n, st: T.LW[:, H * p + i:H * p + n:st], H)))
+        def shown_list(p, P, pk=None):
+            PE(["LW%d" % p, "cb%d" % CLK], [pk or LK[p]], *group(*combed(P, CLK, lambda i, n, st: T.LW[:, H * p + i:H * p + n:st], H)))
 
         def next_targets(a, b):
             if rnd == 0:
                 targets(1, T.PA, "#A", a, b)
+
+        def new_rows():
+            V(["C0"], ["NL"], ts(z("NL"), cm(0, 8), 1024.0, OP.add))
+            S(WTK + [nk], ["ug"], ac(z("ug"), wt(0, 2304).indirect(nl), AF.Identity, bias=128.3, scale=0.5))
+        hh, wc = PM[:, 640:768], 2048 + 128 * rnd
         dup(0)
-        next_targets(0, 2)
-        S(WTK + [nk], ["ug"], ac(z("ug"), T.WT[:, 0:2304].indirect(nl), AF.Identity, bias=128.3, scale=0.5))
+        pairs(1)
+        gather_next(0, rnd, 0)
+        winners(0)
+        V(["#N", "hF"], ["hh"], tt(hh, oh, z("hF"), OP.mult))
+        keys(0)
+        gather_next(0, rnd, 1)
+        V(["AR0", "hh", "#N"], ["m1"], tt(z("m1"), zs("AR", 0, 128), hh, OP.mult))
+        equal(1)
+        offsets(0)
+        V(["POSF0", "POSF1"], ["POG"], ts(z("POG"), z("POSF"), 384.0, OP.min))
         if rnd == 0:
+            contexts_after(0)
+            dup(1)
+            V(["#LB"], ["T1"], ts(z("T1"), sl, -0.5, OP.is_lt))
+            V(["#LB", "JL"], ["LNF"], tt(z("LNF"), sl, z("JL", 0, 24), OP.subtract))
+            V(["#N", "AR0"], ["OA"], tt(z("OA"), oh, zs("AR", 0, 128), OP.mult))
+            new_rows()
+            next_targets(0, 2)
+            V(["LNF", "T1", "PJ"], ["PJ"], tt(z("PJ", 0, 48, 2), z("LNF"), z("T1"), OP.mult))
+            gather_next(1, rnd, 1)
+            S(["OA"], ["nOA"], ac(z("nOA"), z("OA"), AF.Identity, bias=1.0, scale=-1.0))
             S(AUXK + [nk], ["AFn"], ac(T.AUF[:, 2048:OD], T.AUX[:, 0:2048].indirect(nl), AF.Copy))
             S(DTK + [nk], ["DTn"], ac(T.DT[:, OD + 2048:OD + OD], T.DT[:, OD:OD + 2048].indirect(nl), AF.Copy))
-            later("v", 60, V, ["#LB"], ["T1"], ts(z("T1"), sl, -0.5, OP.is_lt))
-            later("v", 60, V, ["#LB", "JL"], ["LNF"], tt(z("LNF"), sl, z("JL", 0, 24), OP.subtract))
-            later("v", 200, V, ["LNF", "T1", "PJ"], ["PJ"], tt(z("PJ", 0, 48, 2), z("LNF"), z("T1"), OP.mult))
-        dm = T.AUX[:, 2304 + 128 * rnd:2432 + 128 * rnd]
-        if rnd:
-            equal(1)
-        V(["XF"] + AUXK, ["XD0"], tt(zs("XD", 0, 128), zs("XF", 0, 128), dm, OP.subtract))
-        winners(0)
-        V(["#LA", "hF"], ["hh"], tt(z("hh"), oh, z("hF"), OP.mult))
-        keys(0)
-        if rnd == 0:
-            equal(1)
-        else:
-            gather_next(1, rnd)
-        V(["AR0", "hh"], ["m1"], tt(z("m1"), zs("AR", 0, 128), z("hh"), OP.mult))
-        offsets(0)
-        dup(1)
-        next_targets(2, 5)
-        V(["XF"] + AUXK, ["XD1"], tt(zs("XD", 1, 128), zs("XF", 1, 128), dm, OP.subtract))
-        V(["gF", "m1", "OF0"], TBK, tt(TB[:, :].indirect(z("OFF")), z("gF"), z("m1"), OP.add))
-        if rnd == 0:
-            V(["#LA", "AR0"], ["OA"], tt(z("OA"), oh, zs("AR", 0, 128), OP.mult))
-            S(["OA"], ["nOA"], ac(z("nOA"), z("OA"), AF.Identity, bias=1.0, scale=-1.0))
-        gap()
-        winners(1)
-        gap()
-        V(["#LA", "AR1"], ["OBm"], tt(z("OBm"), oh, zs("AR", 1, 128), OP.mult))
-        keys(1)
-        if rnd:
-            next_list(1, i4, rnd, gap)
-        if rnd == 0:
+            plain_pointers(2)
+            plain_pointers(3)
             tz("u2", "ug", -128.0625, OP.add, -TINY, OP.max)
         else:
-            tz("u2", "ug", -128.0, OP.add)
-        V(TBK + ["FK", "OBm"], ["s1"], tt(z("s1"), TB[:, :].indirect(z("FK", 8, 16)), z("OBm"), OP.add))
+            dup(1)
+            contexts_after(0)
+        V(["gF", "m1", "OF0"] + ["ug"] * (1 - rnd), TBK, tt(TB.indirect(z("OFF")), z("gF"), z("m1"), OP.add))
+        if rnd:
+            gather_next(1, rnd, 0)
+        winners(1)
+        if rnd == 0:
+            V(["u2", "AR0"], [TBn], tt(tb(wc, wc + 128), z("u2"), zs("AR", 0, 128), OP.mult))
+        keys(1)
+        V(["#N", "AR1"], ["OBm"], tt(z("OBm"), oh, zs("AR", 1, 128), OP.mult))
+        if rnd:
+            gather_next(1, rnd, 1)
+            unwrap(0, True)
+        else:
+            next_targets(2, 4)
+            gather_next(1, rnd, 0)
+            contexts_after(1)
+        V(TBK + ["FK", "OBm"], ["s1"], tt(z("s1"), TB.indirect(z("FK", 8, 16)), z("OBm"), OP.add))
         if rnd == 0:
             t2("qS", "OA", "WR", OP.mult)
             tz("s2", "s1", 15.0, OP.min, 128.0, OP.add)
             V(STK + ["FK", "nOA"], ["tS"], tt(z("tS"), T.ST[:, :].indirect(z("FK", 0, 8)), z("nOA"), OP.mult))
-            PE(["SH16", "tS", "qS", "AFn", "cb%d" % CID], ["#B"], *(group((T.PB[:, 0:128], z("SH16"), z("tS")), (T.PB[:, 0:128], z("SH16"), z("qS")))
-                                                                    + group((T.PB[:, 128:256], comb(CID, 15), T.AUF[:, 2048:OD]))))
-            S(["#B"], ["xs"], ac(z("xs"), T.PB[:, 0:128], AF.Copy))
+            PE(["SH16", "tS", "qS", "AFn", "cb%d" % CID], ["#M"], *(group((PM[:, 0:128], z("SH16"), z("tS")), (PM[:, 0:128], z("SH16"), z("qS")))
+                                                                    + group((PM[:, 128:256], comb(CID, 15), T.AUF[:, 2048:OD]))))
+            S(["#M"], ["xs"], ac(z("xs"), PM[:, 0:128], AF.Copy))
             tz("s3", "s2", -128.0625, OP.add, -TINY, OP.max)
         else:
-            tz("POG", "POSF", 384.0, OP.min)
+            new_rows()
             landed(0, "s")
+            contexts_after(1)
             tz("s3", "s1", 15.0, OP.min)
-        wc = 2048 + 128 * rnd
-        V(["u2", "AR0"], [TBn], tt(TB[:, wc:wc + 128], z("u2"), zs("AR", 0, 128), OP.mult))
         offsets(1)
-        if rnd == 0:
-            gather_next(1, rnd)
-            next_targets(5, 8)
-        V(["s3", "OF1"], TBK, cp(TB[:, :].indirect(z("OFD")), z("s3")))
         if rnd:
+            tz("u2", "ug", -128.0, OP.add)
+        V(["s3", "OF1"], TBK, cp(TB.indirect(z("OFD")), z("s3")))
+        if rnd:
+            V(["u2", "AR0"], [TBn], tt(tb(wc, wc + 128), z("u2"), zs("AR", 0, 128), OP.mult))
             for a, q in ((0, "y"), (1152, "y")):
                 dma(q, YNK, [], (T.yn[:, a:a + 1152], T.YN[:, a:a + 1152]))
 
-        def merged(P, pk, a, b):
-            V([pk, "CLF0", "CLF1"], ["mx%d" % a], tt(z("mx", a, b), P, z("CLF", a, b), OP.max))
-            gap()
-            V(["mx%d" % a], ["cc%d" % a], ts(z("cc", a, b), z("mx", a, b), 4095, BA))
-            gap()
+        def merged(p, P, pk=None):
+            V([pk or LK[p], "CLF%d" % p], ["mx%d" % p], tt(zs("mx", p, 48), P, zs("CLF", p, 48), OP.max))
+
+        def flag(p):
+            V(["mx%d" % p], ["rr%d" % p], ts(zs("rr", p, 48), zs("mx", p, 48), 2.0 * OW, OP.is_ge, 2.0 * OW, OP.mult))
+
+        def plain(p):
+            V(["mx%d" % p, "rr%d" % p], ["YC%d" % p], tt(zs("YC", p, 48), zs("mx", p, 48), zs("rr", p, 48), OP.subtract))
         if rnd == 0:
-            S(["#B", "X1"], ["DFn"], ac(T.DT[:, 2048:OD], T.PB[:, 128:256], AF.Copy))
-            next_list(1, i4, rnd, gap)
-            tz("kk", "xs", M35, OP.add, -M35, OP.add)
-            tz("POG", "POSF", 384.0, OP.min)
+            dma("y", WTK, ["WTl"], (T.WT[:, 0:OW], wt(0, OW)))
+            for j in range(4):
+                later("s", 400, S, WTK, ["WTh%d" % j], ac(T.WT[:, 2 * OW + 544 * j:2 * OW + 544 * j + 544], wt(544 * j, 544 * j + 544), AF.Copy))
+            tz("k1", "xs", 1.0 / 4096, OP.mult, M23, OP.add)
+            S(["#M"], ["DFn"], ac(T.DT[:, 2048:OD], PM[:, 128:256], AF.Copy))
+            next_targets(4, 7)
+            tz("kk", "k1", -M23, OP.add, float(OW), OP.mult)
             V(["FS"], ["DL"], cp(z("DL", 0, 40, 5), z("FS", 4, 40, 5)))
-            V(["kk", "xs", "OF0"], DTK, tt(T.DT[:, OD:OD + NW].indirect(z("OFF")), z("xs"), z("kk"), OP.subtract))
             zeros()
             landed(0, "s")
-            targets_out(1, T.PA, "#A")
             landed(1, "s")
+            spend("s", 400)
             V([rk, "PJ"], ["TF"], scan(z("TF"), RCV[:, 384:432], z("PJ"), 0.0, OP.mult))
             V(["TF"], ["TO"], cp(z("TO"), z("TF", 1, 48, 2)))
             V([rk, "TO", "m0", "m1", "mz"], ["m0", "m1", "mz"], cp(T.MM[:, :].indirect(z("TO")), RCV[:, 432:816]))
-            for p in (0, 1):
-                shown_list(p, LP[p][:, 368:416])
+            shown_list(0, LA[:, 368:416])
+            next_targets(7, 8)
+            shown_list(1, LB[:, 368:416])
+            targets_out(1, T.PA, "#A")
 
             def hopped(p):
                 off, ck = lists(p, SP + 1)
-                V(["cc%d" % (48 * p)], [ck], cp(off, zs("cc", p, 48)))
-                V(["cc%d" % (48 * p)], ["C16%d" % p], ts(zs("C16", p, 48), zs("cc", p, 48), -1024.0, OP.add))
-                root(p)
-            merged(LA[:, 368:416], "#LA", 0, 48)
-            hopped(0)
+                V(["YC%d" % p], [ck], cp(off, zs("YC", p, 48)))
+                S(["YC%d" % p], ["C%d" % p], ac(cm(p), zs("YC", p, 48), AF.Identity, bias=-1024.0))
+                S(["YC%d" % p], ["RT%d" % p], ac(zs("RT", p, 48), zs("YC", p, 48), AF.Sigmoid, bias=128.0, scale=-256.0))
+            merged(0, LA[:, 368:416])
             S(["#LA"], ["HF"], ac(z("HF"), LA[:, 368:376], AF.Sigmoid, bias=-2048.0))
-            later("v", 260, V, ["#LB", "CLF1"], ["mx48"], tt(z("mx", 48, 96), LB[:, 368:416], z("CLF", 48, 96), OP.max))
+            flag(0)
+            plain(0)
+            hopped(0)
+            merged(1, LB[:, 368:416])
+            later("v", 130, flag, 1)
+            later("v", 60, lambda: (plain(1), spend("v", 190), hopped(1)))
             later("v", 60, V, ["HF", "E8"], ["HT"], tt(z("HT", 1, 40, 5), z("E8"), z("HF"), OP.subtract))
-            later("v", 260, V, ["mx48"], ["cc48"], ts(z("cc", 48, 96), z("mx", 48, 96), 4095, BA))
-            later("v", 120, hopped, 1)
+            later("v", 450, V, ["kk", "xs", "OF0"], DTK, tt(T.DT[:, OD:OD + NW].indirect(z("OFF")), z("xs"), z("kk"), OP.subtract))
             for j in range(9):
-                later("v", 190, V, WTK, ["yn%d" % j], ts(T.YN[:, 256 * j:256 * j + 256], T.WT[:, 256 * j:256 * j + 256], M23, OP.add, -M23, OP.add))
+                later("v", 190, V, WTK, ["yn%d" % j], ts(T.YN[:, 256 * j:256 * j + 256], wt(256 * j, 256 * j + 256), M23, OP.add, -M23, OP.add))
         else:
             landed(1, "v")
-            for p in (0, 1):
-                shown_list(p, LP[p][:, 448:496])
-            for p in (0, 1):
-                V([LK[p], "CLF%d" % p], ["mx%d" % p], tt(zs("mx", p, 48), LP[p][:, 448:496], zs("CLF", p, 48), OP.max))
-            V(["mx0", "mx1"], ["cc0"], ts(z("cc"), z("mx"), 4095, BA))
-            V(["cc0"], ["YC"], cp(z("YC"), z("cc")))
-            dma("s", ["YC"], [], (T.yc[:, :], z("YC")))
+            shown_list(0, LA[:, 448:496])
+            shown_list(1, PM[:, 0:48], "#M")
+            unwrap(1, True)
+            merged(0, LA[:, 448:496])
+            flag(0)
+            plain(0)
+            merged(1, PM[:, 0:48], "#M")
+            flag(1)
+            plain(1)
+            dma("s", ["YC0", "YC1"], [], (T.yc[:, :], z("YC")))
 
     for q in ("v", "s", "t", "q"):
         g.wait_ge(T.sem[q], cnt[q])

from concourse.mybir import AluOpType, ActivationFunctionType, AxisListType

OP = AluOpType
AF = ActivationFunctionType
RO, SP = 2, 4
NW = 2560
OD = 2176
H = 768
OW = NW
B0 = 1280.0
TINY = 2.0 ** -20
M23, M35 = 1.5 * 2 ** 23, 1.5 * 2 ** 35
F32, B16, I32, F16, U16 = "float32", "bfloat16", "int32", "float16", "uint16"
ROWS = [(a, 512, 8) for a in range(8)] + [(512 + a, H, 4) for a in range(4)]
TURN = [("lo", 8 * r, (r, 2), (0, 32)) for r in range(2)] + [("q2", 4 * r - 8, (r, 4), (32, 48)) for r in range(4)]
BACK = [("lo", 0), ("hi", -8), ("q0", 8), ("q1", 4), ("q2", 0), ("q3", -4)]
MASKS = {"lo": (0, 8), "hi": (8, 16), "q0": (0, 4), "q1": (4, 8), "q2": (8, 12), "q3": (12, 16)}
C1, C0, CID, CLK, CSA, CSB = range(6)
WEIGHTS = {CID: {4: -1024 - 4128, 7: 32, 8: 1}, CLK: {2: 32, 3: 1, 4: 2 * OW - 4128}, CSA: {15: -1536}, CSB: {15: H - 1536}}
SCRATCH = {}
WHERE = {}


def sb(dtype, **kw):
    for name, n in kw.items():
        SCRATCH[name] = ("sbuf", [128, n], dtype)


def pool(buf, dtype, **kw):
    o = 0
    for name, n in kw.items():
        WHERE[name] = (buf, o, n)
        o += -(-n // 16) * 16
    SCRATCH[buf] = ("sbuf", [128, o], dtype)


sb(I32, tabI=2048, CI=2048, CPI=416, CPL=288, BI=640)
sb(F32, YB=2048, ST=NW, DT=OD + NW, LBB=H, SW=4608)
sb(B16, WT=3 * NW, AUX=NW, AUF=OD, VV=12288, VL=1024, w0=H, w1=H, k0=H, k1=H, MM=1920, YN=NW, BB=640, LBA=1024,
   VW=4608, A2=1552, SND0=816, SND1=400, RCV0=816, RCV1=400, LW=1536, SELK=1024, NSELK=1024, TRW=1024, EQ0=1024, EQ1=1024,
   COMB=864)
sb(F16, X0=H, X1=H, COMBX=144, SH=2048, BC=1536, FB=2048, TU=960)
sb(U16, CL=960)
pool("zi", I32, CXI=96, i_rm=16, i_pc=16, i_g8=8, i_bm=128, i_dp=160, i_sf=144, i_wr=128, i_jc=64)
pool("zf", F32, RM=16, PC=1, G8=8, JI=96, JL=96, JQ=96, DUM0=16, DUM1=16, CLF=96, YC=96, HT=40, FC=128,
     DL=40, hd=40, d1=40, FS=40, KK=16, CAND=8, ND=8, N2=8, D1=96, POSF=96, PJ=48, TF=48, E8=8, MK=8, KB=1, CB=1,
     LNF=24, T1=24, HF=8, xs=128, kk=128, ZF=384, rr=96, xb=48, mx=96, k1=128, XW=96, W16=64, WM=64, WC=4, TWO=16, Z16=16)
pool("zb", B16, BM=128, IDN=128, NLT=128, NUT=128, N16=128, NI=128, JW=96, CANDM=128, BID=128, U1=128, U2=128, LTu=128, LTB=128,
     SELV=144, OB=240, SWb=384, EB=112, HB=288, LB=288, XF=256, XD=256, ZW=256, AR=256, OA=128, nOA=128, OBm=128, gF=128,
     hF=128, hh=128, m1=128, s1=128, s2=128, s3=128, ug=128, u2=128, ZB=384)
pool("zh", F16, SH16=128, ID16=128, NI16=128, IDW=160, SELH=144, WR=128, tS=128, qS=128, QB=112, C4=96, RT=96, D0=512,
     SC=512, eb=128, FH=128, DU=16)
pool("zu", U16, POS=96, POG=96, LNE=24, TO=24, FK=16, OFF=8, OFD=8, XL=96, FL=128, CC=96, NL=8)
for nm, nc in (("PA", 1024), ("PB", 1024), ("PM", 1024), ("LA", 512), ("LB", 512)):
    SCRATCH[nm] = ("psum", [128, nc], F32)

SEMAPHORES = ["v", "s", "t", "q", "arr0", "arr1", "snt0", "snt1"] + ["d%d" % i for i in range(60)]


def rank_program(g, core, T, topo):
    rank = T.rank_of(core)
    if rank is None:
        return
    Q = {"v": g.vector, "s": g.scalar, "t": g.tensor, "q": g, "y": g.sync}
    cnt = {"v": 0, "s": 0, "t": 0, "q": 0}
    know = {q: {} for q in Q}
    res, acc, used, nd = {}, {}, {}, [0]

    def do_waits(q, R, W):
        deps = []
        for k in R:
            if k[0] != "#":
                deps += res.get(k, ([], []))[0]
        for k in W:
            if k[0] != "#":
                ws, rs = res.get(k, ([], []))
                deps += ws + rs
        for k in list(R) + list(W):
            if k[0] == "#":
                deps += [e for e in acc.get(k, []) if e[0] != q]
        best = {}
        for e in deps:
            if know[q].get(e[1], 0) < e[2] and (e[1] not in best or best[e[1]][2] < e[2]):
                best[e[1]] = e
        for e in [e for e in best.values() if not any(o is not e and o[3].get(e[1], 0) >= e[2] for o in best.values())]:
            Q[q].wait_ge(T.sem[e[1]], e[2])
            k = know[q]
            k[e[1]] = max(k.get(e[1], 0), e[2])
            for s, v in e[3].items():
                k[s] = max(k.get(s, 0), v)

    def record(ent, R, W):
        for k in W:
            if k[0] != "#":
                res[k] = ([ent], [])
        for k in R:
            if k[0] != "#" and k not in W:
                ws, rs = res.get(k, ([], []))
                res[k] = (ws, [e for e in rs if e[0] != ent[0]] + [ent])
        for k in list(R) + list(W):
            if k[0] == "#":
                acc[k] = [ent]

    def op(q, R, W, *fns):
        do_waits(q, R, W)
        for fn in fns:
            fn(Q[q]).then_inc(T.sem[q], 1)
            cnt[q] += 1
        clock = dict(know[q])
        clock[q] = cnt[q]
        record((q, q, cnt[q], clock), R, W)

    def dma(q, R, W, *pairs):
        do_waits(q, R, W)
        name = "d%d" % nd[0]
        nd[0] += 1
        for o, i in pairs:
            Q[q].dma_start(o, i).then_inc(T.sem[name], 16)
        used[name] = 16 * len(pairs)
        record((name, name, 16 * len(pairs), dict(know[q])), R, W)

    def z(name, a=0, b=None, st=1, p=128):
        buf, o, n = WHERE[name]
        return T[buf][0:p, o + a:o + (n if b is None else b):st]

    def ts(out, a, s1, o1, s2=None, o2=None):
        if o2 is None:
            return lambda e: e.tensor_scalar(out, a, s1, None, o1)
        return lambda e: e.tensor_scalar(out, a, s1, s2, o1, o2)

    def tt(out, a, b, o):
        return lambda e: e.tensor_tensor(out, a, b, o)

    def cp(out, a):
        return lambda e: e.tensor_copy(out, a)

    def ms(out, c):
        return lambda e: e.memset(out, c)

    def ac(out, a, f, **kw):
        return lambda e: e.activation(out, a, f, **kw)

    def mm(out, l, r, st, sp):
        return lambda e: e.matmul(out, l, r, st, sp)

    def scan(out, d0, d1, first, o0):
        return lambda e: e.tensor_tensor_scan(out, d0, d1, first, o0, OP.add)

    def rowsum(out, a):
        return lambda e: e.tensor_reduce(out, a, AxisListType.X, OP.add)

    def group(*terms):
        return [mm(o, l, r, j == 0, j == len(terms) - 1) for j, (o, l, r) in enumerate(terms)]

    def V(R, W, *f):
        op("v", R, W, *f)

    def S(R, W, *f):
        op("s", R, W, *f)

    def PE(R, W, *f):
        op("t", R, W, *f)

    def tz(out, a, s1, o1, *more):
        V([a], [out], ts(z(out), z(a), s1, o1, *more))

    def t2(out, a, b, o):
        V([a, b], [out], tt(z(out), z(a), z(b), o))

    PX, LP, PK, LK = [T.PA, T.PB], [T.LA, T.LB], ["#A", "#B"], ["#LA", "#LB"]
    MK, BK = ["#M", "#N"], [["#A", "#A1"], ["#B", "#B1"]]
    LA, LB, PM = T.LA, T.LB, T.PM
    w, cond, X = ([T["%s%d" % (a, p)] for p in (0, 1)] for a in ("w", "k", "X"))
    AUXK = ["AUX"] + ["ar%d" % i for i in range(6)]

    def comb(v, i):
        return T.COMB[:, v * 144 + 15 - i:v * 144 + 143 - i]

    def combed(out, v, src, n):
        return [(out, comb(v, i), src(i, n, 16)) for i in range(16)]

    def RMc(r):
        return z("RM", r, r + 1)

    def turn(mask, shift):
        o = 160 * list(MASKS).index(mask) + 16 - shift
        return T.TU[:, o:o + 128]

    def zs(name, p, n=64, a=0, st=1):
        return z(name, n * p + a, n * p + n, st)

    def wt(a, b):
        return T.WT[:, OW + a:OW + b]

    def cm(p, n=48):
        return z("C4", 48 * p, 48 * p + n)

    spare = {"v": [], "s": []}

    def later(q, ns, f, *a):
        spare[q].append((ns, lambda: f(*a)))

    def spend(q, ns):
        while spare[q] and spare[q][0][0] <= ns:
            c, f = spare[q].pop(0)
            f()
            ns -= c

    def tab_load(k, q):
        dma(q, [], ["tab%d" % k], (T.tabI[:, 512 * k:512 * k + 512], T.tab[:, 512 * k:512 * k + 512]))
    tab_load(0, "s")
    dma("y", [], ["cpF"], (T.CPI[:, 288:416], T.suf[:, :]))
    dma("s", [], ["vv0"], (T.VV[0:8, 0:6144], T.vv[:, 0:6144]))
    tab_load(1, "y")
    dma("y", [], ["CXI"], (z("CXI"), T.cx[:, :]))
    tab_load(2, "s")
    tab_load(3, "y")
    dma("y", [], ["cpL"], (T.CPI[:, 0:128], T.lnk[:, :]))
    dma("y", [], ["vv1"], (T.VV[0:8, 6144:12288], T.vv[:, 6144:12288]))

    def iota(tile, key, pattern, base, cm, **kw):
        op("q", [], [key], lambda e: e.iota(tile, pattern, base, cm, **kw))

    def select(tile, pattern, test, fill, base, cm):
        op("q", [tile], [tile], lambda e: e.affine_select(T[tile][:, :], T[tile][:, :], pattern, test, fill, base, cm))
    fl = {"allow_small_or_imprecise_dtypes": True}
    iota(z("i_rm"), "i_rm", [[-1, 16]], 0, 1)
    iota(z("i_g8"), "i_g8", [[-16, 8]], 0, 1)
    iota(z("i_bm"), "i_bm", [[-16, 8], [0, 16]], 0, 1)
    iota(z("i_dp"), "i_dp", [[1, 160]], -16, -1)
    iota(z("i_sf"), "i_sf", [[1, 144]], -15, -16)
    iota(z("i_pc"), "i_pc", [[0, 16]], 0, 1)
    iota(T.DT[:, 0:OD], "DF", [[0, OD]], 0, 0, **fl)
    iota(T.CPI[:, 128:256], "cpj", [[1, 128]], 0, 128)
    iota(T.CPI[:, 256:288], "cpk", [[1, 32]], 0, 32)
    iota(z("i_jc"), "i_jc", [[1, 64]], 0, 64)
    iota(z("JI"), "JI", [[16, 96]], 0, 0, **fl)
    iota(z("i_wr"), "i_wr", [[1, 128]], 0, 0)

    def fill(tile, key, n, c):
        iota(tile, key, [[0, n]], c, 0, **fl)
    for name, c in (("DL", 0), ("HT", 0), ("W16", 0), ("TWO", 2), ("Z16", 0)):
        fill(z(name), name, WHERE[name][2], c)
    for j, wts in enumerate(WEIGHTS.values()):
        for r, c in wts.items():
            fill(z("W16", 16 * j + r, 16 * j + r + 1), "W16", 1, c)
    fill(T.LBA[:, :], "LBA", 1024, 1)
    for i in range(6):
        iota(T.BB[:, 64 * i:64 * i + 64], "bb%d" % i, [[0, 32 >> i], [1, 2], [0, 1 << i]], 0, 0, **fl)
    for name, c in (("ZB", 0), ("ZF", 0), ("D1", 16), ("OB", 0)):
        fill(z(name), name, WHERE[name][2], c)
    for tile, key, n, c in ((z("EB", 0, 16), "EB", 16, 0), (T.A2[:, 1536:1552], "A2z", 16, 0), (T.MM[:, 1536:1552], "mz", 16, 0),
                            (T.SND0[:, 384:432], "SND0z", 48, 0), (T.SND1[:, 384:400], "SND1z", 16, 0), (z("OB", 112, 128), "OB", 16, -1)):
        fill(tile, key, n, c)
    for tile, sg in (("SELK", 1.0), ("NSELK", -1.0)):
        iota(T[tile][:, :], tile, [[0, 1024]], 0, 0, **fl)
        for r, c in ((7, 32.0), (8, 1.0)):
            select(tile, [[-16, 8], [0, 128]], OP.not_equal, sg * c, -r, 1)
    iota(T.TRW[:, :], "TRW", [[0, 1024]], 0, 0, **fl)
    select("TRW", [[0, 8], [1, 128]], OP.is_gt, 8192.0, 0, -1)
    iota(T.ST[:, 2048:NW], "STz", [[0, 512]], 0, 0, **fl)
    iota(T.YN[:, 2304:NW], "YNz", [[0, 256]], 0, 0, **fl)

    SR, BA = OP.logical_shift_right, OP.bitwise_and
    dp = z("i_dp", 16, 144)
    V([], ["w0"], ms(w[0][:, :], 0.0))
    tz("i_rm", "i_rm", 15, BA)
    tz("i_g8", "i_g8", 4, OP.arith_shift_right)
    V([], ["COMBX"], ms(T.COMBX[:, :], 0.0))
    tz("i_bm", "i_bm", 4, OP.arith_shift_right)
    tz("RM", "i_rm", 0.0, OP.is_equal)
    V([], ["COMB"], ms(T.COMB[:, :], 0.0))
    V(["RM"], ["CB"], tt(z("CB"), RMc(4), RMc(9), OP.add))
    tz("G8", "i_g8", 0.0, OP.is_equal)
    tz("BM", "i_bm", 0.0, OP.is_equal)
    for name, c, o in (("U1", -1.0, OP.is_equal), ("IDN", 0.0, OP.is_equal), ("LTu", 0.0, OP.is_ge)):
        V(["i_dp"], [name], ts(z(name), dp, c, o))
    tz("SELV", "i_sf", 0.0, OP.is_equal, 1.0 / 16, OP.mult)
    t2("U1", "U1", "BM", OP.mult)
    V(["G8", "COMB"], ["cb%d" % C1], ts(T.COMB[:, C1 * 144 + 15:C1 * 144 + 143:16], z("G8"), -1.0, OP.mult))
    V(["G8", "COMBX"], ["COMBX"], cp(T.COMBX[:, 15:143:16], z("G8")))
    tz("IDW", "i_dp", 0.0, OP.is_equal, float(OD), OP.mult)
    t2("SH16", "IDN", "U1", OP.subtract)
    t2("LTB", "LTu", "BM", OP.mult)
    V(["RM"], ["MK"], *[rowsum(z("MK", j, j + 1), z("RM", a, b)) for j, (a, b) in enumerate(MASKS.values())])

    tz("SELH", "i_sf", 0.0, OP.is_equal)

    def const(out, n, c):
        return ac(out, w[0][:, 0:n], AF.Identity, bias=c)
    S(["w0"], ["D00", "D01", "WTz"], const(z("D0", 0, 512, 4), 128, 0.0), const(z("D0", 2, 512, 4), 128, 1.0), const(wt(2048, NW), 512, 0.0))
    for p in (0, 1):
        S(["w0", LK[p]], ["D1%d" % p], const(LP[p][:, 0:256:4], 64, 1.0625), const(LP[p][:, 1:256:4], 64, -1.0625 * B0),
          const(LP[p][:, 3:256:4], 64, B0 - 255.0 / 512))

    def scaled(out, a, col, key):
        S([a, key], [out], ac(z(out), z(a), AF.Copy, scale=col))

    def root(p):
        S(["C%d" % p], ["RT%d" % p], ac(zs("RT", p, 48), cm(p), AF.Sigmoid, bias=-256 * 1023.5, scale=-256.0))

    S(["RM"], ["KB"], ac(z("KB"), RMc(15), AF.Identity, bias=4096 * B0 - 128, scale=1e9))
    S(["IDN"], ["ID16"], ac(z("ID16"), z("IDN"), AF.Sigmoid, bias=-128.0, scale=256.0))
    S(["w0", "CB", "RM"], ["AUX"], *([const(T.AUX[:, a:a + H], H, z("CB")) for a in range(0, 2304, H)]
                                     + [const(T.AUX[:, 2304:NW], 256, RMc(4))]))

    def targets(rnd, P, pk, h0, h1):
        o = WHERE["SELV"][1]
        for hs in range(h0, h1):
            b = (8 * rnd + hs) * H
            PE(["vv%d" % rnd, "SELV"], [pk], *group(*[(P[:, 64 * hs:64 * hs + 64], T.zb[0:8, o + 15 - a:o + 143 - a],
                                                       T.VV[0:8, b + c0:b + c1:st]) for a, (c0, c1, st) in enumerate(ROWS)]))

    def targets_out(rnd, P, pk):
        S([pk], ["VL%d" % rnd], ac(T.VL[:, 512 * rnd:512 * rnd + 512], P[:, 0:512], AF.Copy))

    def counts(k):
        a, b = 512 * k, 512 * k + 512
        V(["tab%d" % k], ["ci%d" % k], ts(T.CI[:, a:b], T.tabI[:, a:b], 15, BA))
        return lambda: V(["ci%d" % k], ["wt%d" % k], ts(wt(a, b), T.CI[:, a:b], -1.0 / 16, OP.add, -TINY, OP.max))

    def pointers(k):
        a, b = 512 * k, 512 * k + 512
        V(["tab%d" % k], ["yb%d" % k], ts(T.YB[:, a:b], T.tabI[:, a:b], -7.5, OP.add, 201326592.0, OP.add))
        S(["yb%d" % k], ["sh%d" % k], ac(T.SH[:, a:b], T.YB[:, a:b], AF.Identity, bias=-12583936.0, scale=0.0625))

    def differences(k):
        a, b = 512 * k, 512 * k + 512
        P, pk = ((T.PA, "#A"), (T.PB, "#B"), (PM, "#M"), (PM, "#M"))[k]
        PE(["sh%d" % k, "SH16"], [pk], mm(P[:, 0:512], z("SH16"), T.SH[:, a:b], True, True))
        S([pk], ["dt%d" % k], ac(T.DT[:, OD + a:OD + b], P[:, 0:512], AF.Copy))
    rest = counts(0)
    V(["cpF"], ["FH"], cp(z("FH"), T.CPI[:, 288:416]))
    V(["cpF"], ["FC"], ts(z("FC"), T.CPI[:, 288:416], -1024.0, OP.add))
    dma("y", ["FH"], ["FB"], (T.FB[0:8, :], z("FH")))
    dma("y", ["FC", "DF"], ["DF"], (T.DT[15:128:16, 0:2048], z("FC")))
    rest()
    pointers(0)
    V(["IDW", "MK"], ["TU"], *[ts(T.TU[:, 160 * j:160 * j + 160], z("IDW"), z("MK", j, j + 1), OP.mult) for j in range(6)])
    rest = counts(1)
    pointers(1)
    rest()
    V(["CXI"], ["C0", "C1"], ts(z("C4"), z("CXI"), -1024.0, OP.add))
    V(["CXI"], ["c0_0", "c0_1"], cp(T.CL[:, 0:96], z("CXI")))
    root(0)
    root(1)
    scaled("NLT", "LTB", -1.0, "LTB")
    scaled("N16", "IDN", -1.0 / 16, "IDN")
    targets(0, PM, "#M", 0, 8)
    differences(0)
    differences(1)
    targets_out(0, PM, "#M")
    rest = counts(2)
    pointers(2)
    rest()
    differences(2)
    o = WHERE["SELH"][1]
    PE(["FB", "SELH"], ["#N"], *group(*[(PM[:, 640:768], T.zh[0:8, o + 15 - i:o + 143 - i], T.FB[0:8, i:2048:16]) for i in range(16)]))
    rest = counts(3)
    V(["BM", "RM"], ["BC0"], *[ts(T.BC[:, 128 * a:128 * a + 128], z("BM"), RMc(a), OP.mult) for a in range(3)])
    rest()
    WTK = ["WT", "WTz", "WTn"] + ["wt%d" % k for k in range(4)]
    YNK = ["YN", "YNz", "YNn"] + ["yn%d" % k for k in range(9)]
    DTK = ["DT", "DF", "DTn", "DFn"] + ["dt%d" % k for k in range(4)]
    STK = ["STz"] + ["st%d" % k for k in range(4)]
    AFK = ["AFn"] + ["af%d" % k for k in range(8)]
    LBK = ["LBA"] + ["lb%d" % i for i in range(10)]

    def first_gap():
        V(["tab3"], ["yb3"], ts(T.YB[:, 1536:2048], T.tabI[:, 1536:2048], -7.5, OP.add, 201326592.0, OP.add))
        V(["BM", "RM", "BC0"], ["BC"], *[ts(T.BC[:, 128 * a:128 * a + 128], z("BM"), RMc(a), OP.mult) for a in range(3, 12)])

    def last_pointers():
        S(["yb3"], ["sh3"], ac(T.SH[:, 1536:2048], T.YB[:, 1536:2048], AF.Identity, bias=-12583936.0, scale=0.0625))

    def zeros():
        dma("y", ["ZB", "VW"], ["VW"], (T.VW[:, 0:384], z("ZB")))
        dma("y", ["ZF", "SW"], ["SW"], (T.SW[:, 0:384], z("ZF")))

    b32 = 129.0 - 31.0 / 64

    def aux_rows():
        for j, (r, key, t, a) in enumerate(((2, "HBa", "HB", 0), (3, "LB", "LB", 0), (7, "HBa", "HB", 128), (8, "LB", "LB", 128))):
            dma("y", [key, "AUX"], ["ar%d" % j], (T.AUX[r:128:16, 0:2048], z(t, a, a + 128)))
        dma("y", ["HBb", "AUX"], ["ar4"], (T.AUX[7:128:16, 2048:NW], z("HB", 256, 288)))
        dma("y", ["LB", "AUX"], ["ar5"], (T.AUX[8:128:16, 2048:NW], z("LB", 256, 288)))
        zeros()

    def lane_bits():
        for i in range(10):
            dma("y", ["BB1" if i > 5 else "bb%d" % i, "LBA"], ["lb%d" % i], (T.LBA[i:128:16, :], T.BB[:, 64 * i:64 * i + 64]))

    for ns, R, W, f in (
            (60, ["i_pc"], ["i_pc"], ts(z("i_pc"), z("i_pc"), 15, BA)),
            (110, ["cpj"], ["cpj"], ts(T.CPI[:, 128:256], T.CPI[:, 128:256], 2047, BA)),
            (60, ["cpk"], ["cpk"], ts(T.CPI[:, 256:288], T.CPI[:, 256:288], 511, BA)),
            (60, ["i_pc"], ["PC"], cp(z("PC"), z("i_pc", 0, 1))),
            (240, ["cpL", "cpj", "cpk"], ["cpl"], ts(T.CPL[:, :], T.CPI[:, 0:288], 31, BA)),
            (220, ["cpL", "cpj"], ["HBa"], ts(z("HB", 0, 256), T.CPI[:, 0:256], 1.0 / 32, OP.mult, b32, OP.add)),
            (60, ["cpk"], ["HBb"], ts(z("HB", 256, 288), T.CPI[:, 256:288], 1.0 / 32, OP.mult, b32 + 64.0, OP.add)),
            (240, ["cpl"], ["LB"], cp(z("LB"), T.CPL[:, :]))):
        later("v", ns, V, R, W, f)
    later("v", 0, aux_rows)
    for i in range(4):
        later("v", 60, V, ["i_jc"], ["BI%d" % i], ts(T.BI[:, 64 * i:64 * i + 64], z("i_jc"), 6 + i, SR, 1, BA))
    for j in (2, 3):
        later("v", 60, V, ["W16", "TWO", "Z16"], ["W%d" % j], scan(z("W16", 16 * j, 16 * j + 10), z("TWO", 0, 10), z("Z16", 0, 10), 0.5, OP.mult))
    later("v", 220, V, ["BI%d" % i for i in range(4)], ["BB1"], cp(T.BB[:, 384:640], T.BI[:, 0:256]))
    later("v", 0, lane_bits)
    for j in range(4):
        later("v", 60, V, ["RM", "W2", "W3", "W16"], ["WM%d" % j], tt(z("WM", 16 * j, 16 * j + 16), z("W16", 16 * j, 16 * j + 16), z("RM"), OP.mult))
    later("v", 60, V, [], ["QB"], ms(z("QB", 0, 16), 0.0))
    later("v", 200, t2, "NUT", "LTB", "BM", OP.subtract)
    for j in range(4):
        later("v", 60, V, ["WM%d" % j], ["WC%d" % j], rowsum(z("WC", j, j + 1), z("WM", 16 * j, 16 * j + 16)))
    later("v", 60, V, ["PC", "D1"], ["D1"], cp(z("D1", 0, 1), z("PC")))
    later("v", 110, V, ["i_dp"], ["U2"], ts(z("U2"), dp, 1.0, OP.is_equal))
    for j, v in enumerate(WEIGHTS):
        later("v", 60, V, ["WC%d" % j, "G8", "COMB"], ["cb%d" % v], ts(T.COMB[:, v * 144 + 15:v * 144 + 143:16], z("G8"), z("WC", j, j + 1), OP.mult))
    later("v", 200, t2, "U2", "U2", "BM", OP.mult)
    later("v", 110, tz, "WR", "i_wr", 1024.0, OP.add)
    later("v", 200, t2, "BID", "IDN", "U2", OP.subtract)

    def shifted(out, a, na, c, o=0, scale=1.0, st=1):
        S([a, "PC"], [out], ac(z(out, o, o + na * st, st), z(a, 0, na), AF.Identity, bias=c, scale=scale))

    def plain_pointers(k):
        S(["yb%d" % k], ["st%d" % k], ac(T.ST[:, 512 * k:512 * k + 512], T.YB[:, 512 * k:512 * k + 512], AF.Identity,
                                         bias=-12583936.0, scale=0.0625))

    def suffix_aux(k):
        S(AUXK + ["FL"], ["af%d" % k], ac(T.AUF[:, 256 * k:256 * k + 256], T.AUX[:, 0:2048].indirect(z("FL", 16 * k, 16 * k + 16)), AF.Copy))
    later("s", 80, shifted, "JL", "JI", 96, z("PC"))
    later("s", 110, scaled, "NI16", "IDN", -1.0, "IDN")
    later("s", 110, scaled, "NI", "IDN", -1.0, "IDN")
    later("s", 110, scaled, "CANDM", "BM", RMc(9), "RM")
    later("s", 60, S, ["RM", "G8", "COMB"], ["cb%d" % C0], ac(T.COMB[:, C0 * 144 + 15:C0 * 144 + 143:16], z("G8"), AF.Copy, scale=RMc(0)))
    later("s", 60, shifted, "JQ", "JL", 48, 1536.0, 0, 2.0)
    later("s", 60, shifted, "PJ", "JL", 24, 1536.0, 1, 1.0, 2)
    later("s", 60, shifted, "DUM0", "JL", 8, 2304.0)
    later("s", 60, shifted, "DUM1", "JL", 8, 2432.0)
    later("s", 60, shifted, "JQ", "JL", 48, 1536.0 / OD, 48, 2.0 / OD)
    later("s", 60, shifted, "DU", "JL", 16, 256.0)
    for k in range(8):
        later("s", 400, suffix_aux, k)
    later("s", 700, S, LBK, ["LBB"], ac(T.LBB[:, :], T.LBA[:, 0:H], AF.Identity, bias=-200.0, scale=400.0))

    def lists(p, idx):
        return T.CL[:, idx * 96 + 48 * p:idx * 96 + 48 * p + 48], "c%d_%d" % (idx, p)

    def halves(P, l, src):
        return [mm(P[:, 0:512], l, src[:, 0:512], True, False), mm(P[:, 512:H], l, src[:, 512:H], True, False)]

    def spread(P, src):
        return [mm(P[:, c0:c1:st], T.BC[:, 128 * a:128 * a + 128], src, False, a in (7, 11)) for a, (c0, c1, st) in enumerate(ROWS)]

    PART = ((0, 512), (512, H))

    def both(key, p):
        return ["%s%d0" % (key, p), "%s%d1" % (key, p)]

    def gather_counts(p, idx, k, part):
        a, b = PART[part]
        off, ck = T.CL[:, idx * 96 + 48 * p + a // 16:idx * 96 + 48 * p + b // 16], "c%d_%d" % (idx, p)
        wi = (wt(0, 2304) if k <= SP else T.WT[:, 0:2 * OW + OD]).indirect(off)
        W = ["w%d%d" % (p, part)]
        if k:
            V(WTK + (["WTl"] + ["WTh%d" % j for j in range(4)]) * (k > SP) + [ck, "m%d" % p], W, tt(w[p][:, a:b], wi, T.MM[:, H * p + a:H * p + b], OP.mult))
        else:
            op("vs"[p], WTK + [ck, "AUX"], W, ac(w[p][:, a:b], wi, AF.Copy) if p else cp(w[p][:, a:b], wi))

    def target(p, k):
        S(["VL%d" % (k // SP)], ["D0v%d" % p], ac(zs("D0", p, 256, 3, 4), T.VL[:, 128 * k + 64 * p:128 * k + 64 * p + 64], AF.Copy))

    def total(p, part):
        f = group(*[(LP[p][:, 2:256:4], comb(C1, a), w[p][:, c0:c1:st]) for a, (c0, c1, st) in enumerate(ROWS)])
        PE(["w%d%d" % (p, part), "cb%d" % C1], [LK[p]], *(f[8:] if part else f[:8]))

    def rounding(p):
        S([LK[p]], ["D0a%d" % p], ac(zs("D0", p, 256, 1, 4), LP[p][:, 2:256:4], AF.Identity, bias=B0 + 0.48, scale=-1.003))

    def prefix(p):
        PE(both("w", p) + ["NLT"], BK[p], *halves(PX[p], z("NLT"), w[p]))

    def roots(p):
        o = 512 * p
        PE(["D0%d" % p, "RT%d" % p, "ID16", "TU"], [MK[p]], mm(PM[:, o:o + 64], z("ID16"), zs("D0", p, 256, 0, 4), True, False),
           *[mm(PM[:, o + r:o + 64:st], turn(*BACK[j]), z("RT", 48 * p + c0, 48 * p + c1), False, False)
             for j, (_, _, (r, st), (c0, c1)) in enumerate(TURN)])

    def limit(p):
        PE(["D0a%d" % p, "ID16"], [MK[p]], mm(PM[:, 512 * p:512 * p + 64], z("ID16"), zs("D0", p, 256, 1, 4), False, True))

    def floor_vt(p):
        sp = str(p)
        V([LK[p], "D0" + sp, "D0a" + sp, "D0v" + sp, "D1" + sp], ["SC" + sp], scan(zs("SC", p, 256), zs("D0", p, 256), LP[p][:, 0:256], 0.0, OP.mult))

    def stays(p):
        V([MK[p], "SC%d" % p], ["eb%d" % p], tt(zs("eb", p), zs("SC", p, 256, 3, 4), PM[:, 512 * p:512 * p + 64], OP.is_lt))

    def turned(p):
        return [(LP[p][:, 320 + c0:320 + c1], turn(m, sh), zs("eb", p, 64, r, st)) for m, sh, (r, st), (c0, c1) in TURN]

    def window(p):
        PE(["eb%d" % p, "C%d" % p, "ID16", "TU"], [LK[p]], *group((LP[p][:, 320:368], z("ID16"), cm(p)), *turned(p)))

    def bound(p):
        f = spread(PX[p], zs("SC", p, 256, 3, 4))
        PE(["SC%d" % p, "BC"], [BK[p][0]], *f[:8])
        PE(["SC%d" % p, "BC"], [BK[p][1]], *f[8:])

    def compare(p, parts=(0, 1)):
        a, b = PART[parts[0]][0], PART[parts[-1]][1]
        S([BK[p][j] for j in parts] + ["KB"], ["k%d%d" % (p, j) for j in parts],
          ac(cond[p][:, a:b], PX[p][:, a:b], AF.Sigmoid, bias=z("KB"), scale=-4096.0))

    def history(s):
        S(["#LA", "HT"], ["E8" if s == SP - 1 else "HT"], ac(z("E8") if s == SP - 1 else z("HT", s + 2, 40, 5), LA[:, 320:328],
                                                             AF.Sigmoid, bias=256 * 1151.5, scale=-256.0))
        S(["C0", "DL"], ["DL"], ac(z("DL", s + 1, 40, 5), cm(0, 8), AF.Identity, bias=1024.0))

    def marks_banks(p, k):
        return (PM, MK) if p and k % SP == SP - 1 else (PX[p], BK[p])

    def marks_sum(p, k):
        P, pk = marks_banks(p, k)
        if k < RO * SP - 1:
            PE(both("w", p) + ["N16", "eb%d" % p, "BC"], pk, *(halves(P, z("N16"), w[p]) + spread(P, zs("eb", p))))

    def marks(p, k):
        P, pk = marks_banks(p, k)
        if k < RO * SP - 1:
            S(pk, ["m%d" % p], ac(T.MM[:, H * p:H * p + H], P[:, 0:H], AF.Sigmoid, bias=-128.0, scale=2.0 ** 32))

    def shown(p, rnd, q, a=0, b=H):
        off = T.CL[:, (SP - 1) * 96 + 48 * p + a // 16:(SP - 1) * 96 + 48 * p + b // 16] if rnd == 0 else z("CC", 48 * p + a // 16, 48 * p + b // 16)
        o, i = T.A2[:, H * p + a:H * p + b], T.AUF[:, 0:2048 + 128 * rnd].indirect(off)
        op(q, AFK + ["CC%d" % p if rnd else "c%d_%d" % (SP - 1, p)], ["A2%d%d" % (p, a)], ac(o, i, AF.Copy) if q == "s" else cp(o, i))

    def window_offsets(p):
        V([LK[p]], ["XL%d" % p], ts(zs("XL", p, 48), LP[p][:, 320:368], 1024.0, OP.add))

    def gather_next(p, rnd, part):
        a, b = PART[part]
        off = z("XL", 48 * p + a // 16, 48 * p + b // 16)
        V(DTK + ["XL%d" % p, "k%d%d" % (p, part)], ["X%d%d" % (p, part)],
          tt(X[p][:, a:b], T.DT[:, 0:OD + 2048 + 128 * rnd].indirect(off), cond[p][:, a:b], OP.mult))

    def next_sum(p):
        PE(both("X", p) + ["COMBX"], [LK[p]], *group(*[(LP[p][:, 368:416], T.COMBX[:, 15 - i:143 - i], X[p][:, i:H:16]) for i in range(16)]))

    def next_list(p, idx, rnd):
        off, ck = lists(p, idx)
        V([LK[p]], [ck], ts(off, LP[p][:, 368:416], 1024.0 + OW * rnd, OP.add))

    def settle(p, P, bias, after):
        S([LK[p]], ["C%d" % p], ac(cm(p), P, AF.Identity, bias=bias))
        if after is None:
            S([LK[p]], ["RT%d" % p], ac(zs("RT", p, 48), P, AF.Sigmoid, bias=-256 * (1023.5 + bias), scale=-256.0))
        else:
            S([LK[p]], ["CLF%d" % p], ac(zs("CLF", p, 48), P, AF.Identity, bias=bias + 1024.0 + after))

    def keep(p):
        S([LK[p]], ["JW%d" % p], ac(zs("JW", p, 48), LP[p][:, 368:416], AF.Identity, bias=192.0, scale=1.0 / OW))
        S(["JW%d" % p], ["XW%d" % p], ac(zs("XW", p, 48), zs("JW", p, 48), AF.Identity, bias=-192.0 * OW, scale=float(OW)))

    def unwrap(p, last=False):
        V([LK[p], "XW%d" % p], ["C%d" % p], tt(cm(p), LP[p][:, 368:416], zs("XW", p, 48), OP.subtract))
        if last:
            S(["C%d" % p], ["CLF%d" % p], ac(zs("CLF", p, 48), cm(p), AF.Identity, bias=1024.0))
        else:
            root(p)

    nxt = T.cores[(rank + 1) % len(T.cores)]
    rid, pid = topo.addr(nxt, core)
    rmask, ne = topo.mask(core, nxt), len(topo.engines(core, nxt))
    gap = lambda: spend("v", 200)

    for rnd in range(RO):
        base, i4, k3 = 5 * rnd, 5 * rnd + SP, SP * rnd + SP - 1
        DUM = "DUM%d" % rnd
        tb, TBK, TBn, one = (wt, WTK, "WTn", 15.0 / 16) if rnd == 0 else (lambda a, b: T.YN[:, a:b], YNK, "YNn", 1.0)
        k0 = rnd * SP

        def steps_of_rank(p):
            o, a = LP[1 - p][:, 440:488], 16 + 48 * p
            PE(["EB0", "EB%d" % p, "EB", "QB", "QB0", "QB%d" % p, "NLT", "NUT", "ID16", "NI16"], [LK[1 - p]], *group(
                (o, z("ID16"), z("QB", a, a + 48)), (o, z("NI16"), z("QB", a - 1, a + 47)),
                (o, z("NLT"), z("EB", a, a + 48)), (o, z("NUT"), z("EB", a - 1, a + 47))))

        def ranks(p):
            V([LK[1 - p], "D1", "POSF0"], ["POSF%d" % p], scan(zs("POSF", p, 48), LP[1 - p][:, 440:488], zs("D1", p, 48),
                                                              z("POSF", 47, 48) if p else 0.0, OP.add))

        def places(p):
            V(["POSF%d" % p], ["POS%d" % p], cp(zs("POS", p, 48), zs("POSF", p, 48)))

        def out_of_psum(p):
            if rnd:
                keep(p)
            else:
                settle(p, LP[p][:, 368:416], 0.0, None)

        for s in range(SP):
            k, idx, last = k0 + s, base + s, s == SP - 1
            gather_counts(0, idx, k, 0)
            if s and rnd:
                unwrap(0)
            if s:
                next_list(1, idx, rnd)
            elif rnd:
                spend("v", 130)
            total(0, 0)
            gather_counts(0, idx, k, 1)
            total(0, 1)
            if k == SP:
                spend("v", 60)
            if k == 0:
                gather_counts(1, idx, k, 0)
                gather_counts(1, idx, k, 1)
                first_gap()
            if s:
                out_of_psum(1)
            target(0, k)
            rounding(0)
            roots(0)
            prefix(0)
            limit(0)
            target(1, k)
            if last and rnd:
                V(["C0"], ["CC0"], ts(zs("CC", 0, 48), cm(0), 1024.0, OP.add))
            if last:
                while spare["s"] and spare["s"][0][0] <= 400:
                    spend("s", 400)
            elif k == 0:
                last_pointers()
            else:
                spend("s", 800)
            if k:
                gather_counts(1, idx, k, 0)
            if s and rnd:
                unwrap(1)
            floor_vt(0)
            if k:
                gather_counts(1, idx, k, 1)
            total(1, 0)
            if k == 0:
                total(1, 1)
            bound(0)
            if k:
                total(1, 1)
            if not last:
                compare(0, (0,))
            rounding(1)
            if last:
                shown(0, rnd, "s")
            stays(0)
            window(0)
            if k == 0:
                differences(3)
                V(["#N"], ["FL"], cp(z("FL"), PM[:, 640:768]))
            if last and rnd:
                V(["C1"], ["CC1"], ts(zs("CC", 1, 48), cm(1), 1024.0, OP.add))
            if last and rnd == 0:
                shown(1, rnd, "v", 0, 256)
            else:
                spend("v", 500 if k else 900)
            roots(1)
            prefix(1)
            limit(1)
            floor_vt(1)
            window_offsets(0)
            if last:
                break
            compare(0, (1,))
            history(s)
            spend("s", 400 if k else 500)
            bound(1)
            spend("v", 250 if k else 500)
            stays(1)
            window(1)
            marks_sum(0, k)
            gather_next(0, rnd, 0)
            window_offsets(1)
            gather_next(0, rnd, 1)
            compare(1)
            next_sum(0)
            marks(0, k)
            marks_sum(1, k)
            gather_next(1, rnd, 0)
            next_list(0, idx + 1, rnd)
            gather_next(1, rnd, 1)
            out_of_psum(0)
            next_sum(1)
            marks(1, k)
            spend("s", 400 if k else 500)
        nl, nk = z("NL"), "NL"
        V(["#LA", "EB"], ["EB0"], ts(z("EB", 16, 64), LA[:, 320:368], 1151.5, OP.is_ge))
        history(SP - 1)
        compare(0)
        if rnd:
            shown(1, rnd, "s", 0, 256)
        stays(1)
        V(["EB0", "JQ", "QB"], ["QB0"], tt(z("QB", 16, 64), z("EB", 16, 64), z("JQ", 0, 48), OP.mult))
        tu = turned(1)
        PE(["eb1", "TU"], ["#LB"], *(group(*tu[:2]) + group(*tu[2:])))
        steps_of_rank(0)
        spend("s", 9000)
        V(["HT", "EB0"], ["CAND"], tt(z("CAND"), z("HT", 4, 40, 5), z("EB", 16, 24), OP.mult))
        t2("hd", "HT", "DL", OP.mult)
        V(["CAND", DUM], ["N2"], tt(z("N2"), z("CAND"), z(DUM, 0, 8), OP.mult))
        t2("d1", "DL", "hd", OP.subtract)
        V(["N2", DUM], ["ND"], tt(z("ND"), z(DUM, 0, 8), z("N2"), OP.subtract))
        V(["#LB", "JQ", "QB"], ["QB1"], tt(z("QB", 64, 112), LB[:, 320:368], z("JQ", 48, 96), OP.mult))
        V(["#LB", "EB"], ["EB1"], ts(z("EB", 64, 112), LB[:, 320:368], 1.0 / OD, OP.mult))
        ranks(0)
        steps_of_rank(1)
        V(["#LB", "C1"], ["xb"], tt(z("xb"), LB[:, 320:368], cm(1), OP.add))
        V(["HT", "d1"], ["FS"], scan(z("FS"), z("HT"), z("d1"), 0.0, OP.mult))
        places(0)
        S(["LBB", "POS0", "SW"], ["SW"], ac(T.SW[:, :].indirect(zs("POS", 0, 48)), T.LBB[:, :], AF.Sigmoid))
        bound(1)
        ranks(1)
        V(["FS", "DL", "ND"], ["KK"], tt(z("KK", 0, 8), z("FS", 3, 40, 5), z("ND"), OP.max), tt(z("KK", 8, 16), z("DL", 4, 40, 5), z("ND"), OP.max))
        places(1)
        V(["KK"], ["FK"], cp(z("FK"), z("KK")))
        V(["xb"], ["XL1"], ts(zs("XL", 1, 48), z("xb"), 1024.0, OP.add))
        if rnd:
            V(AUXK + ["FK"], ["XF"], cp(z("XF"), T.AUX[:, :].indirect(z("FK"))))
        V(LBK + ["POS1", "VW"], ["VW"], cp(T.VW[:, :].indirect(zs("POS", 1, 48)), T.LBA[:, 0:H]))
        spend("v", 9000)
        marks_sum(0, k3)
        marks_sum(1, k3)
        S(["SW"], ["SWb"], ac(z("SWb"), T.SW[:, 0:384], AF.Copy))
        marks(0, k3)
        marks(1, k3)
        if rnd:
            compare(1)
            shown(1, rnd, "s", 256, H)
        else:
            V(AUXK + ["FK"], ["XF"], cp(z("XF"), T.AUX[:, :].indirect(z("FK"))))
            shown(1, rnd, "v", 256, H)

        def pairs(h, banks=(0, 1)):
            f, xf = [], z("XF", 128 * h, 128 * h + 128)
            for gg in range(4 * banks[0], 4 * banks[-1] + 4):
                o = PX[h][:, 128 * gg:128 * gg + 128]
                f += group((o, T.SELK[:, 128 * gg:128 * gg + 128], xf), (o, xf, T.NSELK[:, 128 * gg:128 * gg + 128]))
            PE(["XF", "SELK", "NSELK"], [BK[h][j] for j in banks], *f)

        def equal(h):
            V(BK[h] + ["TRW"], ["EQ%d" % h], tt(T["EQ%d" % h][:, :], PX[h][:, :], T.TRW[:, :], OP.is_equal))

        def contexts_after(p):
            next_sum(p)
            if rnd:
                keep(p)
            else:
                settle(p, LP[p][:, 368:416], 0.0, 0.0)
        sl = LB[:, 416:440]
        if rnd:
            pairs(0)
        f = group(*(combed(sl, CSA, lambda i, n, st: z("SWb", i, n, st), 384) + combed(sl, CSB, lambda i, n, st: T.VW[:, i:n:st], 384)))
        PE(["SWb", "cb%d" % CSA], ["#LB"], *f[:16])
        PE(["VW", "cb%d" % CSB], ["#LB"], *f[16:])
        if rnd:
            equal(0)
        else:
            pairs(0)
        SND, RCV = T["SND%d" % rnd], T["RCV%d" % rnd]
        sk, rk = "SND%d" % rnd, "RCV%d" % rnd
        V(["#LB"], ["LNE"], ts(z("LNE"), sl, 1536.0, OP.add))
        S(["A200", "A210", "A21256", "A2z", "LNE"], [sk + "a"], ac(SND[:, 0:384], T.A2[:, :].indirect(z("LNE")), AF.Copy))
        if rnd == 0:
            V(["#LB", sk + "z"], [sk + "b"], ts(SND[:, 385:432:2], sl, -0.5, OP.is_lt))
            V(["m0", "m1", "mz", "LNE"], [sk + "c"], cp(SND[:, 432:816], T.MM[:, 0:1552].indirect(z("LNE"))))
            compare(1)
        oh = PM[:, 512:640]
        PE(["k00", "BID"], ["#N"], mm(oh, z("BID"), cond[0][:, 0:128], True, True))
        TB = tb(0, NW)
        S(TBK + ["FK"], ["hF"], ac(z("hF"), TB.indirect(z("FK", 0, 8)), AF.Identity, bias=one, scale=-1.0))
        S(TBK + ["FK"], ["gF"], ac(z("gF"), TB.indirect(z("FK", 0, 8)), AF.Copy))
        if rnd == 0:
            equal(0)
            plain_pointers(0)
            plain_pointers(1)
        do_waits("q", [sk + c for c in "azbc"[:2 if rnd else 4]], [])
        g.remote_dma(RCV[:, :], SND[:, :], T.sem["arr%d" % rnd], T.sem["snt%d" % rnd], pid, rid, rmask)
        used["snt%d" % rnd] = ne
        used["arr%d" % rnd] = ne
        record(("rem%d" % rnd, "arr%d" % rnd, ne, {}), [], [rk])

        PW, WK = [PM, T.PB], ["#M", "#B"]
        dm = T.AUX[:, 2304 + 128 * rnd:2432 + 128 * rnd]

        def dup(h):
            o, EQ, xf = PW[h][:, 0:128], T["EQ%d" % h], zs("XF", h, 128)
            PE(["EQ%d" % h, "OB", "XF", "CANDM", "IDN", "NI"] + AUXK, [WK[h]], *(
                group((PW[h][:, 128:256], z("IDN"), xf), (PW[h][:, 128:256], z("NI"), dm))
                + group((o, z("CANDM"), xf), *[(o, z("OB", 112 - 16 * gg, 240 - 16 * gg), EQ[:, 128 * gg:128 * gg + 128]) for gg in range(8)])))

        def winners(h):
            V([WK[h]], ["AR%d" % h], ts(zs("AR", h, 128), PW[h][:, 0:128], 0.5, OP.is_gt))

        def keys(h):
            V(["AR%d" % h, WK[h]], ["ZW%d" % h], tt(zs("ZW", h, 128), zs("AR", h, 128), PW[h][:, 128:256], OP.mult))
            o = PW[h][:, 256:264]
            PE(["ZW%d" % h, "cb%d" % CID, "ID16", "DU"], [WK[h]], *group(
                (o, z("ID16"), z("DU", 8 * rnd, 8 * rnd + 8)), *combed(o, CID, lambda i, n, st: z("ZW", 128 * h + i, 128 * h + n, st), 128)))

        def offsets(h):
            V([WK[h]], ["OF%d" % h], ts(z(("OFF", "OFD")[h]), PW[h][:, 256:264], 2048.0, OP.add))

        def landed(p, e):
            o, i = T.LW[:, H * p:H * p + H], RCV[:, 0:400].indirect(zs("POG", p, 48))
            op(e, [rk, "POG"], ["LW%d" % p], ac(o, i, AF.Copy) if e == "s" else cp(o, i))

        def shown_list(p, P, pk=None):
            PE(["LW%d" % p, "cb%d" % CLK], [pk or LK[p]], *group(*combed(P, CLK, lambda i, n, st: T.LW[:, H * p + i:H * p + n:st], H)))

        def next_targets(a, b):
            if rnd == 0:
                targets(1, T.PA, "#A", a, b)

        def new_rows():
            V(["C0"], ["NL"], ts(z("NL"), cm(0, 8), 1024.0, OP.add))
            S(WTK + [nk], ["ug"], ac(z("ug"), wt(0, 2304).indirect(nl), AF.Identity, bias=128.3, scale=0.5))
        hh, wc = PM[:, 640:768], 2048 + 128 * rnd
        dup(0)
        pairs(1)
        gather_next(0, rnd, 0)
        winners(0)
        V(["#N", "hF"], ["hh"], tt(hh, oh, z("hF"), OP.mult))
        keys(0)
        gather_next(0, rnd, 1)
        V(["AR0", "hh", "#N"], ["m1"], tt(z("m1"), zs("AR", 0, 128), hh, OP.mult))
        equal(1)
        offsets(0)
        V(["POSF0", "POSF1"], ["POG"], ts(z("POG"), z("POSF"), 384.0, OP.min))
        if rnd == 0:
            contexts_after(0)
            dup(1)
            V(["#LB"], ["T1"], ts(z("T1"), sl, -0.5, OP.is_lt))
            V(["#LB", "JL"], ["LNF"], tt(z("LNF"), sl, z("JL", 0, 24), OP.subtract))
            V(["#N", "AR0"], ["OA"], tt(z("OA"), oh, zs("AR", 0, 128), OP.mult))
            new_rows()
            next_targets(0, 2)
            V(["LNF", "T1", "PJ"], ["PJ"], tt(z("PJ", 0, 48, 2), z("LNF"), z("T1"), OP.mult))
            gather_next(1, rnd, 1)
            S(["OA"], ["nOA"], ac(z("nOA"), z("OA"), AF.Identity, bias=1.0, scale=-1.0))
            S(AUXK + [nk], ["AFn"], ac(T.AUF[:, 2048:OD], T.AUX[:, 0:2048].indirect(nl), AF.Copy))
            S(DTK + [nk], ["DTn"], ac(T.DT[:, OD + 2048:OD + OD], T.DT[:, OD:OD + 2048].indirect(nl), AF.Copy))
            plain_pointers(2)
            plain_pointers(3)
            tz("u2", "ug", -128.0625, OP.add, -TINY, OP.max)
        else:
            dup(1)
            contexts_after(0)
        V(["gF", "m1", "OF0"] + ["ug"] * (1 - rnd), TBK, tt(TB.indirect(z("OFF")), z("gF"), z("m1"), OP.add))
        if rnd:
            gather_next(1, rnd, 0)
        winners(1)
        if rnd == 0:
            V(["u2", "AR0"], [TBn], tt(tb(wc, wc + 128), z("u2"), zs("AR", 0, 128), OP.mult))
        keys(1)
        V(["#N", "AR1"], ["OBm"], tt(z("OBm"), oh, zs("AR", 1, 128), OP.mult))
        if rnd:
            gather_next(1, rnd, 1)
            unwrap(0, True)
        else:
            next_targets(2, 4)
            gather_next(1, rnd, 0)
            contexts_after(1)
        V(TBK + ["FK", "OBm"], ["s1"], tt(z("s1"), TB.indirect(z("FK", 8, 16)), z("OBm"), OP.add))
        if rnd == 0:
            t2("qS", "OA", "WR", OP.mult)
            tz("s2", "s1", 15.0, OP.min, 128.0, OP.add)
            V(STK + ["FK", "nOA"], ["tS"], tt(z("tS"), T.ST[:, :].indirect(z("FK", 0, 8)), z("nOA"), OP.mult))
            PE(["SH16", "tS", "qS", "AFn", "cb%d" % CID], ["#M"], *(group((PM[:, 0:128], z("SH16"), z("tS")), (PM[:, 0:128], z("SH16"), z("qS")))
                                                                    + group((PM[:, 128:256], comb(CID, 15), T.AUF[:, 2048:OD]))))
            S(["#M"], ["xs"], ac(z("xs"), PM[:, 0:128], AF.Copy))
            tz("s3", "s2", -128.0625, OP.add, -TINY, OP.max)
        else:
            new_rows()
            landed(0, "s")
            contexts_after(1)
            tz("s3", "s1", 15.0, OP.min)
        offsets(1)
        if rnd:
            tz("u2", "ug", -128.0, OP.add)
        V(["s3", "OF1"], TBK, cp(TB.indirect(z("OFD")), z("s3")))
        if rnd:
            V(["u2", "AR0"], [TBn], tt(tb(wc, wc + 128), z("u2"), zs("AR", 0, 128), OP.mult))
            for a, q in ((0, "y"), (1152, "y")):
                dma(q, YNK, [], (T.yn[:, a:a + 1152], T.YN[:, a:a + 1152]))

        def merged(p, P, pk=None):
            V([pk or LK[p], "CLF%d" % p], ["mx%d" % p], tt(zs("mx", p, 48), P, zs("CLF", p, 48), OP.max))

        def flag(p):
            V(["mx%d" % p], ["rr%d" % p], ts(zs("rr", p, 48), zs("mx", p, 48), 2.0 * OW, OP.is_ge, 2.0 * OW, OP.mult))

        def plain(p):
            V(["mx%d" % p, "rr%d" % p], ["YC%d" % p], tt(zs("YC", p, 48), zs("mx", p, 48), zs("rr", p, 48), OP.subtract))
        if rnd == 0:
            dma("y", WTK, ["WTl"], (T.WT[:, 0:OW], wt(0, OW)))
            for j in range(4):
                later("s", 400, S, WTK, ["WTh%d" % j], ac(T.WT[:, 2 * OW + 544 * j:2 * OW + 544 * j + 544], wt(544 * j, 544 * j + 544), AF.Copy))
            tz("k1", "xs", 1.0 / 4096, OP.mult, M23, OP.add)
            S(["#M"], ["DFn"], ac(T.DT[:, 2048:OD], PM[:, 128:256], AF.Copy))
            next_targets(4, 7)
            tz("kk", "k1", -M23, OP.add, float(OW), OP.mult)
            V(["FS"], ["DL"], cp(z("DL", 0, 40, 5), z("FS", 4, 40, 5)))
            zeros()
            landed(0, "s")
            landed(1, "s")
            spend("s", 400)
            V([rk, "PJ"], ["TF"], scan(z("TF"), RCV[:, 384:432], z("PJ"), 0.0, OP.mult))
            V(["TF"], ["TO"], cp(z("TO"), z("TF", 1, 48, 2)))
            V([rk, "TO", "m0", "m1", "mz"], ["m0", "m1", "mz"], cp(T.MM[:, :].indirect(z("TO")), RCV[:, 432:816]))
            shown_list(0, LA[:, 368:416])
            next_targets(7, 8)
            shown_list(1, LB[:, 368:416])
            targets_out(1, T.PA, "#A")

            def hopped(p):
                off, ck = lists(p, SP + 1)
                V(["YC%d" % p], [ck], cp(off, zs("YC", p, 48)))
                S(["YC%d" % p], ["C%d" % p], ac(cm(p), zs("YC", p, 48), AF.Identity, bias=-1024.0))
                S(["YC%d" % p], ["RT%d" % p], ac(zs("RT", p, 48), zs("YC", p, 48), AF.Sigmoid, bias=128.0, scale=-256.0))
            merged(0, LA[:, 368:416])
            S(["#LA"], ["HF"], ac(z("HF"), LA[:, 368:376], AF.Sigmoid, bias=-2048.0))
            flag(0)
            plain(0)
            hopped(0)
            merged(1, LB[:, 368:416])
            later("v", 130, flag, 1)
            later("v", 60, lambda: (plain(1), spend("v", 190), hopped(1)))
            later("v", 60, V, ["HF", "E8"], ["HT"], tt(z("HT", 1, 40, 5), z("E8"), z("HF"), OP.subtract))
            later("v", 450, V, ["kk", "xs", "OF0"], DTK, tt(T.DT[:, OD:OD + NW].indirect(z("OFF")), z("xs"), z("kk"), OP.subtract))
            for j in range(9):
                later("v", 190, V, WTK, ["yn%d" % j], ts(T.YN[:, 256 * j:256 * j + 256], wt(256 * j, 256 * j + 256), M23, OP.add, -M23, OP.add))
        else:
            landed(1, "v")
            shown_list(0, LA[:, 448:496])
            shown_list(1, PM[:, 0:48], "#M")
            unwrap(1, True)
            merged(0, LA[:, 448:496])
            flag(0)
            plain(0)
            merged(1, PM[:, 0:48], "#M")
            flag(1)
            plain(1)
            dma("s", ["YC0", "YC1"], [], (T.yc[:, :], z("YC")))

    for q in ("v", "s", "t", "q"):
        g.wait_ge(T.sem[q], cnt[q])
    for name, val in used.items():
        g.wait_ge(T.sem[name], val)
